import numpy as np, ml_dtypes
CORES = [48,51,52,55]
N = 4
BF = ml_dtypes.bfloat16
W, H, P, RO, ST, TH = 4096, 2048, 256, 5, 1, 36
def place(o, i):
    return o[np.arange(8)[None, :, None, None], i]
def ground(rng):
    o = np.argsort(rng.random((8, W)), axis=-1); x = np.zeros((N, 8, 16, W), np.int64); top = np.zeros(8, np.int64)
    for g in range(8):
        m = int(rng.choice(np.array([3, 5, 8]))); c = rng.integers(0, 16, (m, 16)); s = np.linspace(0, m, W, endpoint=False)
        i = np.minimum(s.astype(np.int64), m - 1); f = (s - i)[:, None]
        b = np.rint(c[i] * (1 - f) + c[(i + 1) % m] * f).astype(np.int64).T
        y = b[None] + rng.integers(-1, 2, (N, 16, W))
        y = np.where(rng.random((N, 1, W)) < 0.03, rng.integers(0, 16, (N, 16, W)), y)
        x[:, g] = np.clip(y, 0, 15)[:, :, np.argsort(o[g])]; top[g] = W * 28 // (85 * m)
    return o, top, x
def knot(rng, r, share):
    k = (N, 8, 1, r.shape[3]); p = rng.integers(0, 15, k); q = np.minimum(p + rng.integers(1, 5, k), 15)
    hit = (rng.random(k) < share) & (np.arange(16)[None, None, :, None] == q)
    return np.where(hit, np.take_along_axis(r, p, 2), r)
def walk(rng, o, top, n):
    st = np.floor((rng.random((N, 8, 15, n)) * 1.2 - 0.2) * top[None, :, None, None]).astype(np.int64)
    st = st + np.where(rng.random(st.shape) < 0.01, rng.integers(0, W, st.shape), 0)
    a = rng.integers(0, W, (N, 8, 1, n))
    return knot(rng, place(o, np.concatenate([a, a + np.add.accumulate(st, axis=2)], axis=2) % W), 0.4)
def ladder(rng, lev):
    pm = np.argsort(rng.random((8, 16)), axis=-1)
    return np.clip(lev[:, :, None, :] - 15 * pm[None, :, :, None], 0, 15)
def pack(x, c, r):
    return {"x": np.ascontiguousarray(x.reshape(N, 128, W)).astype(np.float32).astype(BF), "c0": np.ascontiguousarray(c.reshape(N, 128, H)).astype(np.int32),
            "r0": np.ascontiguousarray(r.reshape(N, 128, P)).astype(np.int32)}
def setup_inputs(rng):
    o, top, x = ground(rng)
    return pack(x, walk(rng, o, top, H), walk(rng, o, top, P))
def setup_inputs_ties(rng):
    o = np.argsort(rng.random((8, W)), axis=-1); cls = np.argsort(o, axis=-1) % 7
    cr = np.where(rng.random((N, 8, W)) < 0.04, rng.integers(0, 7, (N, 8, W)), cls[None])
    lev = np.array([0, 1, TH, TH + 1, 2 * TH, 2 * TH + 1, 3 * TH + 2])[cr]
    def some(n):
        i = rng.integers(0, 6, (N, 8, n)); rows = [i]
        for p in range(15):
            jump = rng.random((N, 8, n)) < 0.04
            d = np.where(jump, rng.choice(np.array([-3, 3]), (N, 8, n)), rng.choice(np.array([-2, -2, -1, 0, 1, 2, 2]), (N, 8, n)))
            i = np.clip(i + d, 0, 5 + jump.astype(np.int64)); rows.append(i)
        i = np.stack(rows, axis=2)
        return place(o, i + 7 * rng.integers(0, W // 7, i.shape))
    return pack(ladder(rng, lev), some(H), some(P))
def setup_inputs_clash(rng):
    hi = np.arange(W - 64, W); last6 = (hi[:, None] * hi[None, :]) % 64 == 63; over = last6 & (hi[:, None] * (hi[None, :] + 64) > 2 ** 24)
    hu, hv = np.nonzero(over if np.any(over) else last6)
    nm = rng.random((8, W)) < 0.5; a = rng.integers(1, H - 1, 8); row = np.arange(16)[None, :, None]
    r = np.zeros((N, 8, 16, P), np.int64); c = np.zeros((N, 8, 16, H), np.int64); lev = np.zeros((N, 8, W), np.int64)
    for g in range(8):
        sp = np.array([0, H - 1, int(a[g]), int(a[g]) + H]); nm[g, sp] = True
        apart = rng.permutation(H)[:P] + H * rng.integers(0, 2, P)
        if g == 4: nm[g, apart] = True
        if g == 5: nm[g, W - 64:] = True
        ne, fa = np.flatnonzero(nm[g]), np.flatnonzero(~nm[g])
        if g < 2: u, v = sp[2:], np.array([0, 0])
        elif g < 4: u, v = sp[:2], np.array([int(rng.choice(ne)), 0])
        elif g == 4: u, v = apart, np.zeros(P, np.int64)
        elif g == 5: u, v = hi[hu], hi[hv]
        else: u, v = rng.choice(ne, 8), rng.choice(ne, 8)
        i = rng.integers(0, len(u), (N, P)); k = rng.integers(0, 16, (N, P))
        if g == 4: i = np.argsort(rng.random((N, P)), axis=-1)
        if g == 1 or g == 4: k = rng.integers(0, 14, (N, P))
        if g == 0: k[0, :3] = 15; k[0, 3] = 5; k[1] = 15; k[1, P - 1] = 3
        k[2] = np.minimum(k[2], 14)
        at = np.where(k < 15, k, rng.integers(0, 15, (N, P)))
        y = np.where(row > k[:, None], rng.choice(fa, (N, 16, P)), rng.choice(ne, (N, 16, P)))
        y = np.where(row == at[:, None], u[i][:, None], y)
        y[:, 15] = np.where(k == 14, y[:, 15], v[i]); r[:, g] = y
        flip = rng.random((N, W)) < 0.02; flip[:, sp] = False; flip[:3] = False
        lev[:, g] = np.where(nm[g][None] ^ flip, 0, 150) + rng.integers(0, 6, (N, W))
        c[:, g] = np.where(rng.random((N, 1, H)) < 0.5, rng.choice(ne, (N, 16, H)), rng.integers(0, W, (N, 16, H)))
    return pack(ladder(rng, lev), c, r)
def setup_inputs_loops(rng):
    o, top, x = ground(rng); x[:, ::2] = rng.integers(0, 3, (N, 4, 16, W))
    e = np.argsort(o, axis=-1); b = 1 + 2 * int(rng.integers(0, 4)); z = int(rng.integers(0, N))
    x[:, b] = np.where(e[b] % 3 == 0, rng.integers(0, 3, (N, 16, W)), x[:, b])
    def tie(r):
        kd = rng.integers(0, 8, (N, 8, r.shape[3]))
        for p in range(1, 16):
            r[:, :, p] = np.where(kd == 1, r[:, :, 0], r[:, :, p])
            if p > 1: r[:, :, p] = np.where(kd == 7, r[:, :, p % 2], r[:, :, p])
        for m, dst, src in ((2, 15, 0), (3, 15, 14), (4, 5, 0), (4, 9, 0), (5, 4, 1), (5, 6, 2), (6, 12, 3), (6, 8, 5)):
            r[:, :, dst] = np.where(kd == m, r[:, :, src], r[:, :, dst])
        return r
    w = walk(rng, o, top, P); w[z, b] = o[b][e[b][w[z, b]] // 3 * 3]
    return pack(x, tie(walk(rng, o, top, H)), tie(w))
def setup_inputs_calm(rng):
    o, top, x = ground(rng); q = rng.permutation(N)
    x[q[0]] = rng.integers(0, 3, (8, 16, W)); x[q[1]] = 15 * rng.integers(0, 2, (8, 16, W))
    x[:, int(rng.integers(0, 8))] = rng.integers(0, 3, (N, 16, W))
    e = np.argsort(o, axis=-1); home = e[None] % N == np.arange(N)[:, None, None]
    x = np.where(home[:, :, None], rng.integers(0, 3, x.shape), x)
    i = place(e, walk(rng, o, top, P)) // N * N + np.arange(N)[:, None, None, None]
    return pack(x, walk(rng, o, top, H), place(o, np.where(i < W, i, i - N)))
def setup_inputs_spread(rng):
    o = np.argsort(rng.random((8, W)), axis=-1); e = np.argsort(o, axis=-1) % 5
    x = np.floor(rng.random((N, 8, 16, W)) * np.exp2(4.0 - e)[None, :, None, :]).astype(np.int64)
    def some(n):
        k = rng.integers(0, 4, (N, 8, 1, n)); u = rng.random((N, 8, 16, n)); b = 5 * np.floor(u * (W // 5)).astype(np.int64)
        i = np.where(k == 0, np.floor(W * u).astype(np.int64), np.floor(W * u ** 4).astype(np.int64))
        i = np.where(k == 2, b + rng.integers(3, 5, u.shape), np.where(k == 3, b + rng.integers(2, 5, u.shape), i))
        return place(o, np.minimum(i, W - 1))
    return pack(x, some(H), some(P))
def check_inputs(d):
    bad = []; a = np.asarray(d["x"]).astype(np.float32)
    if not np.all((a >= 0) & (a <= 15) & (a == np.floor(a))): bad.append("whole numbers of x")
    for k in ("c0", "r0"):
        if np.min(d[k]) < 0 or np.max(d[k]) > W - 1: bad.append("range of " + k)
    return bad
def look(xs, R):
    return np.take_along_axis(xs, R.reshape(N, 8, 1, 16 * P), axis=3).reshape(N, 8, 16, 16, P)
def far(v, d):
    return np.add.reduce(np.abs(v[:, :, :, :16 - d] - v[:, :, :, d:]), axis=2)
def first(bad):
    return np.where(np.any(bad, axis=2), np.argmax(bad, axis=2), 15)[:, :, None, :]
def reference(x, c0, r0):
    xs = x.astype(np.float32).astype(np.int32).reshape(N, 8, 16, W); C = c0.astype(np.int64).reshape(N, 8, 16, H).copy()
    R = r0.astype(np.int64).reshape(N, 8, 16, P)
    kap = np.zeros(N, np.int64); row = np.arange(16)[None, None, :, None]
    for rnd in range(RO):
        if rnd > 0: R = np.roll(R, ST, axis=0)
        bad = far(look(xs, R), 1) > TH; fail = np.any(bad, axis=2); k = first(bad)
        rk = np.take_along_axis(R, k, 2)[:, :, 0]
        h = (((rk * R[:, :, 15]) >> 6) + rk + kap[:, None, None]) & (H - 1)
        R = np.where((row > k) & (row < 15), np.take_along_axis(C, h[:, :, None, :], 3), R)
        same = R[:, :, :, None] == R[:, :, None]
        q = 15 - np.argmax(same[:, :, :, ::-1], axis=3)
        p = first((q > row)[:, :, :15])
        R = np.where((row >= p) & (row <= np.take_along_axis(q, p, 2)), np.take_along_axis(R, p, 2), R)
        v = look(xs, R); k2 = first(far(v, 1) > TH)
        S = np.where((row > k2) & (row < 15), np.take_along_axis(R, k2, 2), R)
        for j in range(P - 1, -1, -1):
            a, g = np.nonzero(fail[:, :, j])
            C[a, g, :, h[a, g, j]] = S[:, :, :, j][a, g]
        near = far(v, 2) <= TH; R = R.copy()
        R[:, :, 1:14:2] = np.where(near[:, :, 0:13:2], R[:, :, 0:13:2], R[:, :, 1:14:2])
        kap = np.add.reduce(fail.astype(np.int64), axis=(1, 2))
    return {"yc": C.reshape(N, 128, H).astype(np.float32), "yr": R.reshape(N, 128, P).astype(np.float32)}

@@ -1,0 +1,489 @@
+from concourse.mybir import AluOpType, AxisListType, ActivationFunctionType
+
+OP = AluOpType
+ID = ActivationFunctionType.Identity
+ABS = ActivationFunctionType.Abs
+ROUNDS = 5
+TH = 36.0
+OFF = 2048.0
+NO = -8192.0
+CW = 2048 + 256
+NENG = 8
+BIG = float(2 ** 40)
+CFG = {"abs_a": True, "abs_b": False, "abs_2": True,
+       "gv_a": 16, "gv_b": 16, "gv0": (32, 64),
+       "ch_a": 2, "ch_b": 2,
+       "vf": 0.04, "wake": 0.1, "gam": 1.5,
+       "b0": 3.0, "bb": -4.0, "bs": -2.0, "ww": 0.005}
+
+SCRATCH = {
+    "xw": ("sbuf", [128, 4096], "bfloat16"), "cw": ("sbuf", [128, CW], "float32"), "ci": ("sbuf", [128, 2048], "int32"),
+    "ri": ("sbuf", [128, 256], "int32"), "pint": ("sbuf", [128, 4], "int32"), "pf": ("sbuf", [128, 4], "float32"),
+    "icol2": ("sbuf", [128, 256], "float32"), "gcol2": ("sbuf", [128, 256], "float32"),
+    "blk": ("sbuf", [128, 128], "float32"), "mask": ("sbuf", [128, 128], "float32"),
+    "m2": ("sbuf", [128, 256], "bfloat16"), "mq": ("sbuf", [128, 128], "bfloat16"), "mx": ("sbuf", [128, 128], "bfloat16"),
+    "i2": ("sbuf", [128, 128], "float16"), "ni": ("sbuf", [128, 128], "float16"), "c8": ("sbuf", [128, 128], "float16"),
+    "iw": ("sbuf", [128, 17, 128], "bfloat16"), "bo": ("sbuf", [128, 128], "float16"), "tri": ("sbuf", [128, 128], "float16"),
+    "pos": ("sbuf", [128, 256], "float16"), "gs": ("sbuf", [128, 3, 8], "bfloat16"), "gs16": ("sbuf", [128, 8], "float16"),
+    "kc": ("sbuf", [128, 128], "float16"), "cl": ("sbuf", [128, 16], "uint16"), "dumt": ("sbuf", [128, 16], "float32"),
+    "nf": ("sbuf", [128, 2, 16], "float16"), "kk": ("sbuf", [128, 8], "float32"),
+    "r0c": ("sbuf", [128, 2, 128], "float16"), "rl": ("sbuf", [128, 8, 128], "float16"), "rn": ("sbuf", [128, 10, 128], "float16"),
+    "Xm": ("sbuf", [128, 256], "float16"), "XmT": ("sbuf", [128, 256], "float16"), "hexp": ("sbuf", [128, 256], "float32"),
+    "Sc": ("sbuf", [128, 256], "float32"), "Ed": ("sbuf", [128, 4, 256], "bfloat16"), "hw": ("sbuf", [128, 16], "float32"),
+    "ow": ("sbuf", [128, 16], "uint16"), "lw": ("sbuf", [128, 16], "uint16"), "t1": ("sbuf", [128, 2, 16], "float32"),
+    "Pq": ("psum", [128, 512], "float32"), "Pw": ("psum", [128, 32, 16], "float32"),
+}
+for _u in "01":
+    for _n in ("X", "F", "V", "X4", "W2"):
+        SCRATCH[_n + "h" + _u] = ("sbuf", [128, 128], "bfloat16")
+    for _n in ("q1", "q2", "q4", "q6", "HK", "RP", "S", "crow"):
+        SCRATCH[_n + "h" + _u] = ("sbuf", [128, 128], "float16")
+    SCRATCH["R1h" + _u] = ("sbuf", [128, 8, 16], "float16")
+    for _n in ("SA", "Y", "RB"):
+        SCRATCH[_n + "h" + _u] = ("sbuf", [128, 128], "float32")
+    for _n in ("La", "Lb"):
+        SCRATCH[_n + "h" + _u] = ("sbuf", [128, 128], "uint16")
+    for _n in ("Ga", "Gb", "da", "db", "yb"):
+        SCRATCH[_n + "h" + _u] = ("sbuf", [128, 2048], "bfloat16")
+    for _n in ("d2", "y2"):
+        SCRATCH[_n + "h" + _u] = ("sbuf", [128, 1024], "bfloat16")
+    SCRATCH["Eh" + _u] = ("sbuf", [128, 8, 8, 16], "bfloat16")
+    SCRATCH["rkh" + _u] = ("sbuf", [128, 4, 8], "float32")
+    SCRATCH["sih" + _u] = ("sbuf", [128, 4, 8], "int32")
+    SCRATCH["hmh" + _u] = ("sbuf", [128, 8], "int32")
+    SCRATCH["Pn" + _u] = ("psum", [128, 16, 32], "float32")
+    SCRATCH["Pd" + _u] = ("psum", [128, 512], "float32")
+    SCRATCH["Pt" + _u] = ("psum", [128, 512], "float32")
+
+DMAS = ["ldr", "ldx0", "ldx1", "ldc", "sty0", "sty1", "stc0", "stc1"]
+SEMAPHORES = ["qv", "qs", "qt", "qg", "sent"] + ["arr%d" % k for k in range(8)] + DMAS
+
+
+def rank_program(g, core, T, topo):
+    rank = T.rank_of(core)
+    if rank is None:
+        return
+    n_ranks = len(T.cores)
+    nxt = T.cores[(rank + 1) % n_ranks]
+    eng = {"v": g.vector, "s": g.scalar, "t": g.tensor, "g": g, "y": g.sync}
+    ops, lastw, readers, banks = [], {}, {}, {}
+    cur = [0.0]
+
+    def add(q, fns, reads, writes, cost, sem=None, val=0, lat=0.0, deps=()):
+        k = len(ops)
+        need = set(deps)
+        for a in reads:
+            if a in lastw:
+                need.add(lastw[a])
+        for a in writes:
+            if a in lastw:
+                need.add(lastw[a])
+            need.update(readers.get(a, ()))
+        for a in set(a.split(":")[0] for a in list(reads) + list(writes) if a[0] == "P"):
+            acc = banks.setdefault(a, [])
+            need.update(i for qq, i in acc[-48:] if qq != q)
+            acc.append((q, k))
+        for a in reads:
+            readers.setdefault(a, []).append(k)
+        for a in writes:
+            lastw[a] = k
+            readers[a] = []
+        need.discard(k)
+        ops.append({"q": q, "f": fns, "need": need, "cost": cost, "sem": sem, "val": val, "lat": lat, "b": cur[0]})
+        return k
+
+    def dur(n, c=1.0):
+        return CFG["vf"] + max(64.0, n * c) * 0.00083 * 1.1
+
+    def size(ap):
+        r = 1
+        for s in ap.shape[1:]:
+            r *= s
+        return r
+
+    def tt(out, a, b, op, c=None):
+        ps = a[0][0] == "P" or b[0][0] == "P"
+        n = size(out[1])
+        return add("v", [lambda: g.vector.tensor_tensor(out=out[1], in0=a[1], in1=b[1], op=op)], [a[0], b[0]], [out[0]], dur(n, c or (1 if ps else 2)))
+
+    def ts(out, a, s1, op0, s2=None, op1=None, c=1.0, extra=()):
+        n = size(out[1])
+        if op1 is None:
+            f = lambda: g.vector.tensor_scalar(out=out[1], in0=a[1], scalar1=s1, scalar2=None, op0=op0)
+        else:
+            f = lambda: g.vector.tensor_scalar(out=out[1], in0=a[1], scalar1=s1, scalar2=s2, op0=op0, op1=op1)
+        return add("v", [f], [a[0]] + list(extra), [out[0]], dur(n, c))
+
+    def cp(out, a, c=1.0, extra=()):
+        return add("v", [lambda: g.vector.tensor_copy(out=out[1], in_=a[1])], [a[0]] + list(extra), [out[0]], dur(size(out[1]), c))
+
+    def scan(out, a, b, op0, op1, c=1.0):
+        return add("v", [lambda: g.vector.tensor_tensor_scan(out=out[1], data0=a[1], data1=b[1], initial=0.0, op0=op0, op1=op1)],
+                   [a[0], b[0]], [out[0]], dur(size(out[1]), c))
+
+    def fill(key, ap, v):
+        return add("v", [lambda: g.vector.memset(ap, v)], [], [key], dur(size(ap)))
+
+    def act(out, a, func, bias=0.0, scale=1.0, c=1.0, extra=()):
+        return add("s", [lambda: g.scalar.activation(out=out[1], in_=a[1], func=func, bias=bias, scale=scale)],
+                   [a[0]] + list(extra), [out[0]], dur(size(out[1]), c))
+
+    def mm(items, reads, writes):
+        fns, cost = [], 0.04
+        for o, l, r, st, sp in items:
+            fns.append(lambda o=o, l=l, r=r, st=st, sp=sp: g.tensor.matmul(out=o, lhsT=l, rhs=r, start=st, stop=sp))
+            cost += max(64, size(r)) * 0.00083 * 0.6
+        return add("t", fns, reads, writes, cost)
+
+    def B(name, u=None):
+        nm = name if u is None else "%sh%d" % (name, u)
+        return (nm, T[nm][:])
+
+    add("y", [lambda: g.sync.dma_start(T.ri[:], T.r0[:])], [], ["ri"], 0.1, "ldr", 16, 2.5)
+    add("s", [lambda: g.scalar.dma_start(T.xw[0:64, :], T.x[0:64, :])], [], ["xw"], 0.1, "ldx0", 16, 6.0)
+    add("y", [lambda: g.sync.dma_start(T.xw[64:128, :], T.x[64:128, :])], [], ["xw_"], 0.1, "ldx1", 16, 6.5)
+    add("y", [lambda: g.sync.dma_start(T.ci[:], T.c0[:])], [], ["ci"], 0.1, "ldc", 16, 5.5, deps=(1, 2))
+
+    add("g", [lambda: g.iota(T.pint[:, 0:1], [[0, 1]], 0, 1)], [], ["pint"], 0.2)
+    add("g", [lambda: g.iota(T.icol2[:], [[0, 16], [1, 16]], 0, 0, allow_small_or_imprecise_dtypes=True)], [], ["icol2"], 0.6)
+    add("g", [lambda: g.iota(T.gcol2[:], [[1, 16], [0, 16]], 0, 0, allow_small_or_imprecise_dtypes=True)], [], ["gcol2"], 0.6)
+    for u in (0, 1):
+        cp(B("La", u), ("ri", T.ri[:, 128 * u:128 * u + 128]))
+        ts(B("crow", u), ("ri", T.ri[:, 128 * u:128 * u + 128]), -OFF, OP.add)
+    ts(("pi2a", T.pint[:, 1:2]), ("pint", T.pint[:, 0:1]), 15, OP.bitwise_and)
+    ts(("pi2b", T.pint[:, 2:3]), ("pint", T.pint[:, 0:1]), 4, OP.arith_shift_right)
+    cp(("pmod", T.pf[:, 0:1]), ("pi2a", T.pint[:, 1:2]))
+    cp(("pdiv", T.pf[:, 1:2]), ("pi2b", T.pint[:, 2:3]))
+    pmod, pdiv = T.pf[:, 0:1], T.pf[:, 1:2]
+    ic, gc_ = ("icol2", T.icol2[:, 0:128]), ("gcol2", T.gcol2[:, 0:128])
+    heads = ("blk", T.blk[:, 0:128:16])
+    ts(B("mask"), ic, pmod, OP.is_equal, extra=["pmod"])
+    ts(B("blk"), gc_, pdiv, OP.is_equal, extra=["pdiv"])
+    tt(B("i2"), B("mask"), B("blk"), OP.mult)
+    ts(B("ni"), B("i2"), -1.0, OP.mult)
+    ts(B("c8"), ic, 0.0, OP.mult, NO, OP.add)
+    ts(B("kc"), ic, 0.0, OP.mult, -64.0 / OFF, OP.add)
+    cp(("gs0", T.gs[:, 0, :]), heads)
+    ts(("gs1", T.gs[:, 1, :]), heads, 2.0, OP.mult)
+    ts(("gs2", T.gs[:, 2, :]), heads, -1.0, OP.mult)
+    cp(B("gs16"), heads)
+    ts(B("m2"), B("icol2"), 0.0, OP.is_gt)
+    ts(B("mq"), ic, 0.0, OP.is_gt, 0.25, OP.mult)
+    cp(B("mx"), ("m2", T.m2[:, 0:128]))
+    fill("mx", T.mx[:, 15:128:16], 0.0)
+    cp(B("cl"), ("gcol2", T.gcol2[:, 0:256:16]))
+    cp(B("bo"), B("blk"))
+    ts(B("tri"), ic, pmod, OP.is_gt, extra=["pmod"])
+    tt(B("tri"), B("tri"), B("blk"), OP.mult)
+    ts(B("pos"), B("icol2"), pmod, OP.is_ge, OFF, OP.mult, extra=["pmod"])
+    ts(B("dumt"), ("gcol2", T.gcol2[:, 0:256:16]), 16.0, OP.mult, pmod, OP.add, extra=["pmod"])
+    ts(B("dumt"), B("dumt"), OFF, OP.add)
+    cp(("iw0", T.iw[:, 0, :]), B("i2"))
+    for d in range(1, 16):
+        act(("iw%d" % d, T.iw[:, d, :]), ("iw0", T.iw[:, 0, :]), ID, 0.0, float(4 ** d))
+    act(("iw16", T.iw[:, 16, :]), ("iw0", T.iw[:, 0, :]), ID, 0.0, -BIG)
+    for u in (0, 1):
+        P = T["Pd%d" % u]
+        fill("Pd%d:D1" % u, P[:, 0:128], 0.0)
+        fill("Pd%d:D2" % u, P[:, 128:256], 10000.0)
+        ts(B("q6", u), ic, 0.0, OP.mult, NO, OP.add)
+    fill("Pw:0", T.Pw[:, 0:8, :], 0.0)
+    fill("Pw:1", T.Pw[:, 8:16, :], 0.0)
+    fill("cw", T.cw[:, 2048:CW], 0.0)
+    for k in range(2):
+        cp(("cw", T.cw[:, 1024 * k:1024 * k + 1024]), ("ci", T.ci[:, 1024 * k:1024 * k + 1024]))
+    for u in (0, 1):
+        Pt = T["Pt%d" % u]
+        mm([(Pt[:, 0:128], T["crowh%d" % u][:], T.i2[:], True, True)], ["crowh%d" % u, "i2"], ["Pt%d:A" % u])
+        cp(("r0c%d" % u, T.r0c[:, u, :]), ("Pt%d:A" % u, Pt[:, 0:128]))
+
+    def gather(u, st, t):
+        L, G = T["L%sh%d" % (st, u)], T["G%sh%d" % (st, u)]
+        kl, win = "L%sh%d" % (st, u), T.xw[:, 0:4096]
+        nch, ndve = CFG["ch_" + st], CFG["gv_" + st]
+        if t == 0 and st == "a":
+            ndve = CFG["gv0"][u]
+        for ch in range(nch):
+            a, b = 128 // nch * ch, 128 // nch * (ch + 1)
+            key = "G%sh%d.%d" % (st, u, ch)
+            parts = []
+            if ch == nch - 1 and ndve:
+                parts = [("v", b - ndve, b)]
+                b -= ndve
+            if b > a:
+                parts.append(("s", a, b))
+            for q, a, b in parts:
+                o, i = G[:, 16 * a:16 * b], win.indirect(L[:, a:b])
+                if q == "s":
+                    act((key + q, o), ("xw", i), ID, 16.0, c=CFG["gam"], extra=["xw_", kl])
+                else:
+                    ts((key + q, o), ("xw", i), 16.0, OP.add, c=CFG["gam"], extra=["xw_", kl])
+
+    def dist(u, st, step):
+        G = T["G%sh%d" % (st, u)]
+        dn = "d2" if step == 2 else "d" + st
+        absact = CFG["abs_2" if step == 2 else "abs_" + st]
+        d = T["%sh%d" % (dn, u)]
+        y = d if absact else T["%sh%d" % ("y2" if step == 2 else "y" + st, u)]
+        nch = CFG["ch_" + st]
+        w = 2048 // nch
+        n = w // step
+        for ch in range(nch):
+            a, b = w * ch, w * ch + w
+            key = "G%sh%d.%d" % (st, u, ch)
+            kd, ky = "%sh%d.%d" % (dn, u, ch), "%sh%d.%d%s" % (dn, u, ch, "" if absact else "y")
+            o = d[:, n * ch:n * ch + n - 1]
+            add("v", [lambda o=o, a=a, b=b: g.vector.tensor_tensor_scan(out=o, data0=G[:, a:b - step:step], data1=G[:, a + step:b:step], initial=0.0, op0=OP.max, op1=OP.subtract)],
+                [key + "s", key + "v"], [kd], dur(n, 0.5))
+            yo = y[:, n * ch:n * ch + n - 1]
+            if absact:
+                act((ky, yo), (kd, o), ABS)
+            else:
+                ts((ky, yo), (kd, o), 0.0, OP.max, c=0.5)
+
+    def sums(u, st, step):
+        dn = "d2" if step == 2 else "d" + st
+        absact = CFG["abs_2" if step == 2 else "abs_" + st]
+        d = T["%sh%d" % (dn, u)]
+        P = T["Pd%d" % u]
+        items, wr = [], ["Pd%d:%s" % (u, "D1" if step == 1 else "D2")]
+        per = 16 // step
+        for p in range(7 if step == 2 else 15 if st == "a" else 14):
+            if step == 2:
+                o = P[:, 129 + 2 * p:256:16]
+            elif p < 14:
+                o = P[:, p + 1:128:16]
+            else:
+                o = P[:, 128:256:16]
+                wr.append("Pd%d:D2" % u)
+            if absact:
+                items.append((o, d[:, p:128 * per:per], T.gs[:, 0, :], True, True))
+            else:
+                y = T["%sh%d" % ("y2" if step == 2 else "y" + st, u)]
+                items.append((o, y[:, p:128 * per:per], T.gs[:, 1, :], True, False))
+                items.append((o, d[:, p:128 * per:per], T.gs[:, 2, :], False, True))
+        chs = range(CFG["ch_" + st])
+        rd = ["gs0", "gs1", "gs2"] + ["%sh%d.%d" % (dn, u, ch) for ch in chs] + ([] if absact else ["%sh%d.%dy" % (dn, u, ch) for ch in chs])
+        mm(items, rd, wr)
+
+    def hold(u, reg, out, q, rk, r):
+        P = T["Pd%d" % u]
+        z = {"C": 256, "RB": 384}[reg]
+        kp = "Pd%d:%s" % (u, reg)
+        o = P[:, z:z + 128]
+        mm([(o, T.i2[:], r, True, False), (o, T.i2[:], T.c8[:], False, False), (o, T.ni[:], q[1], False, True)], [rk, q[0], "i2", "c8", "ni"], [kp])
+        scan(out, q, (kp, o), OP.add, OP.max)
+        return kp, o
+
+    def stage_a(t, u):
+        Pn, Pd, Pt = T["Pn%d" % u], T["Pd%d" % u], T["Pt%d" % u]
+        kn, kt, kX = "Pn%d:R" % u, "Pt%d:A" % u, "Xh%d" % u
+        if t == 0:
+            slot, r = "r0c%d" % u, T.r0c[:, u, :]
+        else:
+            slot, r = "rl%d" % (2 * (t - 1) + u), T.rl[:, 2 * (t - 1) + u, :]
+            mm([(Pt[:, 0:128], r, T.i2[:], True, True)], [slot, "i2"], [kt])
+            ts(B("La", u), (kt, Pt[:, 0:128]), OFF, OP.add)
+        gather(u, "a", t)
+        dist(u, "a", 1)
+        sums(u, "a", 1)
+        X = T["Xh%d" % u]
+        scan(B("X", u), B("mx"), ("Pd%d:D1" % u, Pd[:, 0:128]), OP.mult, OP.max)
+        ts(B("q1", u), B("X", u), TH, OP.is_le, NO, OP.mult, c=0.5)
+        kp, rb = hold(u, "RB", B("HK", u), B("q1", u), slot, r)
+        sm, si = T["rkh%d" % u], T["sih%d" % u]
+        ks, kr = "sih%d." % u, "rkh%d." % u
+        HK = T["HKh%d" % u]
+        ts((ks + "q", si[:, 0, :]), (kp, Pd[:, 399:512:16]), OFF + 64.0, OP.add)
+        ts((ks + "m", si[:, 1, :]), (ks + "q", si[:, 0, :]), 63, OP.bitwise_and)
+        if t > 0:
+            ts((kr + "b", sm[:, 2, :]), (ks + "m", si[:, 1, :]), 2048.0, OP.mult, T.kk[:, t - 1:t], OP.add, extra=["kk%d" % (t - 1)])
+        else:
+            ts((kr + "b", sm[:, 2, :]), (ks + "m", si[:, 1, :]), 2048.0, OP.mult)
+        tt((kr + "p", sm[:, 0, :]), ("HKh%d" % u, HK[:, 14:128:16]), (ks + "q", si[:, 0, :]), OP.mult)
+        tt((ks + "s", si[:, 2, :]), (kr + "p", sm[:, 0, :]), (kr + "b", sm[:, 2, :]), OP.add)
+        ts((ks + "h", si[:, 3, :]), (ks + "s", si[:, 2, :]), 6, OP.arith_shift_right, 2047, OP.bitwise_and)
+        act(B("RB", u), (kp, rb), ID)
+        tt((kr + "xf", sm[:, 3, :]), (kX, X[:, 14:128:16]), ("Pd%d:D2" % u, Pd[:, 128:256:16]), OP.max)
+        nf = ("nf%d.%d" % (t % 2, u), T.nf[:, t % 2, 8 * u:8 * u + 8])
+        ts(nf, (kr + "xf", sm[:, 3, :]), TH, OP.is_le, OFF, OP.mult)
+        tt(B("hm", u), (ks + "h", si[:, 3, :]), nf, OP.max)
+        Xm = T.Xm[:, 128 * u:128 * u + 128]
+        add("v", [lambda: g.vector.tensor_tensor(out=Xm, in0=T["hmh%d" % u][:, 0:8].indirect(T.cl[:, 0:8]), in1=T.mask[:], op=OP.mult)],
+            ["hmh%d" % u, "cl", "mask"], ["Xm%d" % u], dur(128, CFG["gam"]))
+        mm([(Pt[:, 0:8], Xm, T.gs16[:], True, True)], ["Xm%d" % u, "gs16"], [kt])
+        ow = ("ow%d" % u, T.ow[:, 8 * u:8 * u + 8])
+        cp(ow, (kt, Pt[:, 0:8]))
+        ts(B("crow", u), ("cw", T.cw[:, 0:CW].indirect(ow[1])), -OFF, OP.add, c=CFG["gam"], extra=[ow[0]])
+        kc, C = "Pd%d:C" % u, Pd[:, 256:384]
+        mm([(C, T["crowh%d" % u][:], T.i2[:], True, False), (C, T.i2[:], T["q1h%d" % u][:], False, True)], ["crowh%d" % u, "q1h%d" % u, "i2"], [kc])
+        tt(B("R1", u), B("RB", u), (kc, C), OP.max)
+        R1, E = T["R1h%d" % u], T["Eh%d" % u]
+        mm([(Pn[:, 0:8, 0:16], T.i2[:], R1[:], True, True), (Pn[:, 0:8, 16:24], T.i2[:], R1[:, :, 0:8], True, True)], ["R1h%d" % u, "i2"], [kn])
+        kw, W = "Pw:%d" % u, T.Pw[:, 8 * u:8 * u + 8, :]
+        for d in range(1, 9):
+            n = 16 if d < 8 else 8
+            ke, e = "Eh%d.%d" % (u, d), 16 - d
+            tt((ke, E[:, d - 1, :, 0:n]), ("R1h%d" % u, R1[:, :, 0:n]), (kn, Pn[:, 0:8, d:d + n]), OP.is_equal)
+            its = [(T.Pw[:, 8 * u:8 * u + 8, 1:e + 1], T.iw[:, d, :], E[:, d - 1, :, 0:e], d == 1, d == 8)]
+            if d < 8:
+                its.append((T.Pw[:, 8 * u:8 * u + 8, 1:d + 1], T.iw[:, e, :], E[:, d - 1, :, e:16], False, False))
+            mm(its, [ke, "iw%d" % d, "iw%d" % e], [kw])
+        cp(B("W2", u), (kw, W))
+        scan(B("F", u), ("m2", T.m2[:, 0:128]), B("W2", u), OP.mult, OP.max, 0.5)
+        mm([(C, T.iw[:, 0, :], T["W2h%d" % u][:], True, False), (Pd[:, 257:384], T.iw[:, 16, :], T["Fh%d" % u][:, 0:127], False, True)],
+           ["W2h%d" % u, "Fh%d" % u, "iw0", "iw16"], [kc])
+        scan(B("V", u), B("mq"), (kc, C), OP.mult, OP.max)
+        ts(B("q2", u), B("V", u), 4.0, OP.is_lt, NO, OP.mult, c=0.5)
+        hold(u, "RB", B("RP", u), B("q2", u), "R1h%d" % u, R1[:])
+        mm([(Pt[:, 0:128], T["RPh%d" % u][:], T.i2[:], True, True)], ["RPh%d" % u, "i2"], [kt])
+        ts(B("Lb", u), (kt, Pt[:, 0:128]), OFF, OP.add)
+
+    def stage_b(t, u):
+        Pd, Pt = T["Pd%d" % u], T["Pt%d" % u]
+        kt = "Pt%d:A" % u
+        RP = T["RPh%d" % u][:]
+        gather(u, "b", t)
+        dist(u, "b", 2)
+        dist(u, "b", 1)
+        sums(u, "b", 2)
+        ts(("q6h%d" % u, T["q6h%d" % u][:, 1:128:2]), ("Pd%d:D2" % u, Pd[:, 129:256:2]), TH, OP.is_gt, NO, OP.mult)
+        k = 2 * t + u
+        slot, rn = "rn%d" % k, T.rn[:, k, :]
+        hold(u, "RB", (slot, rn), B("q6", u), "RPh%d" % u, RP)
+        if t < ROUNDS - 1:
+            rid, pid, _s = topo.addr(nxt)
+            m = 0
+            for e in topo.engines(core, nxt)[:NENG]:
+                m |= 1 << e
+            sd = add("g", [lambda: g.remote_dma(out_ap=T.rl[:, k, :], in_ap=rn, remote_sem=T.sem["arr%d" % k], local_sem=T.sem.sent, pid=pid, routing_id=rid, dma_engine_mask=m)],
+                     [slot], [], 0.3, "none", 0, 1.7)
+            add(None, [], [], ["rl%d" % k], 0.0, "arr%d" % k, NENG, 0.0, deps=[sd])
+        sums(u, "b", 1)
+        scan(B("X4", u), B("mx"), ("Pd%d:D1" % u, Pd[:, 0:128]), OP.mult, OP.max)
+        ts(B("q4", u), B("X4", u), TH, OP.is_le, NO, OP.mult, c=0.5)
+        hold(u, "C", B("S", u), B("q4", u), "RPh%d" % u, RP)
+        mm([(Pt[:, 0:128], T["Sh%d" % u][:], T.i2[:], True, True)], ["Sh%d" % u, "i2"], [kt])
+        act(B("SA", u), (kt, Pt[:, 0:128]), ID, OFF)
+        if t == ROUNDS - 1:
+            mm([(Pt[:, 128:256], rn, T.i2[:], True, True)], [slot, "i2"], ["Pt%d:Y" % u])
+            act(B("Y", u), ("Pt%d:Y" % u, Pt[:, 128:256]), ID, OFF)
+            add("y", [lambda: g.sync.dma_start(T.yr[:, 128 * u:128 * u + 128], T["Yh%d" % u][:])], ["Yh%d" % u], [], 0.1, "sty%d" % u, 16, 2.0)
+
+    def count(t):
+        f = T.nf[:, t % 2, :]
+        mm([(T.Pt1[:, 256:272], T.kc[:], f, True, True)], ["nf%d.0" % (t % 2), "nf%d.1" % (t % 2), "kc"], ["Pt1:K"])
+        add("v", [lambda: g.vector.tensor_reduce(out=T.kk[:, t:t + 1], in_=T.Pt1[:, 256:272], axis=AxisListType.X, op=OP.add)], ["Pt1:K"], ["kk%d" % t], dur(16))
+
+    def winners():
+        q = T.Pq
+        mm([(q[:, 128 * u:128 * u + 128], T.Xm[:, 128 * u:128 * u + 128], T.i2[:], True, True) for u in (0, 1)], ["Xm0", "Xm1", "i2"], ["Pq:L"])
+        cp(B("XmT"), ("Pq:L", q[:, 0:256]))
+        cp(B("hw"), ("ow0", T.ow[:]), extra=["ow1"])
+        act(B("hexp"), ("hw", T.hw[:, 0:16].indirect(T.cl[:, 0:16])), ID, c=CFG["gam"], extra=["cl"])
+        mm([(q[:, 0:256], T.bo[:], T.XmT[:], True, True)], ["XmT", "bo"], ["Pq:L"])
+        mm([(q[:, 256:512], T.tri[:], T.XmT[:], True, False), (q[:, 256:512], T.i2[:], T.pos[:], False, True)], ["XmT", "tri", "i2", "pos"], ["Pq:R"])
+        for k in range(4):
+            w = 256 - 16 * k
+            a = ("Pq:R", q[:, 256:512]) if k == 0 else ("Pq:L", q[:, 0:w])
+            tt(("Ed%d" % k, T.Ed[:, k, 0:w]), ("hexp", T.hexp[:, 16 * k:256]), a, OP.is_equal)
+        mm([(q[:, 16 * k:256], T.iw[:, 6, :], T.Ed[:, k, 0:256 - 16 * k], k == 0, k == 3) for k in range(4)],
+           ["Ed%d" % k for k in range(4)] + ["iw6"], ["Pq:L"])
+        scan(B("Sc"), B("m2"), ("Pq:L", q[:, 0:256]), OP.mult, OP.max)
+        tt(("t1a", T.t1[:, 0, :]), ("Sc", T.Sc[:, 15:256:16]), B("dumt"), OP.min)
+        tt(("t1b", T.t1[:, 1, :]), ("t1a", T.t1[:, 0, :]), B("hw"), OP.max)
+        cp(B("lw"), ("t1b", T.t1[:, 1, :]))
+
+    def scatter(u):
+        for k in (1, 0):
+            o = T.cw[:, 0:CW].indirect(T.lw[:, 8 * u + 4 * k:8 * u + 4 * k + 4])
+            add("v", [lambda o=o, k=k: g.vector.tensor_copy(out=o, in_=T["SAh%d" % u][:, 64 * k:64 * k + 64])], ["SAh%d" % u, "lw"], ["cw"], dur(64, 3.5))
+
+    for t in range(ROUNDS):
+        cur[0] = CFG["b0"]
+        stage_a(t, 0)
+        cur[0] = 0.0
+        stage_a(t, 1)
+        if t < ROUNDS - 1:
+            count(t)
+        winners()
+        cur[0] = CFG["b0"] + CFG["bb"]
+        stage_b(t, 0)
+        cur[0] = CFG["bb"]
+        stage_b(t, 1)
+        cur[0] = CFG["bs"]
+        scatter(1)
+        scatter(0)
+    add("s", [lambda: g.scalar.dma_start(T.yc[0:64, :], T.cw[0:64, 0:2048])], ["cw"], [], 0.1, "stc0", 16, 5.0)
+    add("y", [lambda: g.sync.dma_start(T.yc[64:128, :], T.cw[64:128, 0:2048])], ["cw"], [], 0.1, "stc1", 16, 5.0)
+
+    n = len(ops)
+    users = [[] for _ in range(n)]
+    for k, o in enumerate(ops):
+        for d in o["need"]:
+            users[d].append(k)
+    way = [0.0] * n
+    for k in range(n - 1, -1, -1):
+        o = ops[k]
+        way[k] = o["cost"] + o["lat"] + CFG["wake"] + max([way[j] for j in users[k]] or [0.0])
+    way = [w + o["b"] for w, o in zip(way, ops)]
+    left = [len(o["need"]) for o in ops]
+    at = [0.0] * n
+    free = {q: 0.0 for q in ("v", "s", "t", "g", "y", None)}
+    pool = [k for k in range(n) if left[k] == 0]
+    order = []
+    while pool:
+        best, bs, bst = None, None, 0.0
+        for k in pool:
+            o = ops[k]
+            st = max(free[o["q"]] if o["q"] else 0.0, at[k])
+            key = (st - CFG["ww"] * way[k], -way[k])
+            if bs is None or key < bs:
+                best, bs, bst = k, key, st
+        pool.remove(best)
+        o = ops[best]
+        st = bst
+        if o["q"]:
+            free[o["q"]] = st + o["cost"]
+        done = st + o["cost"] + o["lat"]
+        order.append(best)
+        for j in users[best]:
+            lag = 0.0 if ops[j]["q"] == o["q"] == "t" else CFG["wake"]
+            at[j] = max(at[j], done + lag)
+            left[j] -= 1
+            if left[j] == 0:
+                pool.append(j)
+    CFG["ms"] = max(free.values())
+
+    total = {"qv": 0, "qs": 0, "qt": 0, "qg": 0}
+    known = {q: {} for q in eng}
+    for k in order:
+        o = ops[k]
+        q = o["q"]
+        if q is None:
+            continue
+        want = {}
+        for d in o["need"]:
+            p = ops[d]
+            if p["sem"] == "none" or (p["q"] == q and q == "t"):
+                continue
+            want[p["sem"]] = max(want.get(p["sem"], 0), p["val"])
+        for s in sorted(want):
+            if known[q].get(s, 0) < want[s]:
+                known[q][s] = want[s]
+                eng[q].wait_ge(T.sem[s], want[s])
+        fresh = o["sem"] is None
+        for f in o["f"]:
+            ins = f()
+            if fresh:
+                o["sem"] = "q" + q
+                total["q" + q] += 1
+                o["val"] = total["q" + q]
+                ins.then_inc(T.sem["q" + q], 1)
+            elif o["sem"] != "none":
+                ins.then_inc(T.sem[o["sem"]], 16)
+    for s in sorted(total):
+        g.wait_ge(T.sem[s], total[s])
+    for s in DMAS:
+        g.wait_ge(T.sem[s], 16)
+    g.wait_ge(T.sem.sent, 2 * (ROUNDS - 1) * NENG)

@@ -1,62 +1,70 @@
-from concourse.mybir import AluOpType, AxisListType, ActivationFunctionType
+from concourse.bass import DstId, RemoteDMATransfer
+from concourse.mybir import AluOpType, ActivationFunctionType
 
 OP = AluOpType
 ID = ActivationFunctionType.Identity
-ABS = ActivationFunctionType.Abs
+RELU = ActivationFunctionType.Relu
+SIGN = ActivationFunctionType.Sign
 ROUNDS = 5
-TH = 36.0
+TH = 36.5
 OFF = 2048.0
 NO = -8192.0
-CW = 2048 + 256
-NENG = 8
-BIG = float(2 ** 40)
-CFG = {"abs_a": True, "abs_b": False, "abs_2": True,
-       "gv_a": 16, "gv_b": 16, "gv0": (32, 64),
+CW = 2048 + 16
+NENG = 16
+TOP = float(2 ** 20)
+CFG = {"gv_a": 0, "gv_b": 0, "gv0": (48, 48), "gv4": 32,
        "ch_a": 2, "ch_b": 2,
-       "vf": 0.04, "wake": 0.1, "gam": 1.5,
-       "b0": 3.0, "bb": -4.0, "bs": -2.0, "ww": 0.005}
+       "e_dp": "s", "e_wt": "s", "e_dn": "s",
+       "vf": 0.04, "wake": 0.1, "gam": 1.5, "pe": 0.42,
+       "b0": 3.0, "ba": 0.0, "bb": 0.0, "bs": -2.0, "bc": -30.0, "lr": 2.7, "lx": 6.0, "look": 0.0, "gain": 0.1, "iters": 8}
+PLAN = []
 
 SCRATCH = {
-    "xw": ("sbuf", [128, 4096], "bfloat16"), "cw": ("sbuf", [128, CW], "float32"), "ci": ("sbuf", [128, 2048], "int32"),
-    "ri": ("sbuf", [128, 256], "int32"), "pint": ("sbuf", [128, 4], "int32"), "pf": ("sbuf", [128, 4], "float32"),
-    "icol2": ("sbuf", [128, 256], "float32"), "gcol2": ("sbuf", [128, 256], "float32"),
-    "blk": ("sbuf", [128, 128], "float32"), "mask": ("sbuf", [128, 128], "float32"),
-    "m2": ("sbuf", [128, 256], "bfloat16"), "mq": ("sbuf", [128, 128], "bfloat16"), "mx": ("sbuf", [128, 128], "bfloat16"),
-    "i2": ("sbuf", [128, 128], "float16"), "ni": ("sbuf", [128, 128], "float16"), "c8": ("sbuf", [128, 128], "float16"),
-    "iw": ("sbuf", [128, 17, 128], "bfloat16"), "bo": ("sbuf", [128, 128], "float16"), "tri": ("sbuf", [128, 128], "float16"),
-    "pos": ("sbuf", [128, 256], "float16"), "gs": ("sbuf", [128, 3, 8], "bfloat16"), "gs16": ("sbuf", [128, 8], "float16"),
-    "kc": ("sbuf", [128, 128], "float16"), "cl": ("sbuf", [128, 16], "uint16"), "dumt": ("sbuf", [128, 16], "float32"),
-    "nf": ("sbuf", [128, 2, 16], "float16"), "kk": ("sbuf", [128, 8], "float32"),
-    "r0c": ("sbuf", [128, 2, 128], "float16"), "rl": ("sbuf", [128, 8, 128], "float16"), "rn": ("sbuf", [128, 10, 128], "float16"),
-    "Xm": ("sbuf", [128, 256], "float16"), "XmT": ("sbuf", [128, 256], "float16"), "hexp": ("sbuf", [128, 256], "float32"),
-    "Sc": ("sbuf", [128, 256], "float32"), "Ed": ("sbuf", [128, 4, 256], "bfloat16"), "hw": ("sbuf", [128, 16], "float32"),
-    "ow": ("sbuf", [128, 16], "uint16"), "lw": ("sbuf", [128, 16], "uint16"), "t1": ("sbuf", [128, 2, 16], "float32"),
-    "Pq": ("psum", [128, 512], "float32"), "Pw": ("psum", [128, 32, 16], "float32"),
+    "xw": ("sbuf", [128, 4096], "bfloat16"), "cw": ("sbuf", [128, CW], "float32"), "cf": ("sbuf", [128, CW], "float32"),
+    "ci": ("sbuf", [128, 2048], "int32"), "ri": ("sbuf", [128, 256], "int32"),
+    "pint": ("sbuf", [128, 4], "int32"), "pf": ("sbuf", [128, 16], "float32"),
+    "ic": ("sbuf", [128, 128], "float32"), "gcl": ("sbuf", [128, 128], "float32"), "pd": ("sbuf", [128, 128], "float32"),
+    "cm": ("sbuf", [128, 128], "float32"), "ev": ("sbuf", [128, 64], "float32"), "fw": ("sbuf", [128, 64], "float32"),
+    "cy": ("sbuf", [128, 192], "bfloat16"), "sely": ("sbuf", [128, 192], "float16"), "dm": ("sbuf", [128, 64], "float16"),
+    "ca": ("sbuf", [128, 8, 24], "bfloat16"), "cb1": ("sbuf", [128, 8, 16], "bfloat16"), "cb2": ("sbuf", [128, 8, 8], "bfloat16"),
+    "gs4": ("sbuf", [128, 8, 4], "bfloat16"), "gm": ("sbuf", [128, 8], "bfloat16"), "hd": ("sbuf", [128, 8], "float32"),
+    "blk": ("sbuf", [128, 128], "float32"), "mask": ("sbuf", [128, 128], "float32"), "i4": ("sbuf", [128, 128], "float32"),
+    "t0": ("sbuf", [128, 128], "float32"), "t1": ("sbuf", [128, 128], "float32"), "t2": ("sbuf", [128, 128], "float32"),
+    "c15": ("sbuf", [128, 144], "float16"), "pair": ("sbuf", [128, 8, 128], "float16"), "wm": ("sbuf", [128, 16, 128], "float16"),
+    "wt": ("sbuf", [128, 16], "bfloat16"), "w16": ("sbuf", [128, 6, 16], "float32"), "lohi": ("sbuf", [128, 2, 16], "float32"),
+    "kc": ("sbuf", [128, 128], "float32"), "acc": ("sbuf", [128, 4], "float32"), "ft": ("sbuf", [128, 256], "bfloat16"),
+    "qi": ("sbuf", [128, 2, 16], "int32"), "qb": ("sbuf", [128, 4, 32], "float32"), "bk": ("sbuf", [128, 16], "float32"),
+    "hs": ("sbuf", [128, 16], "float32"), "hi": ("sbuf", [128, 2, 16], "int32"), "ow": ("sbuf", [128, 16], "uint16"),
+    "h16": ("sbuf", [128, 16], "float16"), "ew": ("sbuf", [128, 256], "bfloat16"), "lw": ("sbuf", [128, 32], "uint16"),
+    "la": ("sbuf", [128, 10, 128], "uint16"), "lb": ("sbuf", [128, 10, 128], "uint16"),
+    "ns": ("sbuf", [128, 10, 8, 8], "bfloat16"), "nl": ("sbuf", [128, 8, 8, 8], "bfloat16"),
+    "PE0": ("psum", [128, 512], "float32"), "PE1": ("psum", [128, 512], "float32"),
 }
+for _n in ("i2", "ni", "c8", "bm", "am"):
+    SCRATCH[_n] = ("sbuf", [128, 128], "float16")
+for _n in ("ib", "nib", "pk", "nk", "ib4", "c2k", "mp", "posw", "g10", "gw"):
+    SCRATCH[_n] = ("sbuf", [128, 128], "bfloat16")
 for _u in "01":
-    for _n in ("X", "F", "V", "X4", "W2"):
+    for _n in ("WT", "Dn", "p4", "X4"):
         SCRATCH[_n + "h" + _u] = ("sbuf", [128, 128], "bfloat16")
-    for _n in ("q1", "q2", "q4", "q6", "HK", "RP", "S", "crow"):
+    for _n in ("RA", "R1", "q2", "RP", "S"):
         SCRATCH[_n + "h" + _u] = ("sbuf", [128, 128], "float16")
-    SCRATCH["R1h" + _u] = ("sbuf", [128, 8, 16], "float16")
-    for _n in ("SA", "Y", "RB"):
+    for _n in ("SA", "Z", "dl", "Y"):
         SCRATCH[_n + "h" + _u] = ("sbuf", [128, 128], "float32")
-    for _n in ("La", "Lb"):
-        SCRATCH[_n + "h" + _u] = ("sbuf", [128, 128], "uint16")
-    for _n in ("Ga", "Gb", "da", "db", "yb"):
+    for _n in ("Ga", "Gb", "Ma", "Mb"):
         SCRATCH[_n + "h" + _u] = ("sbuf", [128, 2048], "bfloat16")
-    for _n in ("d2", "y2"):
+    for _n in ("Na", "Nb", "E"):
         SCRATCH[_n + "h" + _u] = ("sbuf", [128, 1024], "bfloat16")
-    SCRATCH["Eh" + _u] = ("sbuf", [128, 8, 8, 16], "bfloat16")
-    SCRATCH["rkh" + _u] = ("sbuf", [128, 4, 8], "float32")
-    SCRATCH["sih" + _u] = ("sbuf", [128, 4, 8], "int32")
-    SCRATCH["hmh" + _u] = ("sbuf", [128, 8], "int32")
-    SCRATCH["Pn" + _u] = ("psum", [128, 16, 32], "float32")
-    SCRATCH["Pd" + _u] = ("psum", [128, 512], "float32")
-    SCRATCH["Pt" + _u] = ("psum", [128, 512], "float32")
+    SCRATCH["Dph" + _u] = ("sbuf", [128, 192], "bfloat16")
+    SCRATCH["Wh" + _u] = ("sbuf", [128, 192], "float32")
+    SCRATCH["Wch" + _u] = ("sbuf", [128, 10], "bfloat16")
+    SCRATCH["Tah" + _u] = ("sbuf", [128, 144], "float16")
+    SCRATCH["PA" + _u] = ("psum", [128, 8, 64], "float32")
+    SCRATCH["PB" + _u] = ("psum", [128, 8, 64], "float32")
+    SCRATCH["PM" + _u] = ("psum", [128, 512], "float32")
 
 DMAS = ["ldr", "ldx0", "ldx1", "ldc", "sty0", "sty1", "stc0", "stc1"]
-SEMAPHORES = ["qv", "qs", "qt", "qg", "sent"] + ["arr%d" % k for k in range(8)] + DMAS
+SEMAPHORES = ["qv", "qs", "qt", "qg", "sent"] + ["arq%d" % d for d in (1, 2, 3)] + ["arl%d" % k for k in range(8)] + ["arn%d" % k for k in range(8)] + DMAS
 
 
 def rank_program(g, core, T, topo):
@@ -79,17 +87,14 @@ def rank_program(g, core, T, topo):
             if a in lastw:
                 need.add(lastw[a])
             need.update(readers.get(a, ()))
-        for a in set(a.split(":")[0] for a in list(reads) + list(writes) if a[0] == "P"):
-            acc = banks.setdefault(a, [])
-            need.update(i for qq, i in acc[-48:] if qq != q)
-            acc.append((q, k))
+        bank = sorted(set(a.split(":")[0] for a in list(reads) + list(writes) if a[0] == "P"))
         for a in reads:
             readers.setdefault(a, []).append(k)
         for a in writes:
             lastw[a] = k
             readers[a] = []
         need.discard(k)
-        ops.append({"q": q, "f": fns, "need": need, "cost": cost, "sem": sem, "val": val, "lat": lat, "b": cur[0]})
+        ops.append({"q": q, "f": fns, "need": need, "cost": cost, "sem": sem, "val": val, "lat": lat, "b": cur[0], "bank": bank, "st": False, "sp": False})
         return k
 
     def dur(n, c=1.0):
@@ -101,10 +106,10 @@ def rank_program(g, core, T, topo):
             r *= s
         return r
 
-    def tt(out, a, b, op, c=None):
+    def tt(out, a, b, op, c=None, extra=()):
         ps = a[0][0] == "P" or b[0][0] == "P"
         n = size(out[1])
-        return add("v", [lambda: g.vector.tensor_tensor(out=out[1], in0=a[1], in1=b[1], op=op)], [a[0], b[0]], [out[0]], dur(n, c or (1 if ps else 2)))
+        return add("v", [lambda: g.vector.tensor_tensor(out=out[1], in0=a[1], in1=b[1], op=op)], [a[0], b[0]] + list(extra), [out[0]], dur(n, c or (1 if ps else 2)))
 
     def ts(out, a, s1, op0, s2=None, op1=None, c=1.0, extra=()):
         n = size(out[1])
@@ -117,343 +122,486 @@ def rank_program(g, core, T, topo):
     def cp(out, a, c=1.0, extra=()):
         return add("v", [lambda: g.vector.tensor_copy(out=out[1], in_=a[1])], [a[0]] + list(extra), [out[0]], dur(size(out[1]), c))
 
-    def scan(out, a, b, op0, op1, c=1.0):
+    def scan(out, a, b, op0, op1, c=1.0, extra=()):
         return add("v", [lambda: g.vector.tensor_tensor_scan(out=out[1], data0=a[1], data1=b[1], initial=0.0, op0=op0, op1=op1)],
-                   [a[0], b[0]], [out[0]], dur(size(out[1]), c))
+                   [a[0], b[0]] + list(extra), [out[0]], dur(size(out[1]), c))
 
     def fill(key, ap, v):
         return add("v", [lambda: g.vector.memset(ap, v)], [], [key], dur(size(ap)))
 
-    def act(out, a, func, bias=0.0, scale=1.0, c=1.0, extra=()):
-        return add("s", [lambda: g.scalar.activation(out=out[1], in_=a[1], func=func, bias=bias, scale=scale)],
-                   [a[0]] + list(extra), [out[0]], dur(size(out[1]), c))
+    def act(out, a, func, bias=0.0, scale=1.0, c=1.0, extra=(), acc=None):
+        kw = {"accum_out": acc[1]} if acc else {}
+        return add("s", [lambda: g.scalar.activation(out=out[1], in_=a[1], func=func, bias=bias, scale=scale, **kw)],
+                   [a[0]] + list(extra), [out[0]] + ([acc[0]] if acc else []), dur(size(out[1]), c))
 
-    def mm(items, reads, writes):
-        fns, cost = [], 0.04
-        for o, l, r, st, sp in items:
-            fns.append(lambda o=o, l=l, r=r, st=st, sp=sp: g.tensor.matmul(out=o, lhsT=l, rhs=r, start=st, stop=sp))
-            cost += max(64, size(r)) * 0.00083 * 0.6
-        return add("t", fns, reads, writes, cost)
+    def mm(items, reads, writes, st=True, sp=True, c=1):
+        fns, cost = [], 0.0
+        for n, (o, l, r) in enumerate(items):
+            a, b = st and n == 0, sp and n == len(items) - 1
+            fns.append(lambda o=o, l=l, r=r, a=a, b=b: g.tensor.matmul(out=o, lhsT=l, rhs=r, start=a, stop=b))
+            cost += max(64, size(r)) * 0.001 * CFG["pe"] * 1.1 * c
+        k = add("t", fns, reads, writes, cost, lat=0.05)
+        ops[k]["st"], ops[k]["sp"] = st, sp
+        return k
+
+    def iota(name, pat, base):
+        add("g", [lambda: g.iota(T[name][:], pat, base, 0, allow_small_or_imprecise_dtypes=True)], [], [name], 0.13 + size(T[name][:]) * 0.002)
 
     def B(name, u=None):
         nm = name if u is None else "%sh%d" % (name, u)
         return (nm, T[nm][:])
 
-    add("y", [lambda: g.sync.dma_start(T.ri[:], T.r0[:])], [], ["ri"], 0.1, "ldr", 16, 2.5)
-    add("s", [lambda: g.scalar.dma_start(T.xw[0:64, :], T.x[0:64, :])], [], ["xw"], 0.1, "ldx0", 16, 6.0)
-    add("y", [lambda: g.sync.dma_start(T.xw[64:128, :], T.x[64:128, :])], [], ["xw_"], 0.1, "ldx1", 16, 6.5)
+    def mask_to(dst):
+        m = 0
+        for e in topo.engines(core, dst)[:NENG]:
+            m |= 1 << e
+        return m
+
+    def send(src, dst, sem):
+        rid, pid, _s = topo.addr(nxt)
+        sd = add("g", [lambda: g.remote_dma(out_ap=dst[1], in_ap=src[1], remote_sem=T.sem[sem], local_sem=T.sem.sent, pid=pid, routing_id=rid, dma_engine_mask=mask_to(nxt))],
+                 [src[0]], [], 0.3, "none", 0, 1.7)
+        add(None, [], [], [dst[0]], 0.0, sem, NENG, 0.0, deps=[sd])
+
+    g.sync.dma_start(T.ri[:], T.r0[:]).then_inc(T.sem.ldr, 16)
+    g.scalar.dma_start(T.xw[0:64, :], T.x[0:64, :]).then_inc(T.sem.ldx0, 16)
+    g.sync.dma_start(T.xw[64:128, :], T.x[64:128, :]).then_inc(T.sem.ldx1, 16)
+    add(None, [], [], ["ri"], 0.0, "ldr", 16, CFG["lr"])
+    add(None, [], [], ["xw"], 0.0, "ldx0", 16, CFG["lx"])
+    add(None, [], [], ["xw_"], 0.0, "ldx1", 16, CFG["lx"])
     add("y", [lambda: g.sync.dma_start(T.ci[:], T.c0[:])], [], ["ci"], 0.1, "ldc", 16, 5.5, deps=(1, 2))
 
     add("g", [lambda: g.iota(T.pint[:, 0:1], [[0, 1]], 0, 1)], [], ["pint"], 0.2)
-    add("g", [lambda: g.iota(T.icol2[:], [[0, 16], [1, 16]], 0, 0, allow_small_or_imprecise_dtypes=True)], [], ["icol2"], 0.6)
-    add("g", [lambda: g.iota(T.gcol2[:], [[1, 16], [0, 16]], 0, 0, allow_small_or_imprecise_dtypes=True)], [], ["gcol2"], 0.6)
+    iota("ic", [[0, 8], [1, 16]], 0)
+    iota("gcl", [[1, 8], [0, 16]], 0)
+    iota("ev", [[16, 8], [-2, 8]], 14)
+    iota("cy", [[0, 8], [1, 24]], 128)
+    iota("cm", [[0, 8], [-3, 8], [-1, 2]], 23)
+    iota("fw", [[2, 64]], 0)
+    iota("pd", [[1, 8], [1, 16]], 1)
     for u in (0, 1):
-        cp(B("La", u), ("ri", T.ri[:, 128 * u:128 * u + 128]))
-        ts(B("crow", u), ("ri", T.ri[:, 128 * u:128 * u + 128]), -OFF, OP.add)
-    ts(("pi2a", T.pint[:, 1:2]), ("pint", T.pint[:, 0:1]), 15, OP.bitwise_and)
-    ts(("pi2b", T.pint[:, 2:3]), ("pint", T.pint[:, 0:1]), 4, OP.arith_shift_right)
-    cp(("pmod", T.pf[:, 0:1]), ("pi2a", T.pint[:, 1:2]))
-    cp(("pdiv", T.pf[:, 1:2]), ("pi2b", T.pint[:, 2:3]))
-    pmod, pdiv = T.pf[:, 0:1], T.pf[:, 1:2]
-    ic, gc_ = ("icol2", T.icol2[:, 0:128]), ("gcol2", T.gcol2[:, 0:128])
-    heads = ("blk", T.blk[:, 0:128:16])
-    ts(B("mask"), ic, pmod, OP.is_equal, extra=["pmod"])
-    ts(B("blk"), gc_, pdiv, OP.is_equal, extra=["pdiv"])
-    tt(B("i2"), B("mask"), B("blk"), OP.mult)
-    ts(B("ni"), B("i2"), -1.0, OP.mult)
-    ts(B("c8"), ic, 0.0, OP.mult, NO, OP.add)
-    ts(B("kc"), ic, 0.0, OP.mult, -64.0 / OFF, OP.add)
-    cp(("gs0", T.gs[:, 0, :]), heads)
-    ts(("gs1", T.gs[:, 1, :]), heads, 2.0, OP.mult)
-    ts(("gs2", T.gs[:, 2, :]), heads, -1.0, OP.mult)
-    cp(B("gs16"), heads)
-    ts(B("m2"), B("icol2"), 0.0, OP.is_gt)
-    ts(B("mq"), ic, 0.0, OP.is_gt, 0.25, OP.mult)
-    cp(B("mx"), ("m2", T.m2[:, 0:128]))
-    fill("mx", T.mx[:, 15:128:16], 0.0)
-    cp(B("cl"), ("gcol2", T.gcol2[:, 0:256:16]))
-    cp(B("bo"), B("blk"))
-    ts(B("tri"), ic, pmod, OP.is_gt, extra=["pmod"])
-    tt(B("tri"), B("tri"), B("blk"), OP.mult)
-    ts(B("pos"), B("icol2"), pmod, OP.is_ge, OFF, OP.mult, extra=["pmod"])
-    ts(B("dumt"), ("gcol2", T.gcol2[:, 0:256:16]), 16.0, OP.mult, pmod, OP.add, extra=["pmod"])
-    ts(B("dumt"), B("dumt"), OFF, OP.add)
-    cp(("iw0", T.iw[:, 0, :]), B("i2"))
-    for d in range(1, 16):
-        act(("iw%d" % d, T.iw[:, d, :]), ("iw0", T.iw[:, 0, :]), ID, 0.0, float(4 ** d))
-    act(("iw16", T.iw[:, 16, :]), ("iw0", T.iw[:, 0, :]), ID, 0.0, -BIG)
-    for u in (0, 1):
-        P = T["Pd%d" % u]
-        fill("Pd%d:D1" % u, P[:, 0:128], 0.0)
-        fill("Pd%d:D2" % u, P[:, 128:256], 10000.0)
-        ts(B("q6", u), ic, 0.0, OP.mult, NO, OP.add)
-    fill("Pw:0", T.Pw[:, 0:8, :], 0.0)
-    fill("Pw:1", T.Pw[:, 8:16, :], 0.0)
-    fill("cw", T.cw[:, 2048:CW], 0.0)
-    for k in range(2):
-        cp(("cw", T.cw[:, 1024 * k:1024 * k + 1024]), ("ci", T.ci[:, 1024 * k:1024 * k + 1024]))
-    for u in (0, 1):
-        Pt = T["Pt%d" % u]
-        mm([(Pt[:, 0:128], T["crowh%d" % u][:], T.i2[:], True, True)], ["crowh%d" % u, "i2"], ["Pt%d:A" % u])
-        cp(("r0c%d" % u, T.r0c[:, u, :]), ("Pt%d:A" % u, Pt[:, 0:128]))
+        cp(("la%d" % u, T.la[:, u, :]), ("ri", T.ri[:, 128 * u:128 * u + 128]))
 
-    def gather(u, st, t):
-        L, G = T["L%sh%d" % (st, u)], T["G%sh%d" % (st, u)]
-        kl, win = "L%sh%d" % (st, u), T.xw[:, 0:4096]
+    def col(j):
+        return T.pf[:, j:j + 1]
+
+    def C(j):
+        return ("pf%d" % j, col(j))
+    ts(("pi1", T.pint[:, 1:2]), ("pint", T.pint[:, 0:1]), 15, OP.bitwise_and)
+    ts(("pi2", T.pint[:, 2:3]), ("pint", T.pint[:, 0:1]), 4, OP.arith_shift_right)
+    cp(C(0), ("pi1", T.pint[:, 1:2]))
+    cp(C(1), ("pi2", T.pint[:, 2:3]))
+    cp(C(2), ("pint", T.pint[:, 0:1]))
+    ic, gcl = B("ic"), B("gcl")
+    ts(B("mask"), ic, col(0), OP.is_equal, extra=["pf0"])
+    ts(B("blk"), gcl, col(1), OP.is_equal, extra=["pf1"])
+    tt(B("i4"), B("mask"), B("blk"), OP.mult)
+    for nm, w in (("i2", 1.0), ("ib", 1.0), ("ni", -1.0), ("nib", -1.0), ("pk", 1024.0), ("nk", -1024.0), ("ib4", 4096.0)):
+        if SCRATCH[nm][2] == "bfloat16":
+            act(B(nm), B("i4"), ID, 0.0, w)
+        else:
+            ts(B(nm), B("i4"), w, OP.mult)
+    cp(B("hd"), ("blk", T.blk[:, 0:128:16]))
+    for j in range(4):
+        act(("gs4%d" % j, T.gs4[:, :, j]), B("hd"), ID)
+    gs4 = ["gs4%d" % j for j in range(4)]
+    act(B("gm"), B("hd"), ID, 0.0, -2.0)
+    fill("ca", T.ca[:], 0.0)
+    fill("ca", T.ca[:, :, 1:24:3], -1024.0)
+    fill("ca", T.ca[:, :, 0], 1024.0)
+    act(B("cy"), B("cy"), ID, 0.0, 8192.0)
+    ts(("sely0", T.sely[:, 0:192:3]), B("ev"), 1.0, OP.add, col(2), OP.is_equal, extra=["pf2"])
+    ts(("sely1", T.sely[:, 1:192:3]), B("ev"), col(2), OP.is_equal, extra=["pf2"])
+    ts(("sely2", T.sely[:, 2:192:3]), B("ev"), col(2), OP.is_equal, extra=["pf2"])
+    for u in (0, 1):
+        ts(B("Ta", u), ("cy", T.cy[:, 0:144]), 0.0, OP.mult, c=0.5)
+        fill("Wch%d" % u, T["Wch%d" % u][:], 1.0)
+    ts(C(3), C(0), 15.0, OP.is_equal)
+    ts(B("c15"), ("cy", T.cy[:, 0:144]), 0.0, OP.mult, c=0.5)
+    ts(("c15", T.c15[:, 0:128]), B("i4"), col(3), OP.mult, extra=["pf3"])
+    ts(C(4), C(2), 8.0, OP.is_equal, -8192.0, OP.mult)
+    ts(C(5), C(2), 9.0, OP.is_equal, -TOP, OP.mult)
+    fill("cm", T.cm[:, 15:128:16], 24.0)
+    ts(B("t0"), B("cm"), 0.5, OP.add, col(4), OP.mult, extra=["pf4"])
+    ts(B("t1"), gcl, col(2), OP.is_equal, col(5), OP.add, extra=["pf2", "pf5"])
+    tt(B("g10"), B("t0"), B("t1"), OP.add)
+    ts(B("gw"), gcl, col(2), OP.is_equal, -4096.0, OP.mult, extra=["pf2"])
+    ts(C(6), C(2), 8.0, OP.is_lt, 64.0, OP.mult)
+    act(B("kc"), B("ic"), ID, col(6), 0.0, extra=["pf6"])
+    cur[0] = CFG["bc"]
+    ts(C(7), C(0), 16.0, OP.add)
+    ts(B("t0"), B("pd"), col(0), OP.is_equal, extra=["pf0"])
+    ts(B("t1"), B("pd"), col(7), OP.is_equal, extra=["pf7"])
+    tt(B("t0"), B("t0"), B("t1"), OP.add)
+    tt(B("bm"), B("mask"), B("t0"), OP.subtract)
+    for k in range(8):
+        ts(("pair%d" % k, T.pair[:, k, :]), B("bm"), T.hd[:, k:k + 1], OP.mult, c=0.5, extra=["hd"])
+    ts(C(8), C(0), col(1), OP.add, 1.0, OP.add, extra=["pf1"])
+    ts(C(9), C(8), 16.0, OP.is_ge, -16.0, OP.mult)
+    tt(C(8), C(8), C(9), OP.add)
+    tt(C(9), C(8), C(0), OP.min)
+    tt(C(10), C(8), C(0), OP.max)
+    r16 = ("ic", T.ic[:, 0:16])
+
+    def W(j):
+        return ("w16%d" % j, T.w16[:, j, :])
+    fill("w160", T.w16[:, 0, :], 2.0 ** -10)
+    fill("w161", T.w16[:, 1, :], 0.0)
+    fill("w161", T.w16[:, 1, 0:1], 2.0 ** 75)
+    scan(W(2), W(0), W(1), OP.mult, OP.add)
+    ts(W(3), r16, col(9), OP.is_equal, extra=["pf9"])
+    tt(W(3), W(3), W(2), OP.mult)
+    ts(W(1), W(0), 0.0, OP.mult, 1.0, OP.add)
+    scan(W(2), W(1), W(3), OP.mult, OP.max)
+    ts(W(4), r16, col(9), OP.is_gt, 33.0, OP.mult, extra=["pf9"])
+    ts(W(5), r16, col(10), OP.is_le, extra=["pf10"])
+    tt(W(4), W(4), W(5), OP.mult)
+    ts(B("wt"), W(4), -1.0, OP.add, T.w16[:, 2, 15:16], OP.mult, extra=["w162"])
+    ts(B("c8"), ic, 0.0, OP.mult, NO, OP.add)
+    fill("cb1", T.cb1[:], 0.0)
+    fill("cb1", T.cb1[:, :, 0:16:15], -1000.0)
+    fill("cb2", T.cb2[:], 0.0)
+    fill("cb2", T.cb2[:, :, 0], 1000.0)
+    fill("c2k", T.c2k[:], OFF)
+    fill("mp", T.mp[:], -1.0e9)
+    fill("mp", T.mp[:, 0:128:16], OFF)
+    fill("mp", T.mp[:, 15:128:16], OFF)
+    ts(("t2", T.t2[:, 0:64]), B("fw"), col(2), OP.is_equal, extra=["pf2"])
+    ts(("t2", T.t2[:, 64:128]), B("fw"), 1.0, OP.add, col(2), OP.is_equal, extra=["pf2"])
+    tt(B("dm"), ("t2", T.t2[:, 0:64]), ("t2", T.t2[:, 64:128]), OP.subtract)
+    for u in (0, 1):
+        fill("dlh%d" % u, T["dlh%d" % u][:], 0.0)
+    ts(B("t0"), B("i4"), 2.0, OP.mult)
+    tt(B("am"), B("t0"), B("blk"), OP.subtract)
+    ts(("lo", T.lohi[:, 0, :]), ("mask", T.mask[:, 0:16]), -1.0, OP.mult)
+    ts(("hi_", T.lohi[:, 1, :]), ("mask", T.mask[:, 0:16]), -1.0, OP.mult, 1.0, OP.add)
+    for i in range(16):
+        ts(("wm%d" % i, T.wm[:, i, :]), B("am"), T.lohi[:, 0, i:i + 1], OP.max, T.lohi[:, 1, i:i + 1], OP.min, c=0.5, extra=["lo", "hi_"])
+    ts(B("t1"), ic, col(0), OP.is_gt, 16384.0, OP.mult, extra=["pf0"])
+    ts(B("t2"), ic, col(0), OP.not_equal, 4096.0, OP.mult, extra=["pf0"])
+    tt(B("posw"), B("t1"), B("t2"), OP.add)
+    ts(C(11), C(0), OFF, OP.add)
+    fill("cw", T.cw[:, 2048:CW], 0.0)
+    fill("cf_", T.cf[:, 2048:CW], 0.0)
+    for k in range(4):
+        ts(("cw%d" % k, T.cw[:, 512 * k:512 * k + 512]), ("ci", T.ci[:, 512 * k:512 * k + 512]), -OFF, OP.add)
+    cws = ["cw%d" % k for k in range(4)]
+    cur[0] = 0.0
+
+    def gather(u, st, t, lst):
+        G, M, N = (T["%s%sh%d" % (n, st, u)] for n in "GMN")
+        win, slot = T.xw[:, 0:4096], 2 * t + u
         nch, ndve = CFG["ch_" + st], CFG["gv_" + st]
         if t == 0 and st == "a":
             ndve = CFG["gv0"][u]
-        for ch in range(nch):
-            a, b = 128 // nch * ch, 128 // nch * (ch + 1)
-            key = "G%sh%d.%d" % (st, u, ch)
-            parts = []
-            if ch == nch - 1 and ndve:
-                parts = [("v", b - ndve, b)]
-                b -= ndve
-            if b > a:
-                parts.append(("s", a, b))
-            for q, a, b in parts:
-                o, i = G[:, 16 * a:16 * b], win.indirect(L[:, a:b])
-                if q == "s":
-                    act((key + q, o), ("xw", i), ID, 16.0, c=CFG["gam"], extra=["xw_", kl])
-                else:
-                    ts((key + q, o), ("xw", i), 16.0, OP.add, c=CFG["gam"], extra=["xw_", kl])
-
-    def dist(u, st, step):
-        G = T["G%sh%d" % (st, u)]
-        dn = "d2" if step == 2 else "d" + st
-        absact = CFG["abs_2" if step == 2 else "abs_" + st]
-        d = T["%sh%d" % (dn, u)]
-        y = d if absact else T["%sh%d" % ("y2" if step == 2 else "y" + st, u)]
-        nch = CFG["ch_" + st]
-        w = 2048 // nch
-        n = w // step
-        for ch in range(nch):
-            a, b = w * ch, w * ch + w
-            key = "G%sh%d.%d" % (st, u, ch)
-            kd, ky = "%sh%d.%d" % (dn, u, ch), "%sh%d.%d%s" % (dn, u, ch, "" if absact else "y")
-            o = d[:, n * ch:n * ch + n - 1]
-            add("v", [lambda o=o, a=a, b=b: g.vector.tensor_tensor_scan(out=o, data0=G[:, a:b - step:step], data1=G[:, a + step:b:step], initial=0.0, op0=OP.max, op1=OP.subtract)],
-                [key + "s", key + "v"], [kd], dur(n, 0.5))
-            yo = y[:, n * ch:n * ch + n - 1]
-            if absact:
-                act((ky, yo), (kd, o), ABS)
+        if t == ROUNDS - 1 and st == "b":
+            ndve = CFG["gv4"]
+        w = (128 - ndve) // nch
+        parts = [("s", w * ch, w * ch + w if ch < nch - 1 else 128 - ndve) for ch in range(nch)] + ([("v", 128 - ndve, 128)] if ndve else [])
+        kg, km, kn = [], [], []
+        for n, (q, a, b) in enumerate(parts):
+            key = "G%sh%d.%d" % (st, u, n)
+            kg.append(key)
+            o, i = G[:, 16 * a:16 * b], win.indirect(T[lst][:, slot, a:b])
+            more = ["xw_", "%s%d" % (lst, slot), "done%s%d.%d" % (st, u, t - 1)]
+            if q == "s":
+                act((key, o), ("xw", i), ID, c=CFG["gam"], extra=more)
             else:
-                ts((ky, yo), (kd, o), 0.0, OP.max, c=0.5)
+                cp((key, o), ("xw", i), c=CFG["gam"], extra=more)
+        for step, D, ks in ((2, N, kn), (1, M, km)):
+            if step == 2 and t == 0 and st == "a":
+                continue
+            for n, (q, a, b) in enumerate(parts):
+                key = "%d%sh%d.%d" % (step, st, u, n)
+                ks.append(key)
+                a, b = 16 * a, 16 * b
+                scan((key, D[:, a // step:b // step - 1]), (kg[n], G[:, a:b - step:step]), (kg[n], G[:, a + step:b:step]), OP.max, OP.min, 0.5)
+        return kg, km, kn
 
-    def sums(u, st, step):
-        dn = "d2" if step == 2 else "d" + st
-        absact = CFG["abs_2" if step == 2 else "abs_" + st]
-        d = T["%sh%d" % (dn, u)]
-        P = T["Pd%d" % u]
-        items, wr = [], ["Pd%d:%s" % (u, "D1" if step == 1 else "D2")]
-        per = 16 // step
-        for p in range(7 if step == 2 else 15 if st == "a" else 14):
-            if step == 2:
-                o = P[:, 129 + 2 * p:256:16]
-            elif p < 14:
-                o = P[:, p + 1:128:16]
+    def first_fail(t, u):
+        k = 2 * t + u
+        PA, PM, G, M, N = T["PA%d" % u], T["PM%d" % u], T["Gah%d" % u], T["Mah%d" % u], T["Nah%d" % u]
+        kd, ra = "PA%d:D" % u, B("RA", u)
+        ts(ra, ("la%d" % k, T.la[:, k, :]), -OFF, OP.add, c=0.5)
+        ky, Y = "PM%d:Y" % u, PM[:, 0:192]
+        mm([(Y, T.ib[:], T.cy[:]), (Y, ra[1], T.sely[:])], ["ib", "cy", ra[0], "sely0", "sely1", "sely2"], [ky])
+        kg, km, kn = gather(u, "a", t, "la")
+        items = [(PA[:, :, 0:24], T.ib[:], T.ca[:])]
+        for p in range(16):
+            z = 3 * (7 - p // 2)
+            if p % 2:
+                items.append((PA[:, :, z:z + 3:2], G[:, p:2048:16], T.gs4[:, :, 0:2]))
             else:
-                o = P[:, 128:256:16]
-                wr.append("Pd%d:D2" % u)
-            if absact:
-                items.append((o, d[:, p:128 * per:per], T.gs[:, 0, :], True, True))
-            else:
-                y = T["%sh%d" % ("y2" if step == 2 else "y" + st, u)]
-                items.append((o, y[:, p:128 * per:per], T.gs[:, 1, :], True, False))
-                items.append((o, d[:, p:128 * per:per], T.gs[:, 2, :], False, True))
-        chs = range(CFG["ch_" + st])
-        rd = ["gs0", "gs1", "gs2"] + ["%sh%d.%d" % (dn, u, ch) for ch in chs] + ([] if absact else ["%sh%d.%dy" % (dn, u, ch) for ch in chs])
-        mm(items, rd, wr)
+                n = 4 if p else 2
+                items.append((PA[:, :, z + 1:z + 1 + n], G[:, p:2048:16], T.gs4[:, :, 0:n]))
+        mm(items, ["ib", "ca"] + gs4 + kg, [kd], sp=False)
+        if t:
+            mm([(PA[:, :, 3 * (7 - i) + 1], N[:, i:1024:8], T.gm[:]) for i in range(7)], kn + ["gm"], [kd], st=False, sp=False)
+        mm([(PA[:, :, 3 * (7 - p // 2) + (0 if p % 2 else 2)], M[:, p:2048:16], T.gm[:]) for p in range(15)], km + ["gm"], [kd], st=False, sp=t == 0)
+        if t:
+            nl = T.nl[:, k - 2, :, :]
+            mm([(PA[:, :, 0:24:3], T.nk[:], nl), (PA[:, :, 1:24:3], T.pk[:], nl), (PA[:, :, 2:24:3], T.nk[:], nl)], ["nl%d" % (k - 2), "pk", "nk"], [kd], st=False)
+        s = float(2 ** 22)
+        if CFG["e_dp"] == "s":
+            act(B("Dp", u), (kd, PA[:, :, 0:24]), ID, -TH * s, s)
+        else:
+            ts(B("Dp", u), (kd, PA[:, :, 0:24]), -TH, OP.add, s, OP.mult)
+        lastw["donea%d.%d" % (u, t)] = scan(B("W", u), B("Dp", u), (ky, Y), OP.max, OP.min)
 
-    def hold(u, reg, out, q, rk, r):
-        P = T["Pd%d" % u]
-        z = {"C": 256, "RB": 384}[reg]
-        kp = "Pd%d:%s" % (u, reg)
-        o = P[:, z:z + 128]
-        mm([(o, T.i2[:], r, True, False), (o, T.i2[:], T.c8[:], False, False), (o, T.ni[:], q[1], False, True)], [rk, q[0], "i2", "c8", "ni"], [kp])
-        scan(out, q, (kp, o), OP.add, OP.max)
-        return kp, o
+    def moved(u, near, ra, out, kout, last):
+        PM = T["PM%d" % u]
+        kf, F = "PM%d:F" % u, PM[:, 192:256]
+        mm([(F, ra[1], T.dm[:])], [ra[0], "dm"], [kf])
+        tt(("dlh%d" % u, T["dlh%d" % u][:, 1:128:2]), (kf, F), near, OP.mult)
+        mm([(out, T["dlh%d" % u][:], T.i4[:])], ["dlh%d" % u, "i4"], [kout], sp=False, c=4)
+        mm([(out, T.i2[:], ra[1])], ["i2", ra[0]], [kout], st=False, sp=last)
 
     def stage_a(t, u):
-        Pn, Pd, Pt = T["Pn%d" % u], T["Pd%d" % u], T["Pt%d" % u]
-        kn, kt, kX = "Pn%d:R" % u, "Pt%d:A" % u, "Xh%d" % u
-        if t == 0:
-            slot, r = "r0c%d" % u, T.r0c[:, u, :]
+        k = 2 * t + u
+        PA, PB, PM = T["PA%d" % u], T["PB%d" % u], T["PM%d" % u]
+        Wd, Wc, Ta, WT = T["Wh%d" % u], T["Wch%d" % u], T["Tah%d" % u], T["WTh%d" % u]
+        end = ("Wh%d" % u, Wd[:, 23:192:24])
+        wc = ("Wch%d" % u, Wc[:, 0:8])
+        cp(wc, end)
+        tt(("Tah%d" % u, Ta[:, 15:128:16]), end, wc, OP.subtract)
+        kl, L = "PB%d:L" % u, PB[:, :, 24]
+        mm([(L, Ta[:, 15 - i:143 - i], T.i2[:, i:128:16]) for i in range(16)], ["Tah%d" % u, "i2"], [kl])
+        d = t % n_ranks
+        c0, c1 = 8 * u, 8 * u + 8
+        hs = ("hs%d" % u, T.hs[:, c0:c1])
+        tt(hs, (kl, L), ("qb%d" % d, T.qb[:, d, c0:c1]), OP.mult)
+        kt, TT_ = "PB%d:T" % u, PB[0:10, :, 48:64]
+        mm([(TT_, Wc[:, 0:10], T.ib[:])], [wc[0], "ib"], [kt])
+        wt = ("WTh%d" % u, WT[0:10, :])
+        if CFG["e_wt"] == "s":
+            act(wt, (kt, TT_), ID)
         else:
-            slot, r = "rl%d" % (2 * (t - 1) + u), T.rl[:, 2 * (t - 1) + u, :]
-            mm([(Pt[:, 0:128], r, T.i2[:], True, True)], [slot, "i2"], [kt])
-            ts(B("La", u), (kt, Pt[:, 0:128]), OFF, OP.add)
-        gather(u, "a", t)
-        dist(u, "a", 1)
-        sums(u, "a", 1)
-        X = T["Xh%d" % u]
-        scan(B("X", u), B("mx"), ("Pd%d:D1" % u, Pd[:, 0:128]), OP.mult, OP.max)
-        ts(B("q1", u), B("X", u), TH, OP.is_le, NO, OP.mult, c=0.5)
-        kp, rb = hold(u, "RB", B("HK", u), B("q1", u), slot, r)
-        sm, si = T["rkh%d" % u], T["sih%d" % u]
-        ks, kr = "sih%d." % u, "rkh%d." % u
-        HK = T["HKh%d" % u]
-        ts((ks + "q", si[:, 0, :]), (kp, Pd[:, 399:512:16]), OFF + 64.0, OP.add)
-        ts((ks + "m", si[:, 1, :]), (ks + "q", si[:, 0, :]), 63, OP.bitwise_and)
-        if t > 0:
-            ts((kr + "b", sm[:, 2, :]), (ks + "m", si[:, 1, :]), 2048.0, OP.mult, T.kk[:, t - 1:t], OP.add, extra=["kk%d" % (t - 1)])
+            cp(wt, (kt, TT_))
+        act(("ft%d" % u, T.ft[0:10, 128 * u:128 * u + 128]), (kt, TT_), SIGN, -TOP, acc=("acc%d.%d" % (t % 2, u), T.acc[0:10, 2 * (t % 2) + u:2 * (t % 2) + u + 1]))
+        k1, P1 = "PB%d:U" % u, PB[:, :, 32:48]
+        mm([(P1, T.g10[0:10, :], wt[1])], ["g10", wt[0]], [k1])
+        if CFG["e_dn"] == "s":
+            act(B("Dn", u), (k1, P1), RELU, 0.0, -1.0)
         else:
-            ts((kr + "b", sm[:, 2, :]), (ks + "m", si[:, 1, :]), 2048.0, OP.mult)
-        tt((kr + "p", sm[:, 0, :]), ("HKh%d" % u, HK[:, 14:128:16]), (ks + "q", si[:, 0, :]), OP.mult)
-        tt((ks + "s", si[:, 2, :]), (kr + "p", sm[:, 0, :]), (kr + "b", sm[:, 2, :]), OP.add)
-        ts((ks + "h", si[:, 3, :]), (ks + "s", si[:, 2, :]), 6, OP.arith_shift_right, 2047, OP.bitwise_and)
-        act(B("RB", u), (kp, rb), ID)
-        tt((kr + "xf", sm[:, 3, :]), (kX, X[:, 14:128:16]), ("Pd%d:D2" % u, Pd[:, 128:256:16]), OP.max)
-        nf = ("nf%d.%d" % (t % 2, u), T.nf[:, t % 2, 8 * u:8 * u + 8])
-        ts(nf, (kr + "xf", sm[:, 3, :]), TH, OP.is_le, OFF, OP.mult)
-        tt(B("hm", u), (ks + "h", si[:, 3, :]), nf, OP.max)
-        Xm = T.Xm[:, 128 * u:128 * u + 128]
-        add("v", [lambda: g.vector.tensor_tensor(out=Xm, in0=T["hmh%d" % u][:, 0:8].indirect(T.cl[:, 0:8]), in1=T.mask[:], op=OP.mult)],
-            ["hmh%d" % u, "cl", "mask"], ["Xm%d" % u], dur(128, CFG["gam"]))
-        mm([(Pt[:, 0:8], Xm, T.gs16[:], True, True)], ["Xm%d" % u, "gs16"], [kt])
-        ow = ("ow%d" % u, T.ow[:, 8 * u:8 * u + 8])
-        cp(ow, (kt, Pt[:, 0:8]))
-        ts(B("crow", u), ("cw", T.cw[:, 0:CW].indirect(ow[1])), -OFF, OP.add, c=CFG["gam"], extra=[ow[0]])
-        kc, C = "Pd%d:C" % u, Pd[:, 256:384]
-        mm([(C, T["crowh%d" % u][:], T.i2[:], True, False), (C, T.i2[:], T["q1h%d" % u][:], False, True)], ["crowh%d" % u, "q1h%d" % u, "i2"], [kc])
-        tt(B("R1", u), B("RB", u), (kc, C), OP.max)
+            ts(B("Dn", u), (k1, P1), -1.0, OP.mult, 0.0, OP.max)
+        kk, K = "PA%d:D" % u, PA[:, :, 32:48]
+        if t:
+            moved(u, ("nl%d" % (k - 2), T.nl[:, k - 2, :, 7::-1]), B("RA", u), K, kk, False)
+        else:
+            mm([(K, T.i2[:], T["RAh%d" % u][:])], ["i2", "RAh%d" % u], [kk], sp=False)
+        mm([(K, T.g10[0:10, :], wt[1]), (K, T.ib[:], T["Dnh%d" % u][:])], ["g10", wt[0], "ib", "Dnh%d" % u], [kk], st=False)
+        h0, h1 = ("hi0%d" % u, T.hi[:, 0, c0:c1]), ("hi1%d" % u, T.hi[:, 1, c0:c1])
+        tt(h0, hs, ("bk", T.bk[:, c0:c1]) if t else ("qb0", T.qb[:, 0, 16 + c0:16 + c1]), OP.add)
+        ts(h1, h0, 6, OP.arith_shift_right, 2047, OP.bitwise_and)
+        ow = ("ow%d" % u, T.ow[:, c0:c1])
+        cp(ow, h1)
+        if t:
+            tt(B("Z", u), ("cw", T.cw[:, 0:CW].indirect(ow[1])), B("Dn", u), OP.add, c=CFG["gam"], extra=[ow[0]])
+        else:
+            ts(B("Y", u), ("ci", T.ci[:, 0:2048].indirect(ow[1])), -OFF, OP.add, c=CFG["gam"], extra=[ow[0]])
+            tt(B("Z", u), B("Y", u), B("Dn", u), OP.add)
+        tt(B("R1", u), B("Z", u), (kk, K), OP.min)
         R1, E = T["R1h%d" % u], T["Eh%d" % u]
-        mm([(Pn[:, 0:8, 0:16], T.i2[:], R1[:], True, True), (Pn[:, 0:8, 16:24], T.i2[:], R1[:, :, 0:8], True, True)], ["R1h%d" % u, "i2"], [kn])
-        kw, W = "Pw:%d" % u, T.Pw[:, 8 * u:8 * u + 8, :]
-        for d in range(1, 9):
-            n = 16 if d < 8 else 8
-            ke, e = "Eh%d.%d" % (u, d), 16 - d
-            tt((ke, E[:, d - 1, :, 0:n]), ("R1h%d" % u, R1[:, :, 0:n]), (kn, Pn[:, 0:8, d:d + n]), OP.is_equal)
-            its = [(T.Pw[:, 8 * u:8 * u + 8, 1:e + 1], T.iw[:, d, :], E[:, d - 1, :, 0:e], d == 1, d == 8)]
-            if d < 8:
-                its.append((T.Pw[:, 8 * u:8 * u + 8, 1:d + 1], T.iw[:, e, :], E[:, d - 1, :, e:16], False, False))
-            mm(its, [ke, "iw%d" % d, "iw%d" % e], [kw])
-        cp(B("W2", u), (kw, W))
-        scan(B("F", u), ("m2", T.m2[:, 0:128]), B("W2", u), OP.mult, OP.max, 0.5)
-        mm([(C, T.iw[:, 0, :], T["W2h%d" % u][:], True, False), (Pd[:, 257:384], T.iw[:, 16, :], T["Fh%d" % u][:, 0:127], False, True)],
-           ["W2h%d" % u, "Fh%d" % u, "iw0", "iw16"], [kc])
-        scan(B("V", u), B("mq"), (kc, C), OP.mult, OP.max)
-        ts(B("q2", u), B("V", u), 4.0, OP.is_lt, NO, OP.mult, c=0.5)
-        hold(u, "RB", B("RP", u), B("q2", u), "R1h%d" % u, R1[:])
-        mm([(Pt[:, 0:128], T["RPh%d" % u][:], T.i2[:], True, True)], ["RPh%d" % u, "i2"], [kt])
-        ts(B("Lb", u), (kt, Pt[:, 0:128]), OFF, OP.add)
+        ks, Sc = "PB%d:U" % u, PB[:, :, 32:48]
+        for b in (0, 1):
+            P, kp = T["PE%d" % b], "PE%d:E" % b
+            for j in range(4):
+                mm([(P[:, 128 * j:128 * j + 128], T.pair[:, 4 * b + j, :], R1[:])], ["R1h%d" % u, "pair%d" % (4 * b + j)], [kp])
+            ts(("Eh%d.%d" % (u, b), E[:, 512 * b:512 * b + 512]), (kp, P[:, 0:512]), 0.0, OP.is_equal)
+        for j in range(8):
+            mm([(PB[:, j, 32:48], E[:, 128 * j:128 * j + 128], T.wt[:])], ["Eh%d.%d" % (u, j // 4), "wt"], [ks])
+        ts(B("q2", u), (ks, Sc), 0.0, OP.is_le, NO, OP.mult)
+        kh, H = "PM%d:H" % u, PM[:, 384:512]
+        mm([(H, R1[:], T.i2[:]), (H, T.i2[:], T.c8[:]), (H, T.ni[:], T["q2h%d" % u][:])], ["R1h%d" % u, "i2", "c8", "ni", "q2h%d" % u], [kh])
+        scan(B("RP", u), B("q2", u), (kh, H), OP.add, OP.max)
+        ka, A = "PM%d:A" % u, PM[:, 256:384]
+        mm([(A, T["RPh%d" % u][:], T.i2[:])], ["RPh%d" % u, "i2"], [ka])
+        lb = ("lb%d" % k, T.lb[:, k, :])
+        ts(lb, (ka, A), OFF, OP.add)
+        if t < ROUNDS - 1:
+            send(lb, ("la%d" % (k + 2), T.la[:, k + 2, :]), "arl%d" % k)
 
     def stage_b(t, u):
-        Pd, Pt = T["Pd%d" % u], T["Pt%d" % u]
-        kt = "Pt%d:A" % u
-        RP = T["RPh%d" % u][:]
-        gather(u, "b", t)
-        dist(u, "b", 2)
-        dist(u, "b", 1)
-        sums(u, "b", 2)
-        ts(("q6h%d" % u, T["q6h%d" % u][:, 1:128:2]), ("Pd%d:D2" % u, Pd[:, 129:256:2]), TH, OP.is_gt, NO, OP.mult)
         k = 2 * t + u
-        slot, rn = "rn%d" % k, T.rn[:, k, :]
-        hold(u, "RB", (slot, rn), B("q6", u), "RPh%d" % u, RP)
+        PA, PB, PM, G, M, N = T["PA%d" % u], T["PB%d" % u], T["PM%d" % u], T["Gbh%d" % u], T["Mbh%d" % u], T["Nbh%d" % u]
+        kg, km, kn = gather(u, "b", t, "lb")
+        k2, k1 = "PB%d:D2" % u, "PB%d:D1" % u
+        items = [(PB[:, :, 16:24], T.ib[:], T.cb2[:])]
+        for i in range(8):
+            a, b = max(7 - i, 1), min(9 - i, 8)
+            items.append((PB[:, :, 16 + a:16 + b], G[:, 2 * i:2048:16], T.gs4[:, :, 0:b - a]))
+        mm(items, ["ib", "cb2"] + gs4 + kg, [k2], sp=False)
+        mm([(PB[:, :, 23 - i], N[:, i:1024:8], T.gm[:]) for i in range(7)], kn + ["gm"], [k2], st=False)
+        ns = ("ns%d" % k, T.ns[:, k, :, :])
+        ts(ns, (k2, PB[:, :, 16:24]), TH, OP.is_lt)
         if t < ROUNDS - 1:
-            rid, pid, _s = topo.addr(nxt)
-            m = 0
-            for e in topo.engines(core, nxt)[:NENG]:
-                m |= 1 << e
-            sd = add("g", [lambda: g.remote_dma(out_ap=T.rl[:, k, :], in_ap=rn, remote_sem=T.sem["arr%d" % k], local_sem=T.sem.sent, pid=pid, routing_id=rid, dma_engine_mask=m)],
-                     [slot], [], 0.3, "none", 0, 1.7)
-            add(None, [], [], ["rl%d" % k], 0.0, "arr%d" % k, NENG, 0.0, deps=[sd])
-        sums(u, "b", 1)
-        scan(B("X4", u), B("mx"), ("Pd%d:D1" % u, Pd[:, 0:128]), OP.mult, OP.max)
-        ts(B("q4", u), B("X4", u), TH, OP.is_le, NO, OP.mult, c=0.5)
-        hold(u, "C", B("S", u), B("q4", u), "RPh%d" % u, RP)
-        mm([(Pt[:, 0:128], T["Sh%d" % u][:], T.i2[:], True, True)], ["Sh%d" % u, "i2"], [kt])
-        act(B("SA", u), (kt, Pt[:, 0:128]), ID, OFF)
+            send(ns, ("nl%d" % k, T.nl[:, k, :, :]), "arn%d" % k)
+        cur[0] += CFG["bs"]
+        items = [(PB[:, :, 0:16], T.ib[:], T.cb1[:])]
+        for p in range(15):
+            a, b = max(p, 1), min(p + 2, 15)
+            items.append((PB[:, :, a:b], G[:, p:2048:16], T.gs4[:, :, 0:b - a]))
+        mm(items, ["ib", "cb1"] + gs4 + kg, [k1], sp=False)
+        mm([(PB[:, :, p + 1], M[:, p:2048:16], T.gm[:]) for p in range(14)], km + ["gm"], [k1], st=False)
+        act(B("p4", u), (k1, PB[:, :, 0:16]), RELU, -TH * 8192.0, 8192.0)
+        scan(B("X4", u), B("mp"), B("p4", u), OP.max, OP.subtract, 0.5)
+        kh, H = "PM%d:H" % u, PM[:, 384:512]
+        mm([(H, T.i2[:], T["RPh%d" % u][:]), (H, T.ib[:], T.c2k[:]), (H, T.nib[:], T["X4h%d" % u][:])], ["RPh%d" % u, "i2", "ib", "c2k", "nib", "X4h%d" % u], [kh])
+        scan(B("S", u), B("X4", u), (kh, H), OP.max, OP.min)
+        mm([(H, T["Sh%d" % u][:], T.i2[:])], ["Sh%d" % u, "i2"], [kh])
+        act(B("SA", u), (kh, H), ID, OFF if t == ROUNDS - 1 else 0.0)
         if t == ROUNDS - 1:
-            mm([(Pt[:, 128:256], rn, T.i2[:], True, True)], [slot, "i2"], ["Pt%d:Y" % u])
-            act(B("Y", u), ("Pt%d:Y" % u, Pt[:, 128:256]), ID, OFF)
+            cur[0] -= 3.0
+            ra = B("RA", u)
+            ts(ra, ("lb%d" % k, T.lb[:, k, :]), -OFF, OP.add, c=0.5)
+            kk, K = "PA%d:D" % u, PA[:, :, 32:48]
+            moved(u, (ns[0], T.ns[:, k, :, 7::-1]), ra, K, kk, True)
+            act(B("Y", u), (kk, K), ID, OFF)
             add("y", [lambda: g.sync.dma_start(T.yr[:, 128 * u:128 * u + 128], T["Yh%d" % u][:])], ["Yh%d" % u], [], 0.1, "sty%d" % u, 16, 2.0)
 
     def count(t):
-        f = T.nf[:, t % 2, :]
-        mm([(T.Pt1[:, 256:272], T.kc[:], f, True, True)], ["nf%d.0" % (t % 2), "nf%d.1" % (t % 2), "kc"], ["Pt1:K"])
-        add("v", [lambda: g.vector.tensor_reduce(out=T.kk[:, t:t + 1], in_=T.Pt1[:, 256:272], axis=AxisListType.X, op=OP.add)], ["Pt1:K"], ["kk%d" % t], dur(16))
+        P, c = T.PE1[:, 0:1], 2 * (t % 2)
+        mm([(P, T.kc[0:10, :], T.acc[0:10, c + u:c + u + 1]) for u in (0, 1)], ["kc", "acc%d.0" % (t % 2), "acc%d.1" % (t % 2)], ["PE1:E"], c=4)
+        d = (t + 1) % n_ranks
+        ts(B("bk"), ("qb%d" % d, T.qb[:, d, 16:32]), P, OP.add, extra=["PE1:E"])
 
     def winners():
-        q = T.Pq
-        mm([(q[:, 128 * u:128 * u + 128], T.Xm[:, 128 * u:128 * u + 128], T.i2[:], True, True) for u in (0, 1)], ["Xm0", "Xm1", "i2"], ["Pq:L"])
-        cp(B("XmT"), ("Pq:L", q[:, 0:256]))
-        cp(B("hw"), ("ow0", T.ow[:]), extra=["ow1"])
-        act(B("hexp"), ("hw", T.hw[:, 0:16].indirect(T.cl[:, 0:16])), ID, c=CFG["gam"], extra=["cl"])
-        mm([(q[:, 0:256], T.bo[:], T.XmT[:], True, True)], ["XmT", "bo"], ["Pq:L"])
-        mm([(q[:, 256:512], T.tri[:], T.XmT[:], True, False), (q[:, 256:512], T.i2[:], T.pos[:], False, True)], ["XmT", "tri", "i2", "pos"], ["Pq:R"])
-        for k in range(4):
-            w = 256 - 16 * k
-            a = ("Pq:R", q[:, 256:512]) if k == 0 else ("Pq:L", q[:, 0:w])
-            tt(("Ed%d" % k, T.Ed[:, k, 0:w]), ("hexp", T.hexp[:, 16 * k:256]), a, OP.is_equal)
-        mm([(q[:, 16 * k:256], T.iw[:, 6, :], T.Ed[:, k, 0:256 - 16 * k], k == 0, k == 3) for k in range(4)],
-           ["Ed%d" % k for k in range(4)] + ["iw6"], ["Pq:L"])
-        scan(B("Sc"), B("m2"), ("Pq:L", q[:, 0:256]), OP.mult, OP.max)
-        tt(("t1a", T.t1[:, 0, :]), ("Sc", T.Sc[:, 15:256:16]), B("dumt"), OP.min)
-        tt(("t1b", T.t1[:, 1, :]), ("t1a", T.t1[:, 0, :]), B("hw"), OP.max)
-        cp(B("lw"), ("t1b", T.t1[:, 1, :]))
+        P, kp = T.PE0, "PE0:E"
+        cp(B("h16"), ("hi10", T.hi[:, 1, :]), extra=["hi11"])
+        items = [(P[:, 128 * u:128 * u + 128], T.ib[:], T.posw[:]) for u in (0, 1)]
+        mm([(P[:, 0:256], T.gw[0:10, :], T.ft[0:10, :])] + items, ["ib", "posw", "gw", "ft0", "ft1"], [kp], sp=False)
+        mm([(P[:, i:256:16], T.wm[:, i, :], T.h16[:]) for i in range(16)], ["h16"] + ["wm%d" % i for i in range(16)], [kp], st=False)
+        ts(B("ew"), (kp, P[:, 0:256]), 0.0, OP.is_equal)
+        Q = P[:, 256:272]
+        mm([(Q, T.i2[:], T.h16[:])] + [(Q, T.ib4[:], T.ew[:, i:256:16]) for i in range(16)], ["i2", "h16", "ib4", "ew"], [kp])
+        ts(("lw", T.lw[:, 0:32:2]), (kp, Q), col(11), OP.min, extra=["pf11"])
 
-    def scatter(u):
-        for k in (1, 0):
-            o = T.cw[:, 0:CW].indirect(T.lw[:, 8 * u + 4 * k:8 * u + 4 * k + 4])
-            add("v", [lambda o=o, k=k: g.vector.tensor_copy(out=o, in_=T["SAh%d" % u][:, 64 * k:64 * k + 64])], ["SAh%d" % u, "lw"], ["cw"], dur(64, 3.5))
+    def scatter(t, u):
+        win, key = (T.cw, "cw") if t < ROUNDS - 1 else (T.cf, "cf")
+        for c in range(7, -1, -1):
+            j = 2 * (8 * u + c)
+            o = win[:, 0:CW].indirect(T.lw[:, j:j + 1])
+            add("v", [lambda o=o, c=c: g.vector.tensor_copy(out=o, in_=T["SAh%d" % u][:, 16 * c:16 * c + 16])],
+                ["SAh%d" % u, "lw"] + cws + ["cf_", "cf0", "cf1"], [key], 0.05 + 16 * 3.5 * 0.00083 * 1.1)
 
+    order_u = (1, 0)
+    for u in order_u:
+        cur[0] = CFG["b0"] * u
+        first_fail(0, u)
+    cur[0] = 0.0
+    P = T.PE0[:, 0:16]
+    for u in (0, 1):
+        mm([(T.PE0[:, 8 * u:8 * u + 8], T.c15[:, 15 - i:143 - i], T["RAh%d" % u][:, i:128:16]) for i in range(16)], ["c15", "RAh%d" % u], ["PE0:E"])
+    ts(("qi0", T.qi[:, 0, :]), ("PE0:E", P), OFF + 64.0, OP.add)
+    ts(("qi1", T.qi[:, 1, :]), ("qi0", T.qi[:, 0, :]), 63, OP.bitwise_and)
+    cp(("qb0", T.qb[:, 0, 0:16]), ("qi0", T.qi[:, 0, :]))
+    ts(("qb0", T.qb[:, 0, 16:32]), ("qi1", T.qi[:, 1, :]), 2048.0, OP.mult)
+    for d in range(1, n_ranks):
+        dst = T.cores[(rank + d) % n_ranks]
+        rid, pid, _s = topo.addr(dst)
+        sd = add("g", [lambda d=d, dst=dst, rid=rid, pid=pid: g.remote_dma(out_ap=T.qb[:, d, :], in_ap=T.qb[:, 0, :], remote_sem=T.sem["arq%d" % d], local_sem=T.sem.sent,
+                                                                          pid=pid, routing_id=rid, dma_engine_mask=mask_to(dst))], ["qb0"], [], 0.3, "none", 0, 3.0)
+        add(None, [], [], ["qb%d" % d], 0.0, "arq%d" % d, NENG, 0.0, deps=[sd])
     for t in range(ROUNDS):
-        cur[0] = CFG["b0"]
-        stage_a(t, 0)
-        cur[0] = 0.0
-        stage_a(t, 1)
+        if t == ROUNDS - 1:
+            cur[0] = CFG["bc"]
+            for k in (0, 1):
+                act(("cf%d" % k, T.cf[:, 1024 * k:1024 * k + 1024]), ("cw", T.cw[:, 1024 * k:1024 * k + 1024]), ID, OFF)
+        for u in order_u:
+            cur[0] = CFG["b0"] * u
+            stage_a(t, u)
+        cur[0] = CFG["bs"]
+        winners()
         if t < ROUNDS - 1:
             count(t)
-        winners()
-        cur[0] = CFG["b0"] + CFG["bb"]
-        stage_b(t, 0)
-        cur[0] = CFG["bb"]
-        stage_b(t, 1)
+        for u in order_u:
+            cur[0] = CFG["b0"] * u + CFG["bb"]
+            stage_b(t, u)
         cur[0] = CFG["bs"]
-        scatter(1)
-        scatter(0)
-    add("s", [lambda: g.scalar.dma_start(T.yc[0:64, :], T.cw[0:64, 0:2048])], ["cw"], [], 0.1, "stc0", 16, 5.0)
-    add("y", [lambda: g.sync.dma_start(T.yc[64:128, :], T.cw[64:128, 0:2048])], ["cw"], [], 0.1, "stc1", 16, 5.0)
+        for u in order_u:
+            scatter(t, u)
+        if t < ROUNDS - 1:
+            for u in order_u:
+                cur[0] = CFG["b0"] * u + CFG["ba"]
+                first_fail(t + 1, u)
+    add("s", [lambda: g.scalar.dma_start(T.yc[0:64, :], T.cf[0:64, 0:2048])], ["cf"], [], 0.1, "stc0", 16, 5.0)
+    add("y", [lambda: g.sync.dma_start(T.yc[64:128, :], T.cf[64:128, 0:2048])], ["cf"], [], 0.1, "stc1", 16, 5.0)
 
     n = len(ops)
     users = [[] for _ in range(n)]
     for k, o in enumerate(ops):
         for d in o["need"]:
             users[d].append(k)
-    way = [0.0] * n
-    for k in range(n - 1, -1, -1):
-        o = ops[k]
-        way[k] = o["cost"] + o["lat"] + CFG["wake"] + max([way[j] for j in users[k]] or [0.0])
-    way = [w + o["b"] for w, o in zip(way, ops)]
-    left = [len(o["need"]) for o in ops]
-    at = [0.0] * n
-    free = {q: 0.0 for q in ("v", "s", "t", "g", "y", None)}
-    pool = [k for k in range(n) if left[k] == 0]
-    order = []
-    while pool:
-        best, bs, bst = None, None, 0.0
-        for k in pool:
-            o = ops[k]
-            st = max(free[o["q"]] if o["q"] else 0.0, at[k])
-            key = (st - CFG["ww"] * way[k], -way[k])
-            if bs is None or key < bs:
-                best, bs, bst = k, key, st
-        pool.remove(best)
-        o = ops[best]
-        st = bst
-        if o["q"]:
-            free[o["q"]] = st + o["cost"]
-        done = st + o["cost"] + o["lat"]
-        order.append(best)
-        for j in users[best]:
-            lag = 0.0 if ops[j]["q"] == o["q"] == "t" else CFG["wake"]
-            at[j] = max(at[j], done + lag)
-            left[j] -= 1
-            if left[j] == 0:
-                pool.append(j)
-    CFG["ms"] = max(free.values())
+    wake = CFG["wake"]
+
+    def plan(before, after, urge, fwd):
+        left = [len(b) for b in before]
+        at, begin, more = [0.0] * n, [0.0] * n, [()] * n
+        free = {q: 0.0 for q in ("v", "s", "t", "g", "y", None)}
+        pool = [k for k in range(n) if left[k] == 0]
+        order, opened, banks = [], set(), {}
+        first, last = ("st", "sp") if fwd else ("sp", "st")
+        while pool:
+            cand = []
+            for k in pool:
+                o = ops[k]
+                st = max(free[o["q"]], at[k]) if o["q"] else at[k]
+                if o["bank"]:
+                    if o[first] and o["bank"][0] in opened:
+                        continue
+                    for a in o["bank"]:
+                        for qq, (j, tj) in banks.get(a, {}).items():
+                            if qq != o["q"]:
+                                st = max(st, tj + wake)
+                cand.append((st, k))
+            st0, k0 = min(cand)
+            q0, c0 = ops[k0]["q"], ops[k0]["cost"]
+            best, bst = k0, st0
+            for st, k in sorted(cand, key=lambda e: urge[e[1]]):
+                if ops[k]["q"] == q0 and st <= st0 + CFG["look"] * c0 + 1e-9 + CFG["gain"] * (urge[k0] - urge[k]) * (st < st0 + c0):
+                    best, bst = k, st
+                    break
+            pool.remove(best)
+            o = ops[best]
+            begin[best] = bst
+            if o["q"]:
+                free[o["q"]] = bst + o["cost"]
+            done = bst + o["cost"] + o["lat"]
+            for a in o["bank"]:
+                use = banks.setdefault(a, {})
+                more[best] += tuple(j for qq, (j, tj) in use.items() if qq != o["q"])
+                use[o["q"]] = (best, done)
+                if o[first] and not o[last]:
+                    opened.add(a)
+                if o[last]:
+                    opened.discard(a)
+            order.append(best)
+            for j in after[best]:
+                if ops[j]["q"] == o["q"] == "t":
+                    lag = -o["lat"]
+                else:
+                    lag = wake if fwd else wake - o["lat"] + ops[j]["lat"]
+                at[j] = max(at[j], done + lag)
+                left[j] -= 1
+                if left[j] == 0:
+                    pool.append(j)
+        return max(begin[k] + ops[k]["cost"] + (ops[k]["lat"] if fwd else 0.0) for k in range(n)), order, begin, more
+
+    if not PLAN:
+        needs = [o["need"] for o in ops]
+        way = [0.0] * n
+        for k in range(n - 1, -1, -1):
+            way[k] = ops[k]["cost"] + ops[k]["lat"] + wake + max([way[j] for j in users[k]] or [0.0])
+        urge = [-w - o["b"] for w, o in zip(way, ops)]
+        for it in range(CFG["iters"]):
+            got = plan(needs, users, urge, True)
+            if not PLAN or got[0] < PLAN[0][0]:
+                PLAN[:] = [got]
+            back = plan(users, needs, [-(b + o["cost"]) for b, o in zip(got[2], ops)], False)
+            urge = [-(b + o["cost"]) for b, o in zip(back[2], ops)]
+    CFG["ms"], order, _b, more = PLAN[0]
+    for o, m in zip(ops, more):
+        o["need"].update(m)
 
     total = {"qv": 0, "qs": 0, "qt": 0, "qg": 0}
     known = {q: {} for q in eng}
@@ -486,4 +634,4 @@ def rank_program(g, core, T, topo):
         g.wait_ge(T.sem[s], total[s])
     for s in DMAS:
         g.wait_ge(T.sem[s], 16)
-    g.wait_ge(T.sem.sent, 2 * (ROUNDS - 1) * NENG)
+    g.wait_ge(T.sem.sent, (4 * (ROUNDS - 1) + n_ranks - 1) * NENG)

@@ -1,10 +1,8 @@
-from concourse.bass import DstId, RemoteDMATransfer
 from concourse.mybir import AluOpType, ActivationFunctionType
 
 OP = AluOpType
 ID = ActivationFunctionType.Identity
 RELU = ActivationFunctionType.Relu
-SIGN = ActivationFunctionType.Sign
 ROUNDS = 5
 TH = 36.5
 OFF = 2048.0
@@ -14,40 +12,38 @@ NENG = 16
 TOP = float(2 ** 20)
 CFG = {"gv_a": 0, "gv_b": 0, "gv0": (48, 48), "gv4": 32,
        "ch_a": 2, "ch_b": 2,
-       "e_dp": "s", "e_wt": "s", "e_dn": "s",
+       "e_dp": "s", "e_wt": "s", "e_p4": "s", "e_sa": "s",
        "vf": 0.04, "wake": 0.1, "gam": 1.5, "pe": 0.42,
-       "b0": 3.0, "ba": 0.0, "bb": 0.0, "bs": -2.0, "bc": -30.0, "lr": 2.7, "lx": 6.0, "look": 0.0, "gain": 0.1, "iters": 8}
+       "lr": 5.0, "lx": 6.0, "lc": 5.5,
+       "b0": 3.0, "bs": -2.0, "bc": -30.0, "look": 0.0, "gain": 0.05, "iters": 16}
 PLAN = []
 
 SCRATCH = {
     "xw": ("sbuf", [128, 4096], "bfloat16"), "cw": ("sbuf", [128, CW], "float32"), "cf": ("sbuf", [128, CW], "float32"),
     "ci": ("sbuf", [128, 2048], "int32"), "ri": ("sbuf", [128, 256], "int32"),
     "pint": ("sbuf", [128, 4], "int32"), "pf": ("sbuf", [128, 16], "float32"),
-    "ic": ("sbuf", [128, 128], "float32"), "gcl": ("sbuf", [128, 128], "float32"), "pd": ("sbuf", [128, 128], "float32"),
-    "cm": ("sbuf", [128, 128], "float32"), "ev": ("sbuf", [128, 64], "float32"), "fw": ("sbuf", [128, 64], "float32"),
-    "cy": ("sbuf", [128, 192], "bfloat16"), "sely": ("sbuf", [128, 192], "float16"), "dm": ("sbuf", [128, 64], "float16"),
-    "ca": ("sbuf", [128, 8, 24], "bfloat16"), "cb1": ("sbuf", [128, 8, 16], "bfloat16"), "cb2": ("sbuf", [128, 8, 8], "bfloat16"),
-    "gs4": ("sbuf", [128, 8, 4], "bfloat16"), "gm": ("sbuf", [128, 8], "bfloat16"), "hd": ("sbuf", [128, 8], "float32"),
-    "blk": ("sbuf", [128, 128], "float32"), "mask": ("sbuf", [128, 128], "float32"), "i4": ("sbuf", [128, 128], "float32"),
-    "t0": ("sbuf", [128, 128], "float32"), "t1": ("sbuf", [128, 128], "float32"), "t2": ("sbuf", [128, 128], "float32"),
-    "c15": ("sbuf", [128, 144], "float16"), "pair": ("sbuf", [128, 8, 128], "float16"), "wm": ("sbuf", [128, 16, 128], "float16"),
+    "cy": ("sbuf", [128, 256], "bfloat16"), "posw": ("sbuf", [128, 256], "bfloat16"),
+    "ca": ("sbuf", [128, 8, 32], "bfloat16"), "cb": ("sbuf", [128, 8, 32], "bfloat16"),
+    "gs": ("sbuf", [128, 8, 16], "bfloat16"), "gm": ("sbuf", [128, 8, 16], "bfloat16"),
+    "c15": ("sbuf", [128, 144], "bfloat16"), "pair": ("sbuf", [128, 8, 128], "bfloat16"), "wm": ("sbuf", [128, 16, 128], "bfloat16"),
     "wt": ("sbuf", [128, 16], "bfloat16"), "w16": ("sbuf", [128, 6, 16], "float32"), "lohi": ("sbuf", [128, 2, 16], "float32"),
-    "kc": ("sbuf", [128, 128], "float32"), "acc": ("sbuf", [128, 4], "float32"), "ft": ("sbuf", [128, 256], "bfloat16"),
+    "acc": ("sbuf", [128, 4], "float32"),
     "qi": ("sbuf", [128, 2, 16], "int32"), "qb": ("sbuf", [128, 4, 32], "float32"), "bk": ("sbuf", [128, 16], "float32"),
     "hs": ("sbuf", [128, 16], "float32"), "hi": ("sbuf", [128, 2, 16], "int32"), "ow": ("sbuf", [128, 16], "uint16"),
     "h16": ("sbuf", [128, 16], "float16"), "ew": ("sbuf", [128, 256], "bfloat16"), "lw": ("sbuf", [128, 32], "uint16"),
     "la": ("sbuf", [128, 10, 128], "uint16"), "lb": ("sbuf", [128, 10, 128], "uint16"),
-    "ns": ("sbuf", [128, 10, 8, 8], "bfloat16"), "nl": ("sbuf", [128, 8, 8, 8], "bfloat16"),
+    "rq": ("sbuf", [128, 10, 272], "float16"), "rl": ("sbuf", [128, 10, 16, 16], "float16"),
+    "ns": ("sbuf", [128, 10, 64], "bfloat16"), "nl": ("sbuf", [128, 10, 8, 8], "bfloat16"),
     "PE0": ("psum", [128, 512], "float32"), "PE1": ("psum", [128, 512], "float32"),
 }
-for _n in ("i2", "ni", "c8", "bm", "am"):
-    SCRATCH[_n] = ("sbuf", [128, 128], "float16")
-for _n in ("ib", "nib", "pk", "nk", "ib4", "c2k", "mp", "posw", "g10", "gw"):
+for _n in ("ic", "gcl", "pd", "cm", "blk", "mask", "i4", "kc", "t0", "t1", "t2", "t3"):
+    SCRATCH[_n] = ("sbuf", [128, 128], "float32")
+for _n in ("ib", "nib", "pk", "nk", "i8", "n8", "ib4", "ibk", "c8", "c2k", "mp", "g10", "g10k", "s15", "am"):
     SCRATCH[_n] = ("sbuf", [128, 128], "bfloat16")
 for _u in "01":
     for _n in ("WT", "Dn", "p4", "X4"):
         SCRATCH[_n + "h" + _u] = ("sbuf", [128, 128], "bfloat16")
-    for _n in ("RA", "R1", "q2", "RP", "S"):
+    for _n in ("R1", "S"):
         SCRATCH[_n + "h" + _u] = ("sbuf", [128, 128], "float16")
     for _n in ("SA", "Z", "dl", "Y"):
         SCRATCH[_n + "h" + _u] = ("sbuf", [128, 128], "float32")
@@ -55,8 +51,9 @@ for _u in "01":
         SCRATCH[_n + "h" + _u] = ("sbuf", [128, 2048], "bfloat16")
     for _n in ("Na", "Nb", "E"):
         SCRATCH[_n + "h" + _u] = ("sbuf", [128, 1024], "bfloat16")
-    SCRATCH["Dph" + _u] = ("sbuf", [128, 192], "bfloat16")
-    SCRATCH["Wh" + _u] = ("sbuf", [128, 192], "float32")
+    SCRATCH["Dph" + _u] = ("sbuf", [128, 256], "bfloat16")
+    SCRATCH["Wh" + _u] = ("sbuf", [128, 256], "float32")
+    SCRATCH["thh" + _u] = ("sbuf", [128, 64], "float32")
     SCRATCH["Wch" + _u] = ("sbuf", [128, 10], "bfloat16")
     SCRATCH["Tah" + _u] = ("sbuf", [128, 144], "float16")
     SCRATCH["PA" + _u] = ("psum", [128, 8, 64], "float32")
@@ -64,7 +61,7 @@ for _u in "01":
     SCRATCH["PM" + _u] = ("psum", [128, 512], "float32")
 
 DMAS = ["ldr", "ldx0", "ldx1", "ldc", "sty0", "sty1", "stc0", "stc1"]
-SEMAPHORES = ["qv", "qs", "qt", "qg", "sent"] + ["arq%d" % d for d in (1, 2, 3)] + ["arl%d" % k for k in range(8)] + ["arn%d" % k for k in range(8)] + DMAS
+SEMAPHORES = ["qv", "qs", "qt", "qg", "sent"] + ["arq%d" % d for d in (1, 2, 3)] + ["ar%s%d" % (c, k) for c in "lrn" for k in range(8)] + DMAS
 
 
 def rank_program(g, core, T, topo):
@@ -72,9 +69,8 @@ def rank_program(g, core, T, topo):
     if rank is None:
         return
     n_ranks = len(T.cores)
-    nxt = T.cores[(rank + 1) % n_ranks]
     eng = {"v": g.vector, "s": g.scalar, "t": g.tensor, "g": g, "y": g.sync}
-    ops, lastw, readers, banks = [], {}, {}, {}
+    ops, lastw, readers = [], {}, {}
     cur = [0.0]
 
     def add(q, fns, reads, writes, cost, sem=None, val=0, lat=0.0, deps=()):
@@ -126,13 +122,18 @@ def rank_program(g, core, T, topo):
         return add("v", [lambda: g.vector.tensor_tensor_scan(out=out[1], data0=a[1], data1=b[1], initial=0.0, op0=op0, op1=op1)],
                    [a[0], b[0]] + list(extra), [out[0]], dur(size(out[1]), c))
 
-    def fill(key, ap, v):
-        return add("v", [lambda: g.vector.memset(ap, v)], [], [key], dur(size(ap)))
-
     def act(out, a, func, bias=0.0, scale=1.0, c=1.0, extra=(), acc=None):
         kw = {"accum_out": acc[1]} if acc else {}
         return add("s", [lambda: g.scalar.activation(out=out[1], in_=a[1], func=func, bias=bias, scale=scale, **kw)],
-                   [a[0]] + list(extra), [out[0]] + ([acc[0]] if acc else []), dur(size(out[1]), c))
+                   [a[0]] + list(extra), [out[0]] + ([acc[0]] if acc else []), dur(size(out[1]), c) + 0.01)
+
+    def fill(key, ap, v):
+        return act((key, ap), ("cy0", T.cy[:, 0:size(ap)]), ID, v, 0.0)
+
+    def lin(e, out, a, add_, mul, extra=()):
+        if e == "s":
+            return act(out, a, ID, add_ * mul if mul != 1.0 else add_, mul, extra=extra)
+        return ts(out, a, add_, OP.add, mul, OP.mult, extra=extra)
 
     def mm(items, reads, writes, st=True, sp=True, c=1):
         fns, cost = [], 0.0
@@ -144,23 +145,21 @@ def rank_program(g, core, T, topo):
         ops[k]["st"], ops[k]["sp"] = st, sp
         return k
 
-    def iota(name, pat, base):
-        add("g", [lambda: g.iota(T[name][:], pat, base, 0, allow_small_or_imprecise_dtypes=True)], [], [name], 0.13 + size(T[name][:]) * 0.002)
+    def iota(name, pat, base, key=None):
+        add("g", [lambda: g.iota(T[name][:], pat, base, 0, allow_small_or_imprecise_dtypes=True)], [], [key or name], 0.13 + size(T[name][:]) * 0.002)
 
     def B(name, u=None):
         nm = name if u is None else "%sh%d" % (name, u)
         return (nm, T[nm][:])
 
-    def mask_to(dst):
+    def send(src, dst, sem, d=1, extra=()):
+        to = T.cores[(rank + d) % n_ranks]
+        rid, pid, _s = topo.addr(to)
         m = 0
-        for e in topo.engines(core, dst)[:NENG]:
+        for e in topo.engines(core, to)[:NENG]:
             m |= 1 << e
-        return m
-
-    def send(src, dst, sem):
-        rid, pid, _s = topo.addr(nxt)
-        sd = add("g", [lambda: g.remote_dma(out_ap=dst[1], in_ap=src[1], remote_sem=T.sem[sem], local_sem=T.sem.sent, pid=pid, routing_id=rid, dma_engine_mask=mask_to(nxt))],
-                 [src[0]], [], 0.3, "none", 0, 1.7)
+        sd = add("g", [lambda: g.remote_dma(out_ap=dst[1], in_ap=src[1], remote_sem=T.sem[sem], local_sem=T.sem.sent, pid=pid, routing_id=rid, dma_engine_mask=m)],
+                 [src[0]] + list(extra), [], 0.3, "none", 0, 1.7)
         add(None, [], [], [dst[0]], 0.0, sem, NENG, 0.0, deps=[sd])
 
     g.sync.dma_start(T.ri[:], T.r0[:]).then_inc(T.sem.ldr, 16)
@@ -169,15 +168,13 @@ def rank_program(g, core, T, topo):
     add(None, [], [], ["ri"], 0.0, "ldr", 16, CFG["lr"])
     add(None, [], [], ["xw"], 0.0, "ldx0", 16, CFG["lx"])
     add(None, [], [], ["xw_"], 0.0, "ldx1", 16, CFG["lx"])
-    add("y", [lambda: g.sync.dma_start(T.ci[:], T.c0[:])], [], ["ci"], 0.1, "ldc", 16, 5.5, deps=(1, 2))
+    add("y", [lambda: g.sync.dma_start(T.ci[:], T.c0[:])], [], ["ci"], 0.1, "ldc", 16, CFG["lc"], deps=(1, 2))
 
     add("g", [lambda: g.iota(T.pint[:, 0:1], [[0, 1]], 0, 1)], [], ["pint"], 0.2)
     iota("ic", [[0, 8], [1, 16]], 0)
     iota("gcl", [[1, 8], [0, 16]], 0)
-    iota("ev", [[16, 8], [-2, 8]], 14)
-    iota("cy", [[0, 8], [1, 24]], 128)
-    iota("cm", [[0, 8], [-3, 8], [-1, 2]], 23)
-    iota("fw", [[2, 64]], 0)
+    iota("cy", [[0, 8], [1, 32]], 128, "cy0")
+    iota("cm", [[0, 8], [-4, 8], [-1, 2]], 31)
     iota("pd", [[1, 8], [1, 16]], 1)
     for u in (0, 1):
         cp(("la%d" % u, T.la[:, u, :]), ("ri", T.ri[:, 128 * u:128 * u + 128]))
@@ -192,50 +189,47 @@ def rank_program(g, core, T, topo):
     cp(C(0), ("pi1", T.pint[:, 1:2]))
     cp(C(1), ("pi2", T.pint[:, 2:3]))
     cp(C(2), ("pint", T.pint[:, 0:1]))
+    ts(C(3), C(0), 15.0, OP.is_equal)
+    ts(C(12), C(3), -1.0, OP.mult, 1.0, OP.add)
+    ts(C(13), C(3), 4096.0, OP.mult)
+    ts(C(14), C(13), -OFF, OP.add)
+    ts(C(15), C(14), -1.0, OP.mult)
     ic, gcl = B("ic"), B("gcl")
     ts(B("mask"), ic, col(0), OP.is_equal, extra=["pf0"])
     ts(B("blk"), gcl, col(1), OP.is_equal, extra=["pf1"])
     tt(B("i4"), B("mask"), B("blk"), OP.mult)
-    for nm, w in (("i2", 1.0), ("ib", 1.0), ("ni", -1.0), ("nib", -1.0), ("pk", 1024.0), ("nk", -1024.0), ("ib4", 4096.0)):
-        if SCRATCH[nm][2] == "bfloat16":
-            act(B(nm), B("i4"), ID, 0.0, w)
-        else:
-            ts(B(nm), B("i4"), w, OP.mult)
-    cp(B("hd"), ("blk", T.blk[:, 0:128:16]))
-    for j in range(4):
-        act(("gs4%d" % j, T.gs4[:, :, j]), B("hd"), ID)
-    gs4 = ["gs4%d" % j for j in range(4)]
-    act(B("gm"), B("hd"), ID, 0.0, -2.0)
-    fill("ca", T.ca[:], 0.0)
-    fill("ca", T.ca[:, :, 1:24:3], -1024.0)
-    fill("ca", T.ca[:, :, 0], 1024.0)
-    act(B("cy"), B("cy"), ID, 0.0, 8192.0)
-    ts(("sely0", T.sely[:, 0:192:3]), B("ev"), 1.0, OP.add, col(2), OP.is_equal, extra=["pf2"])
-    ts(("sely1", T.sely[:, 1:192:3]), B("ev"), col(2), OP.is_equal, extra=["pf2"])
-    ts(("sely2", T.sely[:, 2:192:3]), B("ev"), col(2), OP.is_equal, extra=["pf2"])
+    for nm, w in (("ib", 1.0), ("nib", -1.0), ("pk", 1024.0), ("nk", -1024.0), ("i8", 0.125), ("n8", -0.125), ("ib4", 4096.0)):
+        act(B(nm), B("i4"), ID, 0.0, w)
+    act(B("ibk"), B("i4"), ID, 0.0, col(12), extra=["pf12"])
+    act(B("s15"), B("blk"), ID, 0.0, col(3), extra=["pf3"])
+    act(B("gs"), B("blk"), ID)
+    fill("gs", T.gs[:, :, 1:3], 0.0)
+    fill("gs", T.gs[:, :, 8], 0.0)
+    act(B("gm"), B("blk"), ID, 0.0, -2.0)
+    for ap, v in ((T.ca[:], 0.0), (T.ca[:, :, 1:32:4], -3072.0), (T.ca[:, :, 2:32:4], -2048.0), (T.ca[:, :, 0], 2048.0)):
+        fill("ca", ap, v)
     for u in (0, 1):
-        ts(B("Ta", u), ("cy", T.cy[:, 0:144]), 0.0, OP.mult, c=0.5)
+        ts(B("Ta", u), ("cy0", T.cy[:, 0:144]), 0.0, OP.mult, c=0.5)
         fill("Wch%d" % u, T["Wch%d" % u][:], 1.0)
-    ts(C(3), C(0), 15.0, OP.is_equal)
-    ts(B("c15"), ("cy", T.cy[:, 0:144]), 0.0, OP.mult, c=0.5)
-    ts(("c15", T.c15[:, 0:128]), B("i4"), col(3), OP.mult, extra=["pf3"])
+    fill("c15", T.c15[:], 0.0)
+    act(("c15", T.c15[:, 0:128]), B("i4"), ID, 0.0, col(3), extra=["pf3"])
     ts(C(4), C(2), 8.0, OP.is_equal, -8192.0, OP.mult)
     ts(C(5), C(2), 9.0, OP.is_equal, -TOP, OP.mult)
-    fill("cm", T.cm[:, 15:128:16], 24.0)
+    fill("cm", T.cm[:, 15:128:16], 0.0)
     ts(B("t0"), B("cm"), 0.5, OP.add, col(4), OP.mult, extra=["pf4"])
     ts(B("t1"), gcl, col(2), OP.is_equal, col(5), OP.add, extra=["pf2", "pf5"])
     tt(B("g10"), B("t0"), B("t1"), OP.add)
-    ts(B("gw"), gcl, col(2), OP.is_equal, -4096.0, OP.mult, extra=["pf2"])
-    ts(C(6), C(2), 8.0, OP.is_lt, 64.0, OP.mult)
+    act(B("g10k"), B("g10"), ID)
+    fill("g10k", T.g10k[:, 15:128:16], 0.0)
+    ts(C(6), C(3), -1.0 / 64, OP.mult)
     act(B("kc"), B("ic"), ID, col(6), 0.0, extra=["pf6"])
-    cur[0] = CFG["bc"]
     ts(C(7), C(0), 16.0, OP.add)
-    ts(B("t0"), B("pd"), col(0), OP.is_equal, extra=["pf0"])
-    ts(B("t1"), B("pd"), col(7), OP.is_equal, extra=["pf7"])
-    tt(B("t0"), B("t0"), B("t1"), OP.add)
-    tt(B("bm"), B("mask"), B("t0"), OP.subtract)
+    ts(B("t2"), B("pd"), col(0), OP.is_equal, extra=["pf0"])
+    ts(B("t3"), B("pd"), col(7), OP.is_equal, extra=["pf7"])
+    tt(B("t2"), B("t2"), B("t3"), OP.add)
+    tt(B("t2"), B("mask"), B("t2"), OP.subtract)
     for k in range(8):
-        ts(("pair%d" % k, T.pair[:, k, :]), B("bm"), T.hd[:, k:k + 1], OP.mult, c=0.5, extra=["hd"])
+        act(("pair%d" % k, T.pair[:, k, :]), B("t2"), ID, 0.0, T.blk[:, 16 * k:16 * k + 1], extra=["blk"])
     ts(C(8), C(0), col(1), OP.add, 1.0, OP.add, extra=["pf1"])
     ts(C(9), C(8), 16.0, OP.is_ge, -16.0, OP.mult)
     tt(C(8), C(8), C(9), OP.add)
@@ -251,26 +245,27 @@ def rank_program(g, core, T, topo):
     scan(W(2), W(0), W(1), OP.mult, OP.add)
     ts(W(3), r16, col(9), OP.is_equal, extra=["pf9"])
     tt(W(3), W(3), W(2), OP.mult)
-    ts(W(1), W(0), 0.0, OP.mult, 1.0, OP.add)
+    fill("w161", T.w16[:, 1, :], 1.0)
     scan(W(2), W(1), W(3), OP.mult, OP.max)
     ts(W(4), r16, col(9), OP.is_gt, 33.0, OP.mult, extra=["pf9"])
     ts(W(5), r16, col(10), OP.is_le, extra=["pf10"])
     tt(W(4), W(4), W(5), OP.mult)
     ts(B("wt"), W(4), -1.0, OP.add, T.w16[:, 2, 15:16], OP.mult, extra=["w162"])
-    ts(B("c8"), ic, 0.0, OP.mult, NO, OP.add)
-    fill("cb1", T.cb1[:], 0.0)
-    fill("cb1", T.cb1[:, :, 0:16:15], -1000.0)
-    fill("cb2", T.cb2[:], 0.0)
-    fill("cb2", T.cb2[:, :, 0], 1000.0)
+    fill("c8", T.c8[:], NO)
+    ts(("pad", T.rq[:, :, 256:272]), ("cy0", T.cy[:, 0:160]), 0.0, OP.mult, NO, OP.add, c=0.5)
+    for ap, v in ((T.cb[:], -1024.0), (T.cb[:, :, 1:32:4], 2048.0), (T.cb[:, :, 29], 3040.0), (T.cb[:, :, 0:31:30], -2048.0)):
+        fill("cb", ap, v)
     fill("c2k", T.c2k[:], OFF)
     fill("mp", T.mp[:], -1.0e9)
     fill("mp", T.mp[:, 0:128:16], OFF)
     fill("mp", T.mp[:, 15:128:16], OFF)
-    ts(("t2", T.t2[:, 0:64]), B("fw"), col(2), OP.is_equal, extra=["pf2"])
-    ts(("t2", T.t2[:, 64:128]), B("fw"), 1.0, OP.add, col(2), OP.is_equal, extra=["pf2"])
-    tt(B("dm"), ("t2", T.t2[:, 0:64]), ("t2", T.t2[:, 64:128]), OP.subtract)
     for u in (0, 1):
         fill("dlh%d" % u, T["dlh%d" % u][:], 0.0)
+    fill("cw", T.cw[:, 2048:CW], 0.0)
+    fill("cf_", T.cf[:, 2048:CW], 0.0)
+    act(B("cy"), ("cy0", T.cy[:]), ID, 0.0, 8192.0)
+    lastw["cy0"] = lastw["cy"]
+    ops[lastw["cy"]]["need"].update(readers["cy0"][:-1])
     ts(B("t0"), B("i4"), 2.0, OP.mult)
     tt(B("am"), B("t0"), B("blk"), OP.subtract)
     ts(("lo", T.lohi[:, 0, :]), ("mask", T.mask[:, 0:16]), -1.0, OP.mult)
@@ -278,13 +273,13 @@ def rank_program(g, core, T, topo):
     for i in range(16):
         ts(("wm%d" % i, T.wm[:, i, :]), B("am"), T.lohi[:, 0, i:i + 1], OP.max, T.lohi[:, 1, i:i + 1], OP.min, c=0.5, extra=["lo", "hi_"])
     ts(B("t1"), ic, col(0), OP.is_gt, 16384.0, OP.mult, extra=["pf0"])
-    ts(B("t2"), ic, col(0), OP.not_equal, 4096.0, OP.mult, extra=["pf0"])
-    tt(B("posw"), B("t1"), B("t2"), OP.add)
+    ts(B("t3"), B("mask"), -4096.0, OP.mult)
+    tt(("posw", T.posw[:, 0:128]), B("t1"), B("t3"), OP.add)
+    act(("posw", T.posw[:, 128:256]), ("posw", T.posw[:, 0:128]), ID)
     ts(C(11), C(0), OFF, OP.add)
-    fill("cw", T.cw[:, 2048:CW], 0.0)
-    fill("cf_", T.cf[:, 2048:CW], 0.0)
+    cur[0] = CFG["bc"]
     for k in range(4):
-        ts(("cw%d" % k, T.cw[:, 512 * k:512 * k + 512]), ("ci", T.ci[:, 512 * k:512 * k + 512]), -OFF, OP.add)
+        ts(("cw%d" % k, T.cw[:, 512 * k:512 * k + 512]), ("ci", T.ci[:, 512 * k:512 * k + 512]), col(14), OP.add, extra=["pf14"])
     cws = ["cw%d" % k for k in range(4)]
     cur[0] = 0.0
 
@@ -321,51 +316,52 @@ def rank_program(g, core, T, topo):
     def first_fail(t, u):
         k = 2 * t + u
         PA, PM, G, M, N = T["PA%d" % u], T["PM%d" % u], T["Gah%d" % u], T["Mah%d" % u], T["Nah%d" % u]
-        kd, ra = "PA%d:D" % u, B("RA", u)
-        ts(ra, ("la%d" % k, T.la[:, k, :]), -OFF, OP.add, c=0.5)
-        ky, Y = "PM%d:Y" % u, PM[:, 0:192]
-        mm([(Y, T.ib[:], T.cy[:]), (Y, ra[1], T.sely[:])], ["ib", "cy", ra[0], "sely0", "sely1", "sely2"], [ky])
+        kd, kr = "PA%d:D" % u, "rl%d" % k
+        ky, Y = "PM%d:Y" % u, PM[:, 0:256]
+        mm([(Y, T.ib[:], T.cy[:])] + [(PM[:, j:256:4], T.ib[:], T.rl[:, k, 0:8, (14 if j else 15)::-2]) for j in range(4)], ["ib", "cy", kr], [ky])
         kg, km, kn = gather(u, "a", t, "la")
-        items = [(PA[:, :, 0:24], T.ib[:], T.ca[:])]
+        items = [(PA[:, :, 0:32], T.ib[:], T.ca[:])]
         for p in range(16):
-            z = 3 * (7 - p // 2)
+            z = 4 * (7 - p // 2)
             if p % 2:
-                items.append((PA[:, :, z:z + 3:2], G[:, p:2048:16], T.gs4[:, :, 0:2]))
+                items.append((PA[:, :, z:z + 4], G[:, p:2048:16], T.gs[:, :, 7:11]))
             else:
-                n = 4 if p else 2
-                items.append((PA[:, :, z + 1:z + 1 + n], G[:, p:2048:16], T.gs4[:, :, 0:n]))
-        mm(items, ["ib", "ca"] + gs4 + kg, [kd], sp=False)
+                n = 5 if p else 3
+                items.append((PA[:, :, z + 1:z + 1 + n], G[:, p:2048:16], T.gs[:, :, 3:3 + n]))
+        mm(items, ["ib", "ca", "gs"] + kg, [kd], sp=False)
         if t:
-            mm([(PA[:, :, 3 * (7 - i) + 1], N[:, i:1024:8], T.gm[:]) for i in range(7)], kn + ["gm"], [kd], st=False, sp=False)
-        mm([(PA[:, :, 3 * (7 - p // 2) + (0 if p % 2 else 2)], M[:, p:2048:16], T.gm[:]) for p in range(15)], km + ["gm"], [kd], st=False, sp=t == 0)
+            c0, c1 = T.rl[:, k, 8:16, 15::-2], T.rl[:, k, 8:16, 14:0:-2]
+            mm([(PA[:, :, 0:32:4], T.i8[:], c0), (PA[:, :, 1:32:4], T.n8[:], c0), (PA[:, :, 2:32:4], T.n8[:], c0),
+                (PA[:, :, 4:32:4], T.n8[:], c1), (PA[:, :, 5:32:4], T.n8[:], c1), (PA[:, :, 6:32:4], T.i8[:], c1)], [kr, "i8", "n8"], [kd], st=False, sp=False)
+            mm([(PA[:, :, 4 * (7 - i) + 1], N[:, i:1024:8], T.gm[:, :, 0]) for i in range(7)], kn + ["gm"], [kd], st=False, sp=False)
+        items = []
+        for p in range(15):
+            z = 4 * (7 - p // 2)
+            items.append((PA[:, :, z], M[:, p:2048:16], T.gm[:, :, 0]) if p % 2 else (PA[:, :, z + 2:z + 4], M[:, p:2048:16], T.gm[:, :, 0:2]))
+        mm(items, km + ["gm"], [kd], st=False, sp=t == 0)
         if t:
-            nl = T.nl[:, k - 2, :, :]
-            mm([(PA[:, :, 0:24:3], T.nk[:], nl), (PA[:, :, 1:24:3], T.pk[:], nl), (PA[:, :, 2:24:3], T.nk[:], nl)], ["nl%d" % (k - 2), "pk", "nk"], [kd], st=False)
-        s = float(2 ** 22)
-        if CFG["e_dp"] == "s":
-            act(B("Dp", u), (kd, PA[:, :, 0:24]), ID, -TH * s, s)
-        else:
-            ts(B("Dp", u), (kd, PA[:, :, 0:24]), -TH, OP.add, s, OP.mult)
+            nl = T.nl[:, k, :, 7::-1]
+            mm([(PA[:, :, j:32:4], w[:], nl) for j, w in enumerate((T.nk, T.pk, T.pk, T.nk))], ["nl%d" % k, "pk", "nk"], [kd], st=False)
+        lin(CFG["e_dp"], B("Dp", u), (kd, PA[:, :, 0:32]), -TH, float(2 ** 22))
         lastw["donea%d.%d" % (u, t)] = scan(B("W", u), B("Dp", u), (ky, Y), OP.max, OP.min)
 
-    def moved(u, near, ra, out, kout, last):
-        PM = T["PM%d" % u]
-        kf, F = "PM%d:F" % u, PM[:, 192:256]
-        mm([(F, ra[1], T.dm[:])], [ra[0], "dm"], [kf])
+    def moved(u, near, rp, out, kout, last):
+        kf, F = "PM%d:F" % u, T["PM%d" % u][:, 384:448]
+        mm([(F, T.ib[:], rp[2]), (F, T.nib[:], rp[3])], [rp[0], "ib", "nib"], [kf])
         tt(("dlh%d" % u, T["dlh%d" % u][:, 1:128:2]), (kf, F), near, OP.mult)
         mm([(out, T["dlh%d" % u][:], T.i4[:])], ["dlh%d" % u, "i4"], [kout], sp=False, c=4)
-        mm([(out, T.i2[:], ra[1])], ["i2", ra[0]], [kout], st=False, sp=last)
+        mm([(out, rp[1], T.ib[:])], ["ib", rp[0]], [kout], st=False, sp=last)
 
     def stage_a(t, u):
         k = 2 * t + u
         PA, PB, PM = T["PA%d" % u], T["PB%d" % u], T["PM%d" % u]
         Wd, Wc, Ta, WT = T["Wh%d" % u], T["Wch%d" % u], T["Tah%d" % u], T["WTh%d" % u]
-        end = ("Wh%d" % u, Wd[:, 23:192:24])
+        end = ("Wh%d" % u, Wd[:, 31:256:32])
         wc = ("Wch%d" % u, Wc[:, 0:8])
         cp(wc, end)
         tt(("Tah%d" % u, Ta[:, 15:128:16]), end, wc, OP.subtract)
-        kl, L = "PB%d:L" % u, PB[:, :, 24]
-        mm([(L, Ta[:, 15 - i:143 - i], T.i2[:, i:128:16]) for i in range(16)], ["Tah%d" % u, "i2"], [kl])
+        kl, L = "PM%d:L" % u, PM[:, 448:456]
+        mm([(L, Ta[:, 15 - i:143 - i], T.ib[:, i:128:16]) for i in range(16)], ["Tah%d" % u, "ib"], [kl])
         d = t % n_ranks
         c0, c1 = 8 * u, 8 * u + 8
         hs = ("hs%d" % u, T.hs[:, c0:c1])
@@ -373,23 +369,17 @@ def rank_program(g, core, T, topo):
         kt, TT_ = "PB%d:T" % u, PB[0:10, :, 48:64]
         mm([(TT_, Wc[:, 0:10], T.ib[:])], [wc[0], "ib"], [kt])
         wt = ("WTh%d" % u, WT[0:10, :])
-        if CFG["e_wt"] == "s":
-            act(wt, (kt, TT_), ID)
-        else:
-            cp(wt, (kt, TT_))
-        act(("ft%d" % u, T.ft[0:10, 128 * u:128 * u + 128]), (kt, TT_), SIGN, -TOP, acc=("acc%d.%d" % (t % 2, u), T.acc[0:10, 2 * (t % 2) + u:2 * (t % 2) + u + 1]))
+        lin(CFG["e_wt"], wt, (kt, TT_), 0.0, 1.0)
         k1, P1 = "PB%d:U" % u, PB[:, :, 32:48]
         mm([(P1, T.g10[0:10, :], wt[1])], ["g10", wt[0]], [k1])
-        if CFG["e_dn"] == "s":
-            act(B("Dn", u), (k1, P1), RELU, 0.0, -1.0)
-        else:
-            ts(B("Dn", u), (k1, P1), -1.0, OP.mult, 0.0, OP.max)
+        j = 2 * (t % 2) + u
+        act(B("Dn", u), (k1, P1), RELU, 0.0, -1.0, acc=("acc%d" % j, T.acc[:, j:j + 1]))
         kk, K = "PA%d:D" % u, PA[:, :, 32:48]
         if t:
-            moved(u, ("nl%d" % (k - 2), T.nl[:, k - 2, :, 7::-1]), B("RA", u), K, kk, False)
+            moved(u, ("nl%d" % k, T.nl[:, k, :, :]), ("rl%d" % k, T.rl[:, k, 0:8, :], T.rl[:, k, 0:8, 0:16:2], T.rl[:, k, 0:8, 1:16:2]), K, kk, False)
         else:
-            mm([(K, T.i2[:], T["RAh%d" % u][:])], ["i2", "RAh%d" % u], [kk], sp=False)
-        mm([(K, T.g10[0:10, :], wt[1]), (K, T.ib[:], T["Dnh%d" % u][:])], ["g10", wt[0], "ib", "Dnh%d" % u], [kk], st=False)
+            mm([(K, T.rl[:, k, 0:8, :], T.ib[:])], ["ib", "rl%d" % k], [kk], sp=False)
+        mm([(K, T.g10k[0:10, :], wt[1]), (K, T.ibk[:], T["Dnh%d" % u][:])], ["g10k", wt[0], "ibk", "Dnh%d" % u], [kk], st=False)
         h0, h1 = ("hi0%d" % u, T.hi[:, 0, c0:c1]), ("hi1%d" % u, T.hi[:, 1, c0:c1])
         tt(h0, hs, ("bk", T.bk[:, c0:c1]) if t else ("qb0", T.qb[:, 0, 16 + c0:16 + c1]), OP.add)
         ts(h1, h0, 6, OP.arith_shift_right, 2047, OP.bitwise_and)
@@ -398,82 +388,91 @@ def rank_program(g, core, T, topo):
         if t:
             tt(B("Z", u), ("cw", T.cw[:, 0:CW].indirect(ow[1])), B("Dn", u), OP.add, c=CFG["gam"], extra=[ow[0]])
         else:
-            ts(B("Y", u), ("ci", T.ci[:, 0:2048].indirect(ow[1])), -OFF, OP.add, c=CFG["gam"], extra=[ow[0]])
+            ts(B("Y", u), ("ci", T.ci[:, 0:2048].indirect(ow[1])), col(14), OP.add, c=CFG["gam"], extra=[ow[0], "pf14"])
             tt(B("Z", u), B("Y", u), B("Dn", u), OP.add)
         tt(B("R1", u), B("Z", u), (kk, K), OP.min)
+        lb = ("lb%d" % k, T.lb[:, k, :])
+        ts(lb, B("R1", u), OFF, OP.add, c=0.5)
+        if t < ROUNDS - 1:
+            send(lb, ("la%d" % (k + 2), T.la[:, k + 2, :]), "arl%d" % k)
         R1, E = T["R1h%d" % u], T["Eh%d" % u]
-        ks, Sc = "PB%d:U" % u, PB[:, :, 32:48]
+        ks, Sc = "PM%d:H" % u, PM[:, 256:384]
         for b in (0, 1):
             P, kp = T["PE%d" % b], "PE%d:E" % b
             for j in range(4):
                 mm([(P[:, 128 * j:128 * j + 128], T.pair[:, 4 * b + j, :], R1[:])], ["R1h%d" % u, "pair%d" % (4 * b + j)], [kp])
             ts(("Eh%d.%d" % (u, b), E[:, 512 * b:512 * b + 512]), (kp, P[:, 0:512]), 0.0, OP.is_equal)
         for j in range(8):
-            mm([(PB[:, j, 32:48], E[:, 128 * j:128 * j + 128], T.wt[:])], ["Eh%d.%d" % (u, j // 4), "wt"], [ks])
-        ts(B("q2", u), (ks, Sc), 0.0, OP.is_le, NO, OP.mult)
-        kh, H = "PM%d:H" % u, PM[:, 384:512]
-        mm([(H, R1[:], T.i2[:]), (H, T.i2[:], T.c8[:]), (H, T.ni[:], T["q2h%d" % u][:])], ["R1h%d" % u, "i2", "c8", "ni", "q2h%d" % u], [kh])
-        scan(B("RP", u), B("q2", u), (kh, H), OP.add, OP.max)
-        ka, A = "PM%d:A" % u, PM[:, 256:384]
-        mm([(A, T["RPh%d" % u][:], T.i2[:])], ["RPh%d" % u, "i2"], [ka])
-        lb = ("lb%d" % k, T.lb[:, k, :])
-        ts(lb, (ka, A), OFF, OP.add)
+            mm([(PM[:, 256 + 16 * j:272 + 16 * j], E[:, 128 * j:128 * j + 128], T.wt[:])], ["Eh%d.%d" % (u, j // 4), "wt"], [ks])
+        q2 = ("q2%d" % k, T.rq[:, k, 128:256])
+        ts(q2, (ks, Sc), 0.0, OP.is_le, NO, OP.mult)
+        kh, H = "PM%d:H" % u, PM[:, 256:384]
+        mm([(H, R1[:], T.ib[:]), (H, T.ib[:], T.c8[:]), (H, T.nib[:], q2[1])], ["R1h%d" % u, "ib", "c8", "nib", q2[0]], [kh])
+        scan(("rp%d" % k, T.rq[:, k, 0:128]), q2, (kh, H), OP.add, OP.max)
         if t < ROUNDS - 1:
-            send(lb, ("la%d" % (k + 2), T.la[:, k + 2, :]), "arl%d" % k)
+            send(("rp%d" % k, T.rq[:, k, 0:256]), ("rl%d" % (k + 2), T.rl[:, k + 2, :, :]), "arr%d" % k, extra=[q2[0]])
 
     def stage_b(t, u):
         k = 2 * t + u
         PA, PB, PM, G, M, N = T["PA%d" % u], T["PB%d" % u], T["PM%d" % u], T["Gbh%d" % u], T["Mbh%d" % u], T["Nbh%d" % u]
         kg, km, kn = gather(u, "b", t, "lb")
-        k2, k1 = "PB%d:D2" % u, "PB%d:D1" % u
-        items = [(PB[:, :, 16:24], T.ib[:], T.cb2[:])]
-        for i in range(8):
-            a, b = max(7 - i, 1), min(9 - i, 8)
-            items.append((PB[:, :, 16 + a:16 + b], G[:, 2 * i:2048:16], T.gs4[:, :, 0:b - a]))
-        mm(items, ["ib", "cb2"] + gs4 + kg, [k2], sp=False)
-        mm([(PB[:, :, 23 - i], N[:, i:1024:8], T.gm[:]) for i in range(7)], kn + ["gm"], [k2], st=False)
-        ns = ("ns%d" % k, T.ns[:, k, :, :])
-        ts(ns, (k2, PB[:, :, 16:24]), TH, OP.is_lt)
-        if t < ROUNDS - 1:
-            send(ns, ("nl%d" % k, T.nl[:, k, :, :]), "arn%d" % k)
-        cur[0] += CFG["bs"]
-        items = [(PB[:, :, 0:16], T.ib[:], T.cb1[:])]
+        kd, kq, kp = "PB%d:D" % u, "q2%d" % k, "rp%d" % k
+        items = [(PB[:, :, 0:32], T.ib[:], T.cb[:])]
         for p in range(15):
-            a, b = max(p, 1), min(p + 2, 15)
-            items.append((PB[:, :, a:b], G[:, p:2048:16], T.gs4[:, :, 0:b - a]))
-        mm(items, ["ib", "cb1"] + gs4 + kg, [k1], sp=False)
-        mm([(PB[:, :, p + 1], M[:, p:2048:16], T.gm[:]) for p in range(14)], km + ["gm"], [k1], st=False)
-        act(B("p4", u), (k1, PB[:, :, 0:16]), RELU, -TH * 8192.0, 8192.0)
+            z = 4 * (p // 2)
+            if p % 2:
+                items.append((PB[:, :, z + 2:z + 5], G[:, p:2048:16], T.gs[:, :, 3:6]))
+            else:
+                a, b = (4 if p == 0 else 0), (4 if p == 14 else 7)
+                items.append((PB[:, :, z - 3 + a:z - 3 + b], G[:, p:2048:16], T.gs[:, :, a:b]))
+        mm(items, ["ib", "cb", "gs"] + kg, [kd], sp=False)
+        mm([(PB[:, :, 4 * i + 1], N[:, i:1024:8], T.gm[:, :, 0]) for i in range(7)], kn + ["gm"], [kd], st=False, sp=False)
+        items = []
+        for p in range(14):
+            z = 4 * (p // 2)
+            items.append((PB[:, :, z + 4], M[:, p:2048:16], T.gm[:, :, 0]) if p % 2 else (PB[:, :, z + 2:z + 4], M[:, p:2048:16], T.gm[:, :, 0:2]))
+        mm(items, km + ["gm"], [kd], st=False, sp=False)
+        c0, c1 = T.rq[:, k, 129:256:2], T.rq[:, k, 130:258:2]
+        mm([(PB[:, :, 1:32:4], T.n8[:], c0), (PB[:, :, 3:32:4], T.n8[:], c0), (PB[:, :, 1:32:4], T.n8[:], c1), (PB[:, :, 3:32:4], T.i8[:], c1),
+            (PB[:, :, 0:32:2], T.n8[:], T.rq[:, k, 128:256])], [kq, "pad", "i8", "n8"], [kd], st=False)
+        ns = ("ns%d" % k, T.ns[:, k, :])
+        ts(B("th", u), (kd, PB[:, :, 3:32:4]), TH, OP.is_lt, 4096.0 + TH, OP.mult)
+        tt(ns, (kd, PB[:, :, 1:32:4]), B("th", u), OP.is_lt)
+        if t < ROUNDS - 1:
+            send(ns, ("nl%d" % (k + 2), T.nl[:, k + 2, :, :]), "arn%d" % k)
+        cur[0] += CFG["bs"]
+        if CFG["e_p4"] == "s":
+            act(B("p4", u), (kd, PB[:, :, 0:32:2]), RELU, -TH * 8192.0, 8192.0)
+        else:
+            ts(B("p4", u), (kd, PB[:, :, 0:32:2]), TH, OP.is_gt, 4096.0, OP.mult)
         scan(B("X4", u), B("mp"), B("p4", u), OP.max, OP.subtract, 0.5)
-        kh, H = "PM%d:H" % u, PM[:, 384:512]
-        mm([(H, T.i2[:], T["RPh%d" % u][:]), (H, T.ib[:], T.c2k[:]), (H, T.nib[:], T["X4h%d" % u][:])], ["RPh%d" % u, "i2", "ib", "c2k", "nib", "X4h%d" % u], [kh])
+        kh, H = "PM%d:H" % u, PM[:, 256:384]
+        mm([(H, T.ib[:], T.rq[:, k, 0:128]), (H, T.ib[:], T.c2k[:]), (H, T.nib[:], T["X4h%d" % u][:])], [kp, "ib", "c2k", "nib", "X4h%d" % u], [kh])
         scan(B("S", u), B("X4", u), (kh, H), OP.max, OP.min)
-        mm([(H, T["Sh%d" % u][:], T.i2[:])], ["Sh%d" % u, "i2"], [kh])
-        act(B("SA", u), (kh, H), ID, OFF if t == ROUNDS - 1 else 0.0)
+        mm([(H, T["Sh%d" % u][:], T.ib[:])], ["Sh%d" % u, "ib"], [kh])
+        lin(CFG["e_sa"], B("SA", u), (kh, H), OFF if t == ROUNDS - 1 else col(13), 1.0, extra=["pf13"])
         if t == ROUNDS - 1:
             cur[0] -= 3.0
-            ra = B("RA", u)
-            ts(ra, ("lb%d" % k, T.lb[:, k, :]), -OFF, OP.add, c=0.5)
             kk, K = "PA%d:D" % u, PA[:, :, 32:48]
-            moved(u, (ns[0], T.ns[:, k, :, 7::-1]), ra, K, kk, True)
+            moved(u, ns, (kp, T.rq[:, k, 0:128], T.rq[:, k, 0:128:2], T.rq[:, k, 1:128:2]), K, kk, True)
             act(B("Y", u), (kk, K), ID, OFF)
             add("y", [lambda: g.sync.dma_start(T.yr[:, 128 * u:128 * u + 128], T["Yh%d" % u][:])], ["Yh%d" % u], [], 0.1, "sty%d" % u, 16, 2.0)
 
     def count(t):
         P, c = T.PE1[:, 0:1], 2 * (t % 2)
-        mm([(P, T.kc[0:10, :], T.acc[0:10, c + u:c + u + 1]) for u in (0, 1)], ["kc", "acc%d.0" % (t % 2), "acc%d.1" % (t % 2)], ["PE1:E"], c=4)
+        mm([(P, T.kc[:], T.acc[:, c + u:c + u + 1]) for u in (0, 1)], ["kc", "acc%d" % c, "acc%d" % (c + 1)], ["PE1:E"], c=4)
         d = (t + 1) % n_ranks
         ts(B("bk"), ("qb%d" % d, T.qb[:, d, 16:32]), P, OP.add, extra=["PE1:E"])
 
     def winners():
         P, kp = T.PE0, "PE0:E"
         cp(B("h16"), ("hi10", T.hi[:, 1, :]), extra=["hi11"])
-        items = [(P[:, 128 * u:128 * u + 128], T.ib[:], T.posw[:]) for u in (0, 1)]
-        mm([(P[:, 0:256], T.gw[0:10, :], T.ft[0:10, :])] + items, ["ib", "posw", "gw", "ft0", "ft1"], [kp], sp=False)
+        mm([(P[:, 0:256], T.ib[:], T.posw[:])] + [(P[:, 128 * u:128 * u + 128], T.s15[:], T["Dnh%d" % u][:]) for u in (0, 1)],
+           ["ib", "posw", "s15", "Dnh0", "Dnh1"], [kp], sp=False)
         mm([(P[:, i:256:16], T.wm[:, i, :], T.h16[:]) for i in range(16)], ["h16"] + ["wm%d" % i for i in range(16)], [kp], st=False)
         ts(B("ew"), (kp, P[:, 0:256]), 0.0, OP.is_equal)
         Q = P[:, 256:272]
-        mm([(Q, T.i2[:], T.h16[:])] + [(Q, T.ib4[:], T.ew[:, i:256:16]) for i in range(16)], ["i2", "h16", "ib4", "ew"], [kp])
+        mm([(Q, T.ib[:], T.h16[:])] + [(Q, T.ib4[:], T.ew[:, i:256:16]) for i in range(16)], ["ib", "h16", "ib4", "ew"], [kp])
         ts(("lw", T.lw[:, 0:32:2]), (kp, Q), col(11), OP.min, extra=["pf11"])
 
     def scatter(t, u):
@@ -487,26 +486,25 @@ def rank_program(g, core, T, topo):
     order_u = (1, 0)
     for u in order_u:
         cur[0] = CFG["b0"] * u
+        ts(B("R1", u), ("la%d" % u, T.la[:, u, :]), -OFF, OP.add, c=0.5)
+        H = ("PM%d:H" % u, T["PM%d" % u][:, 256:384])
+        mm([(H[1], T["R1h%d" % u][:], T.ib[:])], ["R1h%d" % u, "ib"], [H[0]])
+        cp(("rl%d" % u, T.rl[:, u, 0:8, :]), H)
         first_fail(0, u)
     cur[0] = 0.0
-    P = T.PE0[:, 0:16]
     for u in (0, 1):
-        mm([(T.PE0[:, 8 * u:8 * u + 8], T.c15[:, 15 - i:143 - i], T["RAh%d" % u][:, i:128:16]) for i in range(16)], ["c15", "RAh%d" % u], ["PE0:E"])
-    ts(("qi0", T.qi[:, 0, :]), ("PE0:E", P), OFF + 64.0, OP.add)
+        mm([(T.PE0[:, 8 * u:8 * u + 8], T.c15[:, 15 - i:143 - i], T["R1h%d" % u][:, i:128:16]) for i in range(16)], ["c15", "R1h%d" % u], ["PE0:E"])
+    ts(("qi0", T.qi[:, 0, :]), ("PE0:E", T.PE0[:, 0:16]), OFF + 64.0, OP.add)
     ts(("qi1", T.qi[:, 1, :]), ("qi0", T.qi[:, 0, :]), 63, OP.bitwise_and)
     cp(("qb0", T.qb[:, 0, 0:16]), ("qi0", T.qi[:, 0, :]))
     ts(("qb0", T.qb[:, 0, 16:32]), ("qi1", T.qi[:, 1, :]), 2048.0, OP.mult)
     for d in range(1, n_ranks):
-        dst = T.cores[(rank + d) % n_ranks]
-        rid, pid, _s = topo.addr(dst)
-        sd = add("g", [lambda d=d, dst=dst, rid=rid, pid=pid: g.remote_dma(out_ap=T.qb[:, d, :], in_ap=T.qb[:, 0, :], remote_sem=T.sem["arq%d" % d], local_sem=T.sem.sent,
-                                                                          pid=pid, routing_id=rid, dma_engine_mask=mask_to(dst))], ["qb0"], [], 0.3, "none", 0, 3.0)
-        add(None, [], [], ["qb%d" % d], 0.0, "arq%d" % d, NENG, 0.0, deps=[sd])
+        send(("qb0", T.qb[:, 0, :]), ("qb%d" % d, T.qb[:, d, :]), "arq%d" % d, d)
     for t in range(ROUNDS):
         if t == ROUNDS - 1:
             cur[0] = CFG["bc"]
-            for k in (0, 1):
-                act(("cf%d" % k, T.cf[:, 1024 * k:1024 * k + 1024]), ("cw", T.cw[:, 1024 * k:1024 * k + 1024]), ID, OFF)
+            for k in range(4):
+                act(("cf%d" % (k // 2), T.cf[:, 512 * k:512 * k + 512]), ("cw", T.cw[:, 512 * k:512 * k + 512]), ID, col(15), extra=["pf15"])
         for u in order_u:
             cur[0] = CFG["b0"] * u
             stage_a(t, u)
@@ -515,14 +513,14 @@ def rank_program(g, core, T, topo):
         if t < ROUNDS - 1:
             count(t)
         for u in order_u:
-            cur[0] = CFG["b0"] * u + CFG["bb"]
+            cur[0] = CFG["b0"] * u
             stage_b(t, u)
         cur[0] = CFG["bs"]
         for u in order_u:
             scatter(t, u)
         if t < ROUNDS - 1:
             for u in order_u:
-                cur[0] = CFG["b0"] * u + CFG["ba"]
+                cur[0] = CFG["b0"] * u
                 first_fail(t + 1, u)
     add("s", [lambda: g.scalar.dma_start(T.yc[0:64, :], T.cf[0:64, 0:2048])], ["cf"], [], 0.1, "stc0", 16, 5.0)
     add("y", [lambda: g.sync.dma_start(T.yc[64:128, :], T.cf[64:128, 0:2048])], ["cf"], [], 0.1, "stc1", 16, 5.0)
@@ -634,4 +632,4 @@ def rank_program(g, core, T, topo):
         g.wait_ge(T.sem[s], total[s])
     for s in DMAS:
         g.wait_ge(T.sem[s], 16)
-    g.wait_ge(T.sem.sent, (4 * (ROUNDS - 1) + n_ranks - 1) * NENG)
+    g.wait_ge(T.sem.sent, (6 * (ROUNDS - 1) + n_ranks - 1) * NENG)

@@ -7,38 +7,42 @@ ROUNDS = 5
 TH = 36.5
 OFF = 2048.0
 NO = -8192.0
-CW = 2048 + 16
+CW = 2048 + 32
 NENG = 16
 TOP = float(2 ** 20)
-CFG = {"gv_a": 0, "gv_b": 0, "gv0": (48, 48), "gv4": 32,
+CFG = {"gv_a": 0, "gv_b": 0, "gv0": (32, 64), "gv4": 0,
        "ch_a": 2, "ch_b": 2,
-       "e_dp": "s", "e_wt": "s", "e_p4": "s", "e_sa": "s",
-       "vf": 0.04, "wake": 0.1, "gam": 1.5, "pe": 0.42,
-       "lr": 5.0, "lx": 6.0, "lc": 5.5,
-       "b0": 3.0, "bs": -2.0, "bc": -30.0, "look": 0.0, "gain": 0.05, "iters": 16}
+       "e_dp": "s", "e_wt": "s", "e_p4": "s", "e_sa": "s", "e_q2": "v", "e_th": "v", "e_wc": "v",
+       "cut": {"a0": (64, 48, 16), "b0": (80, 48)},
+       "seq": "",
+       "vf": 0.04, "wake": 0.12, "gam": 1.5, "pe": 0.42,
+       "lr": 5.0, "lx": 6.0, "lc": 5.5, "e2": 0,
+       "b0": 3.0, "bs": -2.0, "bc": -30.0, "look": 0.0, "gain": 0.05, "iters": 8}
 PLAN = []
 
 SCRATCH = {
     "xw": ("sbuf", [128, 4096], "bfloat16"), "cw": ("sbuf", [128, CW], "float32"), "cf": ("sbuf", [128, CW], "float32"),
     "ci": ("sbuf", [128, 2048], "int32"), "ri": ("sbuf", [128, 256], "int32"),
-    "pint": ("sbuf", [128, 4], "int32"), "pf": ("sbuf", [128, 16], "float32"),
-    "cy": ("sbuf", [128, 256], "bfloat16"), "posw": ("sbuf", [128, 256], "bfloat16"),
+    "pint": ("sbuf", [128, 4], "int32"), "pf": ("sbuf", [128, 20], "float32"),
+    "cy": ("sbuf", [128, 256], "bfloat16"), "posw": ("sbuf", [128, 384], "bfloat16"),
     "ca": ("sbuf", [128, 8, 32], "bfloat16"), "cb": ("sbuf", [128, 8, 32], "bfloat16"),
     "gs": ("sbuf", [128, 8, 16], "bfloat16"), "gm": ("sbuf", [128, 8, 16], "bfloat16"),
     "c15": ("sbuf", [128, 144], "bfloat16"), "pair": ("sbuf", [128, 8, 128], "bfloat16"), "wm": ("sbuf", [128, 16, 128], "bfloat16"),
     "wt": ("sbuf", [128, 16], "bfloat16"), "w16": ("sbuf", [128, 6, 16], "float32"), "lohi": ("sbuf", [128, 2, 16], "float32"),
-    "acc": ("sbuf", [128, 4], "float32"),
+    "acc": ("sbuf", [128, 4], "float32"), "mp": ("sbuf", [128, 128], "bfloat16"),
     "qi": ("sbuf", [128, 2, 16], "int32"), "qb": ("sbuf", [128, 4, 32], "float32"), "bk": ("sbuf", [128, 16], "float32"),
     "hs": ("sbuf", [128, 16], "float32"), "hi": ("sbuf", [128, 2, 16], "int32"), "ow": ("sbuf", [128, 16], "uint16"),
-    "h16": ("sbuf", [128, 16], "float16"), "ew": ("sbuf", [128, 256], "bfloat16"), "lw": ("sbuf", [128, 32], "uint16"),
+    "h16": ("sbuf", [128, 16], "float16"), "ew": ("sbuf", [128, 384], "bfloat16"), "lw": ("sbuf", [128, 16], "uint16"),
     "la": ("sbuf", [128, 10, 128], "uint16"), "lb": ("sbuf", [128, 10, 128], "uint16"),
-    "rq": ("sbuf", [128, 10, 272], "float16"), "rl": ("sbuf", [128, 10, 16, 16], "float16"),
+    "rq": ("sbuf", [128, 10, 128], "float16"), "rl": ("sbuf", [128, 10, 8, 16], "float16"),
+    "sq": ("sbuf", [128, 10, 144], "bfloat16"), "sl": ("sbuf", [128, 10, 8, 16], "bfloat16"),
+    "gsb": ("sbuf", [128, 8, 16], "bfloat16"), "gp": ("sbuf", [128, 8], "bfloat16"),
     "ns": ("sbuf", [128, 10, 64], "bfloat16"), "nl": ("sbuf", [128, 10, 8, 8], "bfloat16"),
     "PE0": ("psum", [128, 512], "float32"), "PE1": ("psum", [128, 512], "float32"),
 }
 for _n in ("ic", "gcl", "pd", "cm", "blk", "mask", "i4", "kc", "t0", "t1", "t2", "t3"):
     SCRATCH[_n] = ("sbuf", [128, 128], "float32")
-for _n in ("ib", "nib", "pk", "nk", "i8", "n8", "ib4", "ibk", "c8", "c2k", "mp", "g10", "g10k", "s15", "am"):
+for _n in ("ib", "nib", "pk", "nk", "n4", "ism", "nb4", "ib4", "ibk", "one", "half", "g10", "g10k", "s15", "pb"):
     SCRATCH[_n] = ("sbuf", [128, 128], "bfloat16")
 for _u in "01":
     for _n in ("WT", "Dn", "p4", "X4"):
@@ -53,7 +57,7 @@ for _u in "01":
         SCRATCH[_n + "h" + _u] = ("sbuf", [128, 1024], "bfloat16")
     SCRATCH["Dph" + _u] = ("sbuf", [128, 256], "bfloat16")
     SCRATCH["Wh" + _u] = ("sbuf", [128, 256], "float32")
-    SCRATCH["thh" + _u] = ("sbuf", [128, 64], "float32")
+    SCRATCH["thh" + _u] = ("sbuf", [128, 64], "bfloat16")
     SCRATCH["Wch" + _u] = ("sbuf", [128, 10], "bfloat16")
     SCRATCH["Tah" + _u] = ("sbuf", [128, 144], "float16")
     SCRATCH["PA" + _u] = ("psum", [128, 8, 64], "float32")
@@ -61,7 +65,7 @@ for _u in "01":
     SCRATCH["PM" + _u] = ("psum", [128, 512], "float32")
 
 DMAS = ["ldr", "ldx0", "ldx1", "ldc", "sty0", "sty1", "stc0", "stc1"]
-SEMAPHORES = ["qv", "qs", "qt", "qg", "sent"] + ["arq%d" % d for d in (1, 2, 3)] + ["ar%s%d" % (c, k) for c in "lrn" for k in range(8)] + DMAS
+SEMAPHORES = ["qv", "qs", "qt", "qg", "sent"] + ["arq%d" % d for d in (1, 2, 3)] + ["ar%s%d" % (c, k) for c in "lrns" for k in range(8)] + DMAS
 
 
 def rank_program(g, core, T, topo):
@@ -71,7 +75,7 @@ def rank_program(g, core, T, topo):
     n_ranks = len(T.cores)
     eng = {"v": g.vector, "s": g.scalar, "t": g.tensor, "g": g, "y": g.sync}
     ops, lastw, readers = [], {}, {}
-    cur = [0.0]
+    cur, tag, soft = [0.0], {}, set()
 
     def add(q, fns, reads, writes, cost, sem=None, val=0, lat=0.0, deps=()):
         k = len(ops)
@@ -198,15 +202,18 @@ def rank_program(g, core, T, topo):
     ts(B("mask"), ic, col(0), OP.is_equal, extra=["pf0"])
     ts(B("blk"), gcl, col(1), OP.is_equal, extra=["pf1"])
     tt(B("i4"), B("mask"), B("blk"), OP.mult)
-    for nm, w in (("ib", 1.0), ("nib", -1.0), ("pk", 1024.0), ("nk", -1024.0), ("i8", 0.125), ("n8", -0.125), ("ib4", 4096.0)):
+    for nm, w in (("ib", 1.0), ("nib", -1.0), ("pk", 1024.0), ("nk", -1024.0), ("n4", -988.0), ("ism", 1.0 / 4096), ("nb4", -4096.0), ("ib4", 4096.0)):
         act(B(nm), B("i4"), ID, 0.0, w)
     act(B("ibk"), B("i4"), ID, 0.0, col(12), extra=["pf12"])
     act(B("s15"), B("blk"), ID, 0.0, col(3), extra=["pf3"])
     act(B("gs"), B("blk"), ID)
-    fill("gs", T.gs[:, :, 1:3], 0.0)
     fill("gs", T.gs[:, :, 8], 0.0)
+    act(B("gsb"), B("blk"), ID)
+    fill("gsb", T.gsb[:, :, 1:3], 0.0)
+    act(("gsb", T.gsb[:, :, 0:5:4]), ("gs", T.gs[:, :, 0:2]), ID, 0.0, -1.0)
+    act(B("gp"), ("blk", T.blk[:, 0:128:16]), ID, 0.0, 2.0)
     act(B("gm"), B("blk"), ID, 0.0, -2.0)
-    for ap, v in ((T.ca[:], 0.0), (T.ca[:, :, 1:32:4], -3072.0), (T.ca[:, :, 2:32:4], -2048.0), (T.ca[:, :, 0], 2048.0)):
+    for ap, v in ((T.ca[:], 0.0), (T.ca[:, :, 1:32:4], -2048.0), (T.ca[:, :, 2:32:4], -2048.0), (T.ca[:, :, 0], 1536.0)):
         fill("ca", ap, v)
     for u in (0, 1):
         ts(B("Ta", u), ("cy0", T.cy[:, 0:144]), 0.0, OP.mult, c=0.5)
@@ -227,9 +234,9 @@ def rank_program(g, core, T, topo):
     ts(B("t2"), B("pd"), col(0), OP.is_equal, extra=["pf0"])
     ts(B("t3"), B("pd"), col(7), OP.is_equal, extra=["pf7"])
     tt(B("t2"), B("t2"), B("t3"), OP.add)
-    tt(B("t2"), B("mask"), B("t2"), OP.subtract)
+    tt(B("pb"), B("mask"), B("t2"), OP.subtract)
     for k in range(8):
-        act(("pair%d" % k, T.pair[:, k, :]), B("t2"), ID, 0.0, T.blk[:, 16 * k:16 * k + 1], extra=["blk"])
+        ts(("pair%d" % k, T.pair[:, k, :]), B("pb"), T.blk[:, 16 * k:16 * k + 1], OP.mult, c=0.5, extra=["blk"])
     ts(C(8), C(0), col(1), OP.add, 1.0, OP.add, extra=["pf1"])
     ts(C(9), C(8), 16.0, OP.is_ge, -16.0, OP.mult)
     tt(C(8), C(8), C(9), OP.add)
@@ -251,32 +258,30 @@ def rank_program(g, core, T, topo):
     ts(W(5), r16, col(10), OP.is_le, extra=["pf10"])
     tt(W(4), W(4), W(5), OP.mult)
     ts(B("wt"), W(4), -1.0, OP.add, T.w16[:, 2, 15:16], OP.mult, extra=["w162"])
-    fill("c8", T.c8[:], NO)
-    ts(("pad", T.rq[:, :, 256:272]), ("cy0", T.cy[:, 0:160]), 0.0, OP.mult, NO, OP.add, c=0.5)
-    for ap, v in ((T.cb[:], -1024.0), (T.cb[:, :, 1:32:4], 2048.0), (T.cb[:, :, 29], 3040.0), (T.cb[:, :, 0:31:30], -2048.0)):
+    fill("half", T.half[:], 0.5)
+    fill("pad", T.sq[:, :, 128:144], 0.5)
+    for ap, v in ((T.cb[:], -512.0), (T.cb[:, :, 1:32:4], 1024.0), (T.cb[:, :, 3:32:4], -1024.0), (T.cb[:, :, 29], 512.0), (T.cb[:, :, 0:31:30], -2048.0)):
         fill("cb", ap, v)
-    fill("c2k", T.c2k[:], OFF)
     fill("mp", T.mp[:], -1.0e9)
     fill("mp", T.mp[:, 0:128:16], OFF)
     fill("mp", T.mp[:, 15:128:16], OFF)
     for u in (0, 1):
-        fill("dlh%d" % u, T["dlh%d" % u][:], 0.0)
+        iota("dlh%d" % u, [[0, 128]], 0)
     fill("cw", T.cw[:, 2048:CW], 0.0)
     fill("cf_", T.cf[:, 2048:CW], 0.0)
     act(B("cy"), ("cy0", T.cy[:]), ID, 0.0, 8192.0)
     lastw["cy0"] = lastw["cy"]
     ops[lastw["cy"]]["need"].update(readers["cy0"][:-1])
-    ts(B("t0"), B("i4"), 2.0, OP.mult)
-    tt(B("am"), B("t0"), B("blk"), OP.subtract)
-    ts(("lo", T.lohi[:, 0, :]), ("mask", T.mask[:, 0:16]), -1.0, OP.mult)
-    ts(("hi_", T.lohi[:, 1, :]), ("mask", T.mask[:, 0:16]), -1.0, OP.mult, 1.0, OP.add)
+    iota("one", [[0, 128]], 1)
     for i in range(16):
-        ts(("wm%d" % i, T.wm[:, i, :]), B("am"), T.lohi[:, 0, i:i + 1], OP.max, T.lohi[:, 1, i:i + 1], OP.min, c=0.5, extra=["lo", "hi_"])
+        add("g", [lambda i=i: g.affine_select(T.wm[:, i, :], T.one[:], [[-16, 8], [0, 16]], OP.is_equal, 0.0, -i, 1)], ["one"], ["wm%d" % i], 0.41)
     ts(B("t1"), ic, col(0), OP.is_gt, 16384.0, OP.mult, extra=["pf0"])
     ts(B("t3"), B("mask"), -4096.0, OP.mult)
     tt(("posw", T.posw[:, 0:128]), B("t1"), B("t3"), OP.add)
     act(("posw", T.posw[:, 128:256]), ("posw", T.posw[:, 0:128]), ID)
+    fill("posw", T.posw[:, 256:384], 0.0)
     ts(C(11), C(0), OFF, OP.add)
+    ts(C(16), C(0), OFF + 16.0, OP.add)
     cur[0] = CFG["bc"]
     for k in range(4):
         ts(("cw%d" % k, T.cw[:, 512 * k:512 * k + 512]), ("ci", T.ci[:, 512 * k:512 * k + 512]), col(14), OP.add, extra=["pf14"])
@@ -292,7 +297,10 @@ def rank_program(g, core, T, topo):
         if t == ROUNDS - 1 and st == "b":
             ndve = CFG["gv4"]
         w = (128 - ndve) // nch
-        parts = [("s", w * ch, w * ch + w if ch < nch - 1 else 128 - ndve) for ch in range(nch)] + ([("v", 128 - ndve, 128)] if ndve else [])
+        cut = [w] * (nch - 1) + [128 - ndve - w * (nch - 1)]
+        if 0 < t + (st == "b") < ROUNDS:
+            cut = CFG["cut"].get(st + str(u), cut)
+        parts = [("s", sum(cut[:n]), sum(cut[:n + 1])) for n in range(len(cut))] + ([("v", sum(cut), 128)] if sum(cut) < 128 else [])
         kg, km, kn = [], [], []
         for n, (q, a, b) in enumerate(parts):
             key = "G%sh%d.%d" % (st, u, n)
@@ -300,7 +308,7 @@ def rank_program(g, core, T, topo):
             o, i = G[:, 16 * a:16 * b], win.indirect(T[lst][:, slot, a:b])
             more = ["xw_", "%s%d" % (lst, slot), "done%s%d.%d" % (st, u, t - 1)]
             if q == "s":
-                act((key, o), ("xw", i), ID, c=CFG["gam"], extra=more)
+                tag[(t, st, u, n)] = act((key, o), ("xw", i), ID, c=CFG["gam"], extra=more)
             else:
                 cp((key, o), ("xw", i), c=CFG["gam"], extra=more)
         for step, D, ks in ((2, N, kn), (1, M, km)):
@@ -318,9 +326,15 @@ def rank_program(g, core, T, topo):
         PA, PM, G, M, N = T["PA%d" % u], T["PM%d" % u], T["Gah%d" % u], T["Mah%d" % u], T["Nah%d" % u]
         kd, kr = "PA%d:D" % u, "rl%d" % k
         ky, Y = "PM%d:Y" % u, PM[:, 0:256]
-        mm([(Y, T.ib[:], T.cy[:])] + [(PM[:, j:256:4], T.ib[:], T.rl[:, k, 0:8, (14 if j else 15)::-2]) for j in range(4)], ["ib", "cy", kr], [ky])
+        mm([(Y, T.ib[:], T.cy[:])] + [(PM[:, j:256:4], T.ib4[:], T.rl[:, k, :, (14 if j else 15)::-2]) for j in range(4)], ["ib", "ib4", "cy", kr], [ky])
         kg, km, kn = gather(u, "a", t, "la")
         items = [(PA[:, :, 0:32], T.ib[:], T.ca[:])]
+        if t:
+            c0, c1 = T.sl[:, k, :, 15::-2], T.sl[:, k, :, 14:0:-2]
+            items += [(PA[:, :, 0:32:4], T.nk[:], c0), (PA[:, :, 1:32:4], T.pk[:], c0), (PA[:, :, 2:32:4], T.pk[:], c0),
+                      (PA[:, :, 4:32:4], T.pk[:], c1), (PA[:, :, 5:32:4], T.pk[:], c1), (PA[:, :, 6:32:4], T.nk[:], c1)]
+        mm(items, ["ib", "ca"] + (["sl%d" % k, "pk", "nk"] if t else []), [kd], sp=False)
+        items = []
         for p in range(16):
             z = 4 * (7 - p // 2)
             if p % 2:
@@ -328,11 +342,8 @@ def rank_program(g, core, T, topo):
             else:
                 n = 5 if p else 3
                 items.append((PA[:, :, z + 1:z + 1 + n], G[:, p:2048:16], T.gs[:, :, 3:3 + n]))
-        mm(items, ["ib", "ca", "gs"] + kg, [kd], sp=False)
+        mm(items, ["gs"] + kg, [kd], st=False, sp=False)
         if t:
-            c0, c1 = T.rl[:, k, 8:16, 15::-2], T.rl[:, k, 8:16, 14:0:-2]
-            mm([(PA[:, :, 0:32:4], T.i8[:], c0), (PA[:, :, 1:32:4], T.n8[:], c0), (PA[:, :, 2:32:4], T.n8[:], c0),
-                (PA[:, :, 4:32:4], T.n8[:], c1), (PA[:, :, 5:32:4], T.n8[:], c1), (PA[:, :, 6:32:4], T.i8[:], c1)], [kr, "i8", "n8"], [kd], st=False, sp=False)
             mm([(PA[:, :, 4 * (7 - i) + 1], N[:, i:1024:8], T.gm[:, :, 0]) for i in range(7)], kn + ["gm"], [kd], st=False, sp=False)
         items = []
         for p in range(15):
@@ -342,15 +353,15 @@ def rank_program(g, core, T, topo):
         if t:
             nl = T.nl[:, k, :, 7::-1]
             mm([(PA[:, :, j:32:4], w[:], nl) for j, w in enumerate((T.nk, T.pk, T.pk, T.nk))], ["nl%d" % k, "pk", "nk"], [kd], st=False)
-        lin(CFG["e_dp"], B("Dp", u), (kd, PA[:, :, 0:32]), -TH, float(2 ** 22))
+        tag[(t, "D", u, 0)] = lin(CFG["e_dp"], B("Dp", u), (kd, PA[:, :, 0:32]), -TH, float(2 ** 22))
         lastw["donea%d.%d" % (u, t)] = scan(B("W", u), B("Dp", u), (ky, Y), OP.max, OP.min)
 
     def moved(u, near, rp, out, kout, last):
         kf, F = "PM%d:F" % u, T["PM%d" % u][:, 384:448]
-        mm([(F, T.ib[:], rp[2]), (F, T.nib[:], rp[3])], [rp[0], "ib", "nib"], [kf])
+        mm([(F, T.ib4[:], rp[2]), (F, T.nb4[:], rp[3])], [rp[0], "ib4", "nb4"], [kf])
         tt(("dlh%d" % u, T["dlh%d" % u][:, 1:128:2]), (kf, F), near, OP.mult)
         mm([(out, T["dlh%d" % u][:], T.i4[:])], ["dlh%d" % u, "i4"], [kout], sp=False, c=4)
-        mm([(out, rp[1], T.ib[:])], ["ib", rp[0]], [kout], st=False, sp=last)
+        mm([(out, rp[1], T.ib4[:])], ["ib4", rp[0]], [kout], st=False, sp=last)
 
     def stage_a(t, u):
         k = 2 * t + u
@@ -358,7 +369,7 @@ def rank_program(g, core, T, topo):
         Wd, Wc, Ta, WT = T["Wh%d" % u], T["Wch%d" % u], T["Tah%d" % u], T["WTh%d" % u]
         end = ("Wh%d" % u, Wd[:, 31:256:32])
         wc = ("Wch%d" % u, Wc[:, 0:8])
-        cp(wc, end)
+        tag[(t, "C", u, 0)] = lin(CFG["e_wc"], wc, end, 0.0, 1.0)
         tt(("Tah%d" % u, Ta[:, 15:128:16]), end, wc, OP.subtract)
         kl, L = "PM%d:L" % u, PM[:, 448:456]
         mm([(L, Ta[:, 15 - i:143 - i], T.ib[:, i:128:16]) for i in range(16)], ["Tah%d" % u, "ib"], [kl])
@@ -369,16 +380,16 @@ def rank_program(g, core, T, topo):
         kt, TT_ = "PB%d:T" % u, PB[0:10, :, 48:64]
         mm([(TT_, Wc[:, 0:10], T.ib[:])], [wc[0], "ib"], [kt])
         wt = ("WTh%d" % u, WT[0:10, :])
-        lin(CFG["e_wt"], wt, (kt, TT_), 0.0, 1.0)
+        tag[(t, "W", u, 0)] = lin(CFG["e_wt"], wt, (kt, TT_), 0.0, 1.0)
         k1, P1 = "PB%d:U" % u, PB[:, :, 32:48]
         mm([(P1, T.g10[0:10, :], wt[1])], ["g10", wt[0]], [k1])
         j = 2 * (t % 2) + u
-        act(B("Dn", u), (k1, P1), RELU, 0.0, -1.0, acc=("acc%d" % j, T.acc[:, j:j + 1]))
+        tag[(t, "N", u, 0)] = act(B("Dn", u), (k1, P1), RELU, 0.0, -1.0, acc=("acc%d" % j, T.acc[:, j:j + 1]))
         kk, K = "PA%d:D" % u, PA[:, :, 32:48]
         if t:
-            moved(u, ("nl%d" % k, T.nl[:, k, :, :]), ("rl%d" % k, T.rl[:, k, 0:8, :], T.rl[:, k, 0:8, 0:16:2], T.rl[:, k, 0:8, 1:16:2]), K, kk, False)
+            moved(u, ("nl%d" % k, T.nl[:, k, :, :]), ("rl%d" % k, T.rl[:, k, :, :], T.rl[:, k, :, 0:16:2], T.rl[:, k, :, 1:16:2]), K, kk, False)
         else:
-            mm([(K, T.rl[:, k, 0:8, :], T.ib[:])], ["ib", "rl%d" % k], [kk], sp=False)
+            mm([(K, T.rl[:, k, :, :], T.ib4[:])], ["ib4", "rl%d" % k], [kk], sp=False)
         mm([(K, T.g10k[0:10, :], wt[1]), (K, T.ibk[:], T["Dnh%d" % u][:])], ["g10k", wt[0], "ibk", "Dnh%d" % u], [kk], st=False)
         h0, h1 = ("hi0%d" % u, T.hi[:, 0, c0:c1]), ("hi1%d" % u, T.hi[:, 1, c0:c1])
         tt(h0, hs, ("bk", T.bk[:, c0:c1]) if t else ("qb0", T.qb[:, 0, 16 + c0:16 + c1]), OP.add)
@@ -398,59 +409,65 @@ def rank_program(g, core, T, topo):
         R1, E = T["R1h%d" % u], T["Eh%d" % u]
         ks, Sc = "PM%d:H" % u, PM[:, 256:384]
         for b in (0, 1):
-            P, kp = T["PE%d" % b], "PE%d:E" % b
+            P, kp = T["PE%d" % (b * CFG["e2"])], "PE%d:E" % (b * CFG["e2"])
             for j in range(4):
                 mm([(P[:, 128 * j:128 * j + 128], T.pair[:, 4 * b + j, :], R1[:])], ["R1h%d" % u, "pair%d" % (4 * b + j)], [kp])
             ts(("Eh%d.%d" % (u, b), E[:, 512 * b:512 * b + 512]), (kp, P[:, 0:512]), 0.0, OP.is_equal)
         for j in range(8):
             mm([(PM[:, 256 + 16 * j:272 + 16 * j], E[:, 128 * j:128 * j + 128], T.wt[:])], ["Eh%d.%d" % (u, j // 4), "wt"], [ks])
-        q2 = ("q2%d" % k, T.rq[:, k, 128:256])
-        ts(q2, (ks, Sc), 0.0, OP.is_le, NO, OP.mult)
-        kh, H = "PM%d:H" % u, PM[:, 256:384]
-        mm([(H, R1[:], T.ib[:]), (H, T.ib[:], T.c8[:]), (H, T.nib[:], q2[1])], ["R1h%d" % u, "ib", "c8", "nib", q2[0]], [kh])
-        scan(("rp%d" % k, T.rq[:, k, 0:128]), q2, (kh, H), OP.add, OP.max)
+        q2 = ("q2%d" % k, T.sq[:, k, 0:128])
+        ts(q2, (ks, Sc), 0.0, OP.is_le, -0.5, OP.add)
         if t < ROUNDS - 1:
-            send(("rp%d" % k, T.rq[:, k, 0:256]), ("rl%d" % (k + 2), T.rl[:, k + 2, :, :]), "arr%d" % k, extra=[q2[0]])
+            send(q2, ("sl%d" % (k + 2), T.sl[:, k + 2, :, :]), "ars%d" % k)
+        kh, H = "PM%d:H" % u, PM[:, 256:384]
+        mm([(H, R1[:], T.ism[:]), (H, T.ib[:], T.half[:]), (H, T.nib[:], q2[1])], ["R1h%d" % u, "ib", "ism", "half", "nib", q2[0]], [kh])
+        rp = ("rp%d" % k, T.rq[:, k, :])
+        scan(rp, q2, (kh, H), OP.max, OP.min)
+        if t < ROUNDS - 1:
+            send(rp, ("rl%d" % (k + 2), T.rl[:, k + 2, :, :]), "arr%d" % k)
 
     def stage_b(t, u):
         k = 2 * t + u
         PA, PB, PM, G, M, N = T["PA%d" % u], T["PB%d" % u], T["PM%d" % u], T["Gbh%d" % u], T["Mbh%d" % u], T["Nbh%d" % u]
         kg, km, kn = gather(u, "b", t, "lb")
         kd, kq, kp = "PB%d:D" % u, "q2%d" % k, "rp%d" % k
-        items = [(PB[:, :, 0:32], T.ib[:], T.cb[:])]
+        c0, c1 = T.sq[:, k, 1:128:2], T.sq[:, k, 2:130:2]
+        mm([(PB[:, :, 0:32], T.ib[:], T.cb[:]), (PB[:, :, 1:32:4], T.n4[:], c0), (PB[:, :, 3:32:4], T.pk[:], c0), (PB[:, :, 1:32:4], T.n4[:], c1),
+            (PB[:, :, 3:32:4], T.nk[:], c1), (PB[:, :, 0:32:2], T.pk[:], T.sq[:, k, 0:128])], ["ib", "cb", kq, "pad", "pk", "nk", "n4"], [kd], sp=False)
+        items = []
         for p in range(15):
             z = 4 * (p // 2)
             if p % 2:
                 items.append((PB[:, :, z + 2:z + 5], G[:, p:2048:16], T.gs[:, :, 3:6]))
             else:
                 a, b = (4 if p == 0 else 0), (4 if p == 14 else 7)
-                items.append((PB[:, :, z - 3 + a:z - 3 + b], G[:, p:2048:16], T.gs[:, :, a:b]))
-        mm(items, ["ib", "cb", "gs"] + kg, [kd], sp=False)
-        mm([(PB[:, :, 4 * i + 1], N[:, i:1024:8], T.gm[:, :, 0]) for i in range(7)], kn + ["gm"], [kd], st=False, sp=False)
+                items.append((PB[:, :, z - 3 + a:z - 3 + b], G[:, p:2048:16], T.gsb[:, :, a:b]))
+        mm(items, ["gs", "gsb"] + kg, [kd], st=False, sp=False)
+        mm([(PB[:, :, 4 * i + 1], N[:, i:1024:8], T.gp[:]) for i in range(7)], kn + ["gp"], [kd], st=False, sp=False)
         items = []
         for p in range(14):
             z = 4 * (p // 2)
             items.append((PB[:, :, z + 4], M[:, p:2048:16], T.gm[:, :, 0]) if p % 2 else (PB[:, :, z + 2:z + 4], M[:, p:2048:16], T.gm[:, :, 0:2]))
-        mm(items, km + ["gm"], [kd], st=False, sp=False)
-        c0, c1 = T.rq[:, k, 129:256:2], T.rq[:, k, 130:258:2]
-        mm([(PB[:, :, 1:32:4], T.n8[:], c0), (PB[:, :, 3:32:4], T.n8[:], c0), (PB[:, :, 1:32:4], T.n8[:], c1), (PB[:, :, 3:32:4], T.i8[:], c1),
-            (PB[:, :, 0:32:2], T.n8[:], T.rq[:, k, 128:256])], [kq, "pad", "i8", "n8"], [kd], st=False)
+        mm(items, km + ["gm"], [kd], st=False)
         ns = ("ns%d" % k, T.ns[:, k, :])
-        ts(B("th", u), (kd, PB[:, :, 3:32:4]), TH, OP.is_lt, 4096.0 + TH, OP.mult)
-        tt(ns, (kd, PB[:, :, 1:32:4]), B("th", u), OP.is_lt)
+        if CFG["e_th"] == "s":
+            tag[(t, "T", u, 0)] = act(B("th", u), (kd, PB[:, :, 3:32:4]), RELU, -TH * 8192.0, 8192.0)
+        else:
+            ts(B("th", u), (kd, PB[:, :, 3:32:4]), TH, OP.is_gt, 4096.0, OP.mult)
+        tt(ns, (kd, PB[:, :, 1:32:4]), B("th", u), OP.is_ge)
         if t < ROUNDS - 1:
             send(ns, ("nl%d" % (k + 2), T.nl[:, k + 2, :, :]), "arn%d" % k)
         cur[0] += CFG["bs"]
         if CFG["e_p4"] == "s":
-            act(B("p4", u), (kd, PB[:, :, 0:32:2]), RELU, -TH * 8192.0, 8192.0)
+            tag[(t, "P", u, 0)] = act(B("p4", u), (kd, PB[:, :, 0:32:2]), RELU, -TH * 8192.0, 8192.0)
         else:
             ts(B("p4", u), (kd, PB[:, :, 0:32:2]), TH, OP.is_gt, 4096.0, OP.mult)
         scan(B("X4", u), B("mp"), B("p4", u), OP.max, OP.subtract, 0.5)
         kh, H = "PM%d:H" % u, PM[:, 256:384]
-        mm([(H, T.ib[:], T.rq[:, k, 0:128]), (H, T.ib[:], T.c2k[:]), (H, T.nib[:], T["X4h%d" % u][:])], [kp, "ib", "c2k", "nib", "X4h%d" % u], [kh])
+        mm([(H, T.ib4[:], T.rq[:, k, :]), (H, T.ib4[:], T.half[:]), (H, T.nib[:], T["X4h%d" % u][:])], [kp, "ib4", "half", "nib", "X4h%d" % u], [kh])
         scan(B("S", u), B("X4", u), (kh, H), OP.max, OP.min)
         mm([(H, T["Sh%d" % u][:], T.ib[:])], ["Sh%d" % u, "ib"], [kh])
-        lin(CFG["e_sa"], B("SA", u), (kh, H), OFF if t == ROUNDS - 1 else col(13), 1.0, extra=["pf13"])
+        tag[(t, "S", u, 0)] = lin(CFG["e_sa"], B("SA", u), (kh, H), OFF if t == ROUNDS - 1 else col(13), 1.0, extra=["pf13"])
         if t == ROUNDS - 1:
             cur[0] -= 3.0
             kk, K = "PA%d:D" % u, PA[:, :, 32:48]
@@ -465,31 +482,39 @@ def rank_program(g, core, T, topo):
         ts(B("bk"), ("qb%d" % d, T.qb[:, d, 16:32]), P, OP.add, extra=["PE1:E"])
 
     def winners():
-        P, kp = T.PE0, "PE0:E"
+        P, kp = T.PE1, "PE1:E"
         cp(B("h16"), ("hi10", T.hi[:, 1, :]), extra=["hi11"])
-        mm([(P[:, 0:256], T.ib[:], T.posw[:])] + [(P[:, 128 * u:128 * u + 128], T.s15[:], T["Dnh%d" % u][:]) for u in (0, 1)],
+        mm([(P[:, 0:384], T.ib[:], T.posw[:])] + [(P[:, 128 * u:128 * u + 128], T.s15[:], T["Dnh%d" % u][:]) for u in (0, 1)]
+           + [(P[:, 256 + 16 * m:272 + 16 * m], T.s15[:], T["Dnh%d" % (m // 4)][:, 32 * (m % 4):32 * (m % 4) + 16]) for m in range(8)],
            ["ib", "posw", "s15", "Dnh0", "Dnh1"], [kp], sp=False)
-        mm([(P[:, i:256:16], T.wm[:, i, :], T.h16[:]) for i in range(16)], ["h16"] + ["wm%d" % i for i in range(16)], [kp], st=False)
-        ts(B("ew"), (kp, P[:, 0:256]), 0.0, OP.is_equal)
-        Q = P[:, 256:272]
-        mm([(Q, T.ib[:], T.h16[:])] + [(Q, T.ib4[:], T.ew[:, i:256:16]) for i in range(16)], ["ib", "h16", "ib4", "ew"], [kp])
-        ts(("lw", T.lw[:, 0:32:2]), (kp, Q), col(11), OP.min, extra=["pf11"])
+        for a in range(0, 16, 4):
+            items = []
+            for i in range(a, a + 4):
+                items += [(P[:, i:256:16], T.nib[:], T.h16[:]), (P[:, i:256:16], T.wm[:, i, :], T.h16[:]),
+                          (P[:, 256 + i:384:16], T.nib[:], T.h16[:, 1:16:2]), (P[:, 256 + i:384:16], T.wm[:, i, :], T.h16[:, 0:16:2])]
+            mm(items, ["h16", "nib"] + ["wm%d" % i for i in range(a, a + 4)], [kp], st=False, sp=a == 12)
+        ts(B("ew"), (kp, P[:, 0:384]), 0.0, OP.is_equal)
+        Q = P[:, 384:400]
+        mm([(Q, T.ib[:], T.h16[:])] + [(Q, T.ib4[:], T.ew[:, i:256:16]) for i in range(16)], ["ib", "h16", "ib4", "ew"], [kp], sp=False)
+        mm([(P[:, 385:400:2], T.ib4[:], T.ew[:, 256 + i:384:16]) for i in range(16)], ["ib4", "ew"], [kp], st=False)
+        ts(("lw0", T.lw[:, 0:16:2]), (kp, P[:, 384:400:2]), col(11), OP.min, extra=["pf11"])
+        ts(("lw1", T.lw[:, 1:16:2]), (kp, P[:, 385:400:2]), col(16), OP.min, extra=["pf16"])
 
     def scatter(t, u):
         win, key = (T.cw, "cw") if t < ROUNDS - 1 else (T.cf, "cf")
-        for c in range(7, -1, -1):
-            j = 2 * (8 * u + c)
-            o = win[:, 0:CW].indirect(T.lw[:, j:j + 1])
-            add("v", [lambda o=o, c=c: g.vector.tensor_copy(out=o, in_=T["SAh%d" % u][:, 16 * c:16 * c + 16])],
-                ["SAh%d" % u, "lw"] + cws + ["cf_", "cf0", "cf1"], [key], 0.05 + 16 * 3.5 * 0.00083 * 1.1)
+        for c in range(3, -1, -1):
+            j = 8 * u + 2 * c
+            o = win[:, 0:CW].indirect(T.lw[:, j:j + 2])
+            add("v", [lambda o=o, c=c: g.vector.tensor_copy(out=o, in_=T["SAh%d" % u][:, 32 * c:32 * c + 32])],
+                ["SAh%d" % u, "lw0", "lw1"] + cws + ["cf_", "cf0", "cf1"], [key], 0.05 + 32 * 3.5 * 0.00083 * 1.1)
 
     order_u = (1, 0)
     for u in order_u:
         cur[0] = CFG["b0"] * u
         ts(B("R1", u), ("la%d" % u, T.la[:, u, :]), -OFF, OP.add, c=0.5)
         H = ("PM%d:H" % u, T["PM%d" % u][:, 256:384])
-        mm([(H[1], T["R1h%d" % u][:], T.ib[:])], ["R1h%d" % u, "ib"], [H[0]])
-        cp(("rl%d" % u, T.rl[:, u, 0:8, :]), H)
+        mm([(H[1], T["R1h%d" % u][:], T.ism[:])], ["R1h%d" % u, "ism"], [H[0]])
+        cp(("rl%d" % u, T.rl[:, u, :, :]), H)
         first_fail(0, u)
     cur[0] = 0.0
     for u in (0, 1):
@@ -525,6 +550,16 @@ def rank_program(g, core, T, topo):
     add("s", [lambda: g.scalar.dma_start(T.yc[0:64, :], T.cf[0:64, 0:2048])], ["cf"], [], 0.1, "stc0", 16, 5.0)
     add("y", [lambda: g.sync.dma_start(T.yc[64:128, :], T.cf[64:128, 0:2048])], ["cf"], [], 0.1, "stc1", 16, 5.0)
 
+    seq = []
+    for t in range(ROUNDS):
+        for w in CFG["seq"].split():
+            k = tag.get((t + (w[0] in "aDCWN") - (w[-1] == "-"), w[0], int(w[1]), int(w[2]) if w[0] in "ab" else 0))
+            if k is not None and ops[k]["q"] == "s" and (t < ROUNDS - 1 or w[-1] == "-") and (t or w[-1] != "-"):
+                seq.append(k)
+    for a, b in zip(seq, seq[1:]):
+        if a not in ops[b]["need"]:
+            ops[b]["need"].add(a)
+            soft.update([(a, b), (b, a)])
     n = len(ops)
     users = [[] for _ in range(n)]
     for k, o in enumerate(ops):
@@ -575,7 +610,7 @@ def rank_program(g, core, T, topo):
                     opened.discard(a)
             order.append(best)
             for j in after[best]:
-                if ops[j]["q"] == o["q"] == "t":
+                if ops[j]["q"] == o["q"] == "t" or (best, j) in soft:
                     lag = -o["lat"]
                 else:
                     lag = wake if fwd else wake - o["lat"] + ops[j]["lat"]
@@ -611,7 +646,7 @@ def rank_program(g, core, T, topo):
         want = {}
         for d in o["need"]:
             p = ops[d]
-            if p["sem"] == "none" or (p["q"] == q and q == "t"):
+            if (d, k) in soft or p["sem"] == "none" or (p["q"] == q and q == "t"):
                 continue
             want[p["sem"]] = max(want.get(p["sem"], 0), p["val"])
         for s in sorted(want):
@@ -632,4 +667,4 @@ def rank_program(g, core, T, topo):
         g.wait_ge(T.sem[s], total[s])
     for s in DMAS:
         g.wait_ge(T.sem[s], 16)
-    g.wait_ge(T.sem.sent, (6 * (ROUNDS - 1) + n_ranks - 1) * NENG)
+    g.wait_ge(T.sem.sent, (8 * (ROUNDS - 1) + n_ranks - 1) * NENG)

@@ -1,8 +1,11 @@
+import math
+from concourse.bass import DstId, RemoteDMATransfer
 from concourse.mybir import AluOpType, ActivationFunctionType
 
 OP = AluOpType
 ID = ActivationFunctionType.Identity
 RELU = ActivationFunctionType.Relu
+ABS = ActivationFunctionType.Abs
 ROUNDS = 5
 TH = 36.5
 OFF = 2048.0
@@ -10,14 +13,16 @@ NO = -8192.0
 CW = 2048 + 32
 NENG = 16
 TOP = float(2 ** 20)
-CFG = {"gv_a": 0, "gv_b": 0, "gv0": (32, 64), "gv4": 0,
+CFG = {"gv_a": 0, "gv_b": 0, "gv0": (16, 48), "gv4": (0, 0),
        "ch_a": 2, "ch_b": 2,
-       "e_dp": "s", "e_wt": "s", "e_p4": "s", "e_sa": "s", "e_q2": "v", "e_th": "v", "e_wc": "v",
-       "cut": {"a0": (64, 48, 16), "b0": (80, 48)},
+       "e_dp": "s", "e_wt": "s", "e_p4": "vs", "e_sa": "ss", "e_cf": "ssss", "wmi": 0, "lf": 2.5, "fold": 0, "ciw": 0, "f": 1.1, "ls": 1.7, "e_eq": ["vvvvv"] * 5, "e_th": "v", "e_wc": "v",
+       "cut": {"a0": (64, 48), "b0": (80, 48)},
        "seq": "",
-       "vf": 0.04, "wake": 0.12, "gam": 1.5, "pe": 0.42,
-       "lr": 5.0, "lx": 6.0, "lc": 5.5, "e2": 0,
-       "b0": 3.0, "bs": -2.0, "bc": -30.0, "look": 0.0, "gain": 0.05, "iters": 8}
+       "vf": 0.04, "wake": 0.2, "gam": 1.5, "pe": 0.42,
+       "lr": 5.0, "lx": 4.5, "lc": 2.5, "e2": 0,
+       "b0": 3.0, "bs": -2.0, "bc": -30.0, "look": 0.1, "gain": 0.02, "iters": 3,
+       "starts": [(1, 0.1), (0, 0.1), (0.5, 0.0), (1.5, 0.2), (1, 0.3)], "steps": 400, "tabu": 60,
+       "sets": [(0.92, 1.03, 0.2), (1.27, 1.33, 0.2), (1.1, 0.75, 0.25)]}
 PLAN = []
 
 SCRATCH = {
@@ -27,7 +32,7 @@ SCRATCH = {
     "cy": ("sbuf", [128, 256], "bfloat16"), "posw": ("sbuf", [128, 384], "bfloat16"),
     "ca": ("sbuf", [128, 8, 32], "bfloat16"), "cb": ("sbuf", [128, 8, 32], "bfloat16"),
     "gs": ("sbuf", [128, 8, 16], "bfloat16"), "gm": ("sbuf", [128, 8, 16], "bfloat16"),
-    "c15": ("sbuf", [128, 144], "bfloat16"), "pair": ("sbuf", [128, 8, 128], "bfloat16"), "wm": ("sbuf", [128, 16, 128], "bfloat16"),
+    "c15": ("sbuf", [128, 144], "bfloat16"), "pair": ("sbuf", [128, 8, 128], "bfloat16"), "wm": ("sbuf", [128, 16, 128], "bfloat16"), "wn": ("sbuf", [128, 16, 128], "bfloat16"),
     "wt": ("sbuf", [128, 16], "bfloat16"), "w16": ("sbuf", [128, 6, 16], "float32"), "lohi": ("sbuf", [128, 2, 16], "float32"),
     "acc": ("sbuf", [128, 4], "float32"), "mp": ("sbuf", [128, 128], "bfloat16"),
     "qi": ("sbuf", [128, 2, 16], "int32"), "qb": ("sbuf", [128, 4, 32], "float32"), "bk": ("sbuf", [128, 16], "float32"),
@@ -37,7 +42,8 @@ SCRATCH = {
     "rq": ("sbuf", [128, 10, 128], "float16"), "rl": ("sbuf", [128, 10, 8, 16], "float16"),
     "sq": ("sbuf", [128, 10, 144], "bfloat16"), "sl": ("sbuf", [128, 10, 8, 16], "bfloat16"),
     "gsb": ("sbuf", [128, 8, 16], "bfloat16"), "gp": ("sbuf", [128, 8], "bfloat16"),
-    "ns": ("sbuf", [128, 10, 64], "bfloat16"), "nl": ("sbuf", [128, 10, 8, 8], "bfloat16"),
+    "ns": ("sbuf", [128, 10, 64], "float16"), "tl": ("sbuf", [128, 10, 64], "float16"), "nl": ("sbuf", [128, 10, 8, 8], "float16"),
+    "nf": ("sbuf", [128, 8, 2048], "bfloat16"),
     "PE0": ("psum", [128, 512], "float32"), "PE1": ("psum", [128, 512], "float32"),
 }
 for _n in ("ic", "gcl", "pd", "cm", "blk", "mask", "i4", "kc", "t0", "t1", "t2", "t3"):
@@ -65,7 +71,7 @@ for _u in "01":
     SCRATCH["PM" + _u] = ("psum", [128, 512], "float32")
 
 DMAS = ["ldr", "ldx0", "ldx1", "ldc", "sty0", "sty1", "stc0", "stc1"]
-SEMAPHORES = ["qv", "qs", "qt", "qg", "sent"] + ["arq%d" % d for d in (1, 2, 3)] + ["ar%s%d" % (c, k) for c in "lrns" for k in range(8)] + DMAS
+SEMAPHORES = ["qv", "qs", "qt", "qg", "sent"] + ["arq%d" % d for d in (1, 2, 3)] + ["%s%d" % (c, k) for c in ("arl", "arr", "arn", "ars", "arf", "sf") for k in range(8)] + DMAS
 
 
 def rank_program(g, core, T, topo):
@@ -94,11 +100,12 @@ def rank_program(g, core, T, topo):
             lastw[a] = k
             readers[a] = []
         need.discard(k)
-        ops.append({"q": q, "f": fns, "need": need, "cost": cost, "sem": sem, "val": val, "lat": lat, "b": cur[0], "bank": bank, "st": False, "sp": False})
+        ops.append({"q": q, "f": fns, "need": need, "cost": cost, "sem": sem, "val": val, "lat": lat, "b": cur[0], "bank": bank, "st": False, "sp": False,
+                    "fix": 0.0 if q == "t" else CFG["vf"], "ind": any(a in reads for a in ("xw", "ow0", "ow1", "lw0"))})
         return k
 
     def dur(n, c=1.0):
-        return CFG["vf"] + max(64.0, n * c) * 0.00083 * 1.1
+        return CFG["vf"] + max(64.0, n * c) * 0.00083 * CFG["f"]
 
     def size(ap):
         r = 1
@@ -139,12 +146,20 @@ def rank_program(g, core, T, topo):
             return act(out, a, ID, add_ * mul if mul != 1.0 else add_, mul, extra=extra)
         return ts(out, a, add_, OP.add, mul, OP.mult, extra=extra)
 
+    def zero(e, out, a):
+        if e == "s":
+            act(out, a, ABS)
+            return act(out, out, RELU, 1.0, -1.0)
+        return ts(out, a, 0.0, OP.is_equal)
+
     def mm(items, reads, writes, st=True, sp=True, c=1):
         fns, cost = [], 0.0
         for n, (o, l, r) in enumerate(items):
             a, b = st and n == 0, sp and n == len(items) - 1
             fns.append(lambda o=o, l=l, r=r, a=a, b=b: g.tensor.matmul(out=o, lhsT=l, rhs=r, start=a, stop=b))
             cost += max(64, size(r)) * 0.001 * CFG["pe"] * 1.1 * c
+        if not st and not sp:
+            reads, writes = list(reads) + list(writes), []
         k = add("t", fns, reads, writes, cost, lat=0.05)
         ops[k]["st"], ops[k]["sp"] = st, sp
         return k
@@ -156,14 +171,18 @@ def rank_program(g, core, T, topo):
         nm = name if u is None else "%sh%d" % (name, u)
         return (nm, T[nm][:])
 
-    def send(src, dst, sem, d=1, extra=()):
+    def route(d):
         to = T.cores[(rank + d) % n_ranks]
         rid, pid, _s = topo.addr(to)
         m = 0
         for e in topo.engines(core, to)[:NENG]:
             m |= 1 << e
+        return rid, pid, m
+
+    def send(src, dst, sem, d=1, extra=()):
+        rid, pid, m = route(d)
         sd = add("g", [lambda: g.remote_dma(out_ap=dst[1], in_ap=src[1], remote_sem=T.sem[sem], local_sem=T.sem.sent, pid=pid, routing_id=rid, dma_engine_mask=m)],
-                 [src[0]] + list(extra), [], 0.3, "none", 0, 1.7)
+                 [src[0]] + list(extra), [], 0.3, "none", 0, CFG["ls"])
         add(None, [], [], [dst[0]], 0.0, sem, NENG, 0.0, deps=[sd])
 
     g.sync.dma_start(T.ri[:], T.r0[:]).then_inc(T.sem.ldr, 16)
@@ -172,7 +191,11 @@ def rank_program(g, core, T, topo):
     add(None, [], [], ["ri"], 0.0, "ldr", 16, CFG["lr"])
     add(None, [], [], ["xw"], 0.0, "ldx0", 16, CFG["lx"])
     add(None, [], [], ["xw_"], 0.0, "ldx1", 16, CFG["lx"])
-    add("y", [lambda: g.sync.dma_start(T.ci[:], T.c0[:])], [], ["ci"], 0.1, "ldc", 16, CFG["lc"], deps=(1, 2))
+    if CFG["ciw"]:
+        add("y", [lambda: g.sync.dma_start(T.ci[:], T.c0[:])], [], ["ci"], 0.1, "ldc", 16, CFG["lc"], deps=(1, 2))
+    else:
+        g.sync.dma_start(T.ci[:], T.c0[:]).then_inc(T.sem.ldc, 16)
+        add(None, [], [], ["ci"], 0.0, "ldc", 16, CFG["lx"] + CFG["lc"])
 
     add("g", [lambda: g.iota(T.pint[:, 0:1], [[0, 1]], 0, 1)], [], ["pint"], 0.2)
     iota("ic", [[0, 8], [1, 16]], 0)
@@ -275,6 +298,9 @@ def rank_program(g, core, T, topo):
     iota("one", [[0, 128]], 1)
     for i in range(16):
         add("g", [lambda i=i: g.affine_select(T.wm[:, i, :], T.one[:], [[-16, 8], [0, 16]], OP.is_equal, 0.0, -i, 1)], ["one"], ["wm%d" % i], 0.41)
+        if CFG["wmi"]:
+            add("g", [lambda i=i: g.affine_select(T.wn[:, i, :], T.nib[:], [[-16, 8], [0, 16]], OP.not_equal, 1.0, -i, 1)], ["nib"], ["wn%d" % i], 0.41)
+            add("g", [lambda i=i: g.affine_select(T.wn[:, i, i:128:16], T.wn[:, i, i:128:16], [[-16, 8]], OP.not_equal, 0.0, -i, 1)], ["wn%d" % i], ["wn%d" % i], 0.2)
     ts(B("t1"), ic, col(0), OP.is_gt, 16384.0, OP.mult, extra=["pf0"])
     ts(B("t3"), B("mask"), -4096.0, OP.mult)
     tt(("posw", T.posw[:, 0:128]), B("t1"), B("t3"), OP.add)
@@ -295,7 +321,7 @@ def rank_program(g, core, T, topo):
         if t == 0 and st == "a":
             ndve = CFG["gv0"][u]
         if t == ROUNDS - 1 and st == "b":
-            ndve = CFG["gv4"]
+            ndve = CFG["gv4"][u]
         w = (128 - ndve) // nch
         cut = [w] * (nch - 1) + [128 - ndve - w * (nch - 1)]
         if 0 < t + (st == "b") < ROUNDS:
@@ -314,6 +340,16 @@ def rank_program(g, core, T, topo):
         for step, D, ks in ((2, N, kn), (1, M, km)):
             if step == 2 and t == 0 and st == "a":
                 continue
+            if step == 2 and st == "b" and t < CFG["fold"]:
+                rid, pid, m = route(1)
+                sd = []
+                for n, (q, a, b) in enumerate(parts):
+                    tr = RemoteDMATransfer(dst_ids=[DstId(rid=rid, pnc=pid)], dma_engine_mask=m, remote_sem=T.sem["arf%d" % slot],
+                                           srcs=[G[:, 16 * a:16 * b - 2], G[:, 16 * a + 2:16 * b]], dsts=[T.nf[:, slot, 16 * a:16 * b - 2]], alu_op=3)
+                    sd.append(add("g", [lambda tr=tr: g.remote_dma_fused([tr], local_sem=T.sem["sf%d" % slot])], [kg[n]], [], 0.3, "none", 0, CFG["lf"]))
+                add(None, [], [], ["nf%d" % (slot + 2)], 0.0, "arf%d" % slot, NENG * len(sd), 0.0, deps=sd)
+                add(None, [], [], ["doneb%d.%d" % (u, t)], 0.0, "sf%d" % slot, NENG * len(sd), 0.0, deps=sd)
+                continue
             for n, (q, a, b) in enumerate(parts):
                 key = "%d%sh%d.%d" % (step, st, u, n)
                 ks.append(key)
@@ -328,12 +364,11 @@ def rank_program(g, core, T, topo):
         ky, Y = "PM%d:Y" % u, PM[:, 0:256]
         mm([(Y, T.ib[:], T.cy[:])] + [(PM[:, j:256:4], T.ib4[:], T.rl[:, k, :, (14 if j else 15)::-2]) for j in range(4)], ["ib", "ib4", "cy", kr], [ky])
         kg, km, kn = gather(u, "a", t, "la")
-        items = [(PA[:, :, 0:32], T.ib[:], T.ca[:])]
+        mm([(PA[:, :, 0:32], T.ib[:], T.ca[:])], ["ib", "ca"], [kd], sp=False)
         if t:
             c0, c1 = T.sl[:, k, :, 15::-2], T.sl[:, k, :, 14:0:-2]
-            items += [(PA[:, :, 0:32:4], T.nk[:], c0), (PA[:, :, 1:32:4], T.pk[:], c0), (PA[:, :, 2:32:4], T.pk[:], c0),
-                      (PA[:, :, 4:32:4], T.pk[:], c1), (PA[:, :, 5:32:4], T.pk[:], c1), (PA[:, :, 6:32:4], T.nk[:], c1)]
-        mm(items, ["ib", "ca"] + (["sl%d" % k, "pk", "nk"] if t else []), [kd], sp=False)
+            mm([(PA[:, :, 0:32:4], T.nk[:], c0), (PA[:, :, 1:32:4], T.pk[:], c0), (PA[:, :, 2:32:4], T.pk[:], c0), (PA[:, :, 4:32:4], T.pk[:], c1),
+                (PA[:, :, 5:32:4], T.pk[:], c1), (PA[:, :, 6:32:4], T.nk[:], c1)], ["sl%d" % k, "pk", "nk"], [kd], st=False, sp=False)
         items = []
         for p in range(16):
             z = 4 * (7 - p // 2)
@@ -349,7 +384,13 @@ def rank_program(g, core, T, topo):
         for p in range(15):
             z = 4 * (7 - p // 2)
             items.append((PA[:, :, z], M[:, p:2048:16], T.gm[:, :, 0]) if p % 2 else (PA[:, :, z + 2:z + 4], M[:, p:2048:16], T.gm[:, :, 0:2]))
-        mm(items, km + ["gm"], [kd], st=False, sp=t == 0)
+        mm(items[:8], km + ["gm"], [kd], st=False, sp=False)
+        mm(items[8:], km + ["gm"], [kd], st=False, sp=t == 0)
+        if 0 < t <= CFG["fold"]:
+            kf, F = "PM%d:F" % u, PM[:, 384:448]
+            mm([(F, T.ib[:], T.posw[:, 256:320])] + [(PM[:, 384 + i:448:8], T.nf[:, k - 2, 2 * i:2048:16], T.gp[:]) for i in range(7)],
+               ["ib", "posw", "gp", "nf%d" % k], [kf])
+            tt(("nl%d" % k, T.nl[:, k, :, :]), (kf, F), ("tl%d" % k, T.tl[:, k, :]), OP.is_ge)
         if t:
             nl = T.nl[:, k, :, 7::-1]
             mm([(PA[:, :, j:32:4], w[:], nl) for j, w in enumerate((T.nk, T.pk, T.pk, T.nk))], ["nl%d" % k, "pk", "nk"], [kd], st=False)
@@ -412,7 +453,7 @@ def rank_program(g, core, T, topo):
             P, kp = T["PE%d" % (b * CFG["e2"])], "PE%d:E" % (b * CFG["e2"])
             for j in range(4):
                 mm([(P[:, 128 * j:128 * j + 128], T.pair[:, 4 * b + j, :], R1[:])], ["R1h%d" % u, "pair%d" % (4 * b + j)], [kp])
-            ts(("Eh%d.%d" % (u, b), E[:, 512 * b:512 * b + 512]), (kp, P[:, 0:512]), 0.0, OP.is_equal)
+            zero(CFG["e_eq"][t][2 * u + b], ("Eh%d.%d" % (u, b), E[:, 512 * b:512 * b + 512]), (kp, P[:, 0:512]))
         for j in range(8):
             mm([(PM[:, 256 + 16 * j:272 + 16 * j], E[:, 128 * j:128 * j + 128], T.wt[:])], ["Eh%d.%d" % (u, j // 4), "wt"], [ks])
         q2 = ("q2%d" % k, T.sq[:, k, 0:128])
@@ -432,8 +473,9 @@ def rank_program(g, core, T, topo):
         kg, km, kn = gather(u, "b", t, "lb")
         kd, kq, kp = "PB%d:D" % u, "q2%d" % k, "rp%d" % k
         c0, c1 = T.sq[:, k, 1:128:2], T.sq[:, k, 2:130:2]
-        mm([(PB[:, :, 0:32], T.ib[:], T.cb[:]), (PB[:, :, 1:32:4], T.n4[:], c0), (PB[:, :, 3:32:4], T.pk[:], c0), (PB[:, :, 1:32:4], T.n4[:], c1),
-            (PB[:, :, 3:32:4], T.nk[:], c1), (PB[:, :, 0:32:2], T.pk[:], T.sq[:, k, 0:128])], ["ib", "cb", kq, "pad", "pk", "nk", "n4"], [kd], sp=False)
+        mm([(PB[:, :, 0:32], T.ib[:], T.cb[:])], ["ib", "cb", "lb%d" % k], [kd], sp=False)
+        mm([(PB[:, :, 1:32:4], T.n4[:], c0), (PB[:, :, 3:32:4], T.pk[:], c0), (PB[:, :, 1:32:4], T.n4[:], c1),
+            (PB[:, :, 3:32:4], T.nk[:], c1), (PB[:, :, 0:32:2], T.pk[:], T.sq[:, k, 0:128])], [kq, "pad", "pk", "nk", "n4"], [kd], st=False, sp=False)
         items = []
         for p in range(15):
             z = 4 * (p // 2)
@@ -443,22 +485,28 @@ def rank_program(g, core, T, topo):
                 a, b = (4 if p == 0 else 0), (4 if p == 14 else 7)
                 items.append((PB[:, :, z - 3 + a:z - 3 + b], G[:, p:2048:16], T.gsb[:, :, a:b]))
         mm(items, ["gs", "gsb"] + kg, [kd], st=False, sp=False)
-        mm([(PB[:, :, 4 * i + 1], N[:, i:1024:8], T.gp[:]) for i in range(7)], kn + ["gp"], [kd], st=False, sp=False)
+        if t >= CFG["fold"]:
+            mm([(PB[:, :, 4 * i + 1], N[:, i:1024:8], T.gp[:]) for i in range(7)], kn + ["gp"], [kd], st=False, sp=False)
         items = []
         for p in range(14):
             z = 4 * (p // 2)
             items.append((PB[:, :, z + 4], M[:, p:2048:16], T.gm[:, :, 0]) if p % 2 else (PB[:, :, z + 2:z + 4], M[:, p:2048:16], T.gm[:, :, 0:2]))
-        mm(items, km + ["gm"], [kd], st=False)
+        mm(items[:-1], km + ["gm"], [kd], st=False, sp=False)
+        mm(items[-1:], km + ["gm"], [kd], st=False)
         ns = ("ns%d" % k, T.ns[:, k, :])
         if CFG["e_th"] == "s":
             tag[(t, "T", u, 0)] = act(B("th", u), (kd, PB[:, :, 3:32:4]), RELU, -TH * 8192.0, 8192.0)
         else:
             ts(B("th", u), (kd, PB[:, :, 3:32:4]), TH, OP.is_gt, 4096.0, OP.mult)
-        tt(ns, (kd, PB[:, :, 1:32:4]), B("th", u), OP.is_ge)
-        if t < ROUNDS - 1:
-            send(ns, ("nl%d" % (k + 2), T.nl[:, k + 2, :, :]), "arn%d" % k)
+        if t < CFG["fold"]:
+            tt(ns, B("th", u), (kd, PB[:, :, 1:32:4]), OP.subtract, c=1)
+            send(ns, ("tl%d" % (k + 2), T.tl[:, k + 2, :]), "arn%d" % k)
+        else:
+            tt(ns, (kd, PB[:, :, 1:32:4]), B("th", u), OP.is_ge)
+            if t < ROUNDS - 1:
+                send(ns, ("nl%d" % (k + 2), T.nl[:, k + 2, :, :]), "arn%d" % k)
         cur[0] += CFG["bs"]
-        if CFG["e_p4"] == "s":
+        if CFG["e_p4"][u] == "s":
             tag[(t, "P", u, 0)] = act(B("p4", u), (kd, PB[:, :, 0:32:2]), RELU, -TH * 8192.0, 8192.0)
         else:
             ts(B("p4", u), (kd, PB[:, :, 0:32:2]), TH, OP.is_gt, 4096.0, OP.mult)
@@ -467,7 +515,7 @@ def rank_program(g, core, T, topo):
         mm([(H, T.ib4[:], T.rq[:, k, :]), (H, T.ib4[:], T.half[:]), (H, T.nib[:], T["X4h%d" % u][:])], [kp, "ib4", "half", "nib", "X4h%d" % u], [kh])
         scan(B("S", u), B("X4", u), (kh, H), OP.max, OP.min)
         mm([(H, T["Sh%d" % u][:], T.ib[:])], ["Sh%d" % u, "ib"], [kh])
-        tag[(t, "S", u, 0)] = lin(CFG["e_sa"], B("SA", u), (kh, H), OFF if t == ROUNDS - 1 else col(13), 1.0, extra=["pf13"])
+        tag[(t, "S", u, 0)] = lin(CFG["e_sa"][u], B("SA", u), (kh, H), OFF if t == ROUNDS - 1 else col(13), 1.0, extra=["pf13"])
         if t == ROUNDS - 1:
             cur[0] -= 3.0
             kk, K = "PA%d:D" % u, PA[:, :, 32:48]
@@ -481,7 +529,7 @@ def rank_program(g, core, T, topo):
         d = (t + 1) % n_ranks
         ts(B("bk"), ("qb%d" % d, T.qb[:, d, 16:32]), P, OP.add, extra=["PE1:E"])
 
-    def winners():
+    def winners(t):
         P, kp = T.PE1, "PE1:E"
         cp(B("h16"), ("hi10", T.hi[:, 1, :]), extra=["hi11"])
         mm([(P[:, 0:384], T.ib[:], T.posw[:])] + [(P[:, 128 * u:128 * u + 128], T.s15[:], T["Dnh%d" % u][:]) for u in (0, 1)]
@@ -490,10 +538,10 @@ def rank_program(g, core, T, topo):
         for a in range(0, 16, 4):
             items = []
             for i in range(a, a + 4):
-                items += [(P[:, i:256:16], T.nib[:], T.h16[:]), (P[:, i:256:16], T.wm[:, i, :], T.h16[:]),
-                          (P[:, 256 + i:384:16], T.nib[:], T.h16[:, 1:16:2]), (P[:, 256 + i:384:16], T.wm[:, i, :], T.h16[:, 0:16:2])]
-            mm(items, ["h16", "nib"] + ["wm%d" % i for i in range(a, a + 4)], [kp], st=False, sp=a == 12)
-        ts(B("ew"), (kp, P[:, 0:384]), 0.0, OP.is_equal)
+                items += [(P[:, i:256:16], T.wn[:, i, :], T.h16[:])] if CFG["wmi"] else [(P[:, i:256:16], T.nib[:], T.h16[:]), (P[:, i:256:16], T.wm[:, i, :], T.h16[:])]
+                items += [(P[:, 256 + i:384:16], T.nib[:], T.h16[:, 1:16:2]), (P[:, 256 + i:384:16], T.wm[:, i, :], T.h16[:, 0:16:2])]
+            mm(items, ["h16", "nib"] + ["w%s%d" % (c, i) for c in "mn" for i in range(a, a + 4)], [kp], st=False, sp=a == 12)
+        zero(CFG["e_eq"][t][4], B("ew"), (kp, P[:, 0:384]))
         Q = P[:, 384:400]
         mm([(Q, T.ib[:], T.h16[:])] + [(Q, T.ib4[:], T.ew[:, i:256:16]) for i in range(16)], ["ib", "h16", "ib4", "ew"], [kp], sp=False)
         mm([(P[:, 385:400:2], T.ib4[:], T.ew[:, 256 + i:384:16]) for i in range(16)], ["ib4", "ew"], [kp], st=False)
@@ -506,7 +554,7 @@ def rank_program(g, core, T, topo):
             j = 8 * u + 2 * c
             o = win[:, 0:CW].indirect(T.lw[:, j:j + 2])
             add("v", [lambda o=o, c=c: g.vector.tensor_copy(out=o, in_=T["SAh%d" % u][:, 32 * c:32 * c + 32])],
-                ["SAh%d" % u, "lw0", "lw1"] + cws + ["cf_", "cf0", "cf1"], [key], 0.05 + 32 * 3.5 * 0.00083 * 1.1)
+                ["SAh%d" % u, "lw0", "lw1"] + cws + ["cf_", "cf0", "cf1", "cf2", "cf3"], [key], 0.05 + 32 * 3.5 * 0.00083 * 1.1)
 
     order_u = (1, 0)
     for u in order_u:
@@ -529,12 +577,12 @@ def rank_program(g, core, T, topo):
         if t == ROUNDS - 1:
             cur[0] = CFG["bc"]
             for k in range(4):
-                act(("cf%d" % (k // 2), T.cf[:, 512 * k:512 * k + 512]), ("cw", T.cw[:, 512 * k:512 * k + 512]), ID, col(15), extra=["pf15"])
+                lin(CFG["e_cf"][k], ("cf%d" % k, T.cf[:, 512 * k:512 * k + 512]), ("cw", T.cw[:, 512 * k:512 * k + 512]), col(15), 1.0, extra=["pf15"])
         for u in order_u:
             cur[0] = CFG["b0"] * u
             stage_a(t, u)
         cur[0] = CFG["bs"]
-        winners()
+        winners(t)
         if t < ROUNDS - 1:
             count(t)
         for u in order_u:
@@ -620,18 +668,146 @@ def rank_program(g, core, T, topo):
                     pool.append(j)
         return max(begin[k] + ops[k]["cost"] + (ops[k]["lat"] if fwd else 0.0) for k in range(n)), order, begin, more
 
+    def polish(order, steps):
+        sets = []
+        for f, gam, wk in CFG["sets"]:
+            cost = [o["cost"] if o["q"] not in ("v", "s", "t") else (o["cost"] - o["fix"]) * f * (gam if o["ind"] else 1.0) + o["fix"] for o in ops]
+            sets.append((cost, [c + o["lat"] + wk for c, o in zip(cost, ops)], wk))
+        qs = [o["q"] for o in ops]
+        pre = [[(d, qs[d] == qs[k] == "t", qs[k] is None) for d in ops[k]["need"]] for k in range(n)]
+        lines = {}
+        for k in order:
+            for a in ([qs[k]] if qs[k] else []) + ops[k]["bank"]:
+                lines.setdefault(a, []).append(k)
+        qp, qn, bp, bn = [-1] * n, [-1] * n, [{} for _ in range(n)], [{} for _ in range(n)]
+
+        def link(a):
+            line = lines[a]
+            if a in eng:
+                for x, y in zip([-1] + line, line + [-1]):
+                    if x >= 0:
+                        qn[x] = y
+                    if y >= 0:
+                        qp[y] = x
+                return True
+            seen, on = {}, False
+            for k in line:
+                if ops[k]["st"] and on:
+                    return False
+                on = (on or ops[k]["st"]) and not ops[k]["sp"]
+                bn[k][a] = []
+            for k in line:
+                bp[k][a] = [j for qq, j in seen.items() if qq != qs[k]]
+                for j in bp[k][a]:
+                    bn[j][a].append(k)
+                seen[qs[k]] = k
+            return True
+        for a in lines:
+            link(a)
+
+        def sequence():
+            left = [len(pre[k]) + (qp[k] >= 0) + sum(len(v) for v in bp[k].values()) for k in range(n)]
+            out = [k for k in range(n) if not left[k]]
+            for k in out:
+                for j in users[k] + ([qn[k]] if qn[k] >= 0 else []) + [x for v in bn[k].values() for x in v]:
+                    left[j] -= 1
+                    if not left[j]:
+                        out.append(j)
+            return out
+
+        def head_of(k, head, cost, far, wk, skip):
+            h = 0.0
+            for d, same, none in pre[k]:
+                h = max(h, head[d] + (cost[d] if same else far[d] - wk if none else far[d]))
+            for v in bp[k].values():
+                for d in v:
+                    if d != skip:
+                        h = max(h, head[d] + far[d])
+            return h
+
+        def tail_of(k, tail, cost, far, wk, skip):
+            h = far[k] - wk
+            for j in users[k]:
+                h = max(h, tail[j] + (cost[k] if qs[j] == qs[k] == "t" else far[k] - wk if qs[j] is None else far[k]))
+            for v in bn[k].values():
+                for j in v:
+                    if j != skip:
+                        h = max(h, tail[j] + far[k])
+            return h
+        best, tabu = None, {}
+        for step in range(steps):
+            tp = sequence()
+            got = []
+            for cost, far, wk in sets:
+                head, tail = [0.0] * n, [0.0] * n
+                for k in tp:
+                    h = head_of(k, head, cost, far, wk, -1)
+                    head[k] = max(h, head[qp[k]] + cost[qp[k]]) if qp[k] >= 0 else h
+                for k in reversed(tp):
+                    h = tail_of(k, tail, cost, far, wk, -1)
+                    tail[k] = max(h, tail[qn[k]] + cost[k]) if qn[k] >= 0 else h
+                got.append((head, tail, max(tail)))
+            if not step:
+                base = [e[2] for e in got]
+            score = sum(e[2] / b for e, b in zip(got, base))
+            if best is None or score < best[0] - 1e-9:
+                best = (score, tp, [[j for v in bp[k].values() for j in v] for k in range(n)], [e[2] for e in got])
+            moves = set()
+            for (cost, far, wk), (head, tail, end) in zip(sets, got):
+                for b in range(n):
+                    if head[b] + tail[b] > end - 1e-6:
+                        a = qp[b]
+                        if a >= 0 and abs(head[a] + cost[a] - head[b]) < 1e-6 and a not in ops[b]["need"]:
+                            moves.add((a, b, qs[a]))
+                        for bank, v in bp[b].items():
+                            for a in v:
+                                if abs(head[a] + far[a] - head[b]) < 1e-6 and a not in ops[b]["need"]:
+                                    moves.add((a, b, bank))
+            rated = []
+            for a, b, line in moves:
+                s = 0.0
+                for (cost, far, wk), (head, tail, end), b0 in zip(sets, got, base):
+                    hb, ha = head_of(b, head, cost, far, wk, a), head_of(a, head, cost, far, wk, -1)
+                    tb, ta = tail_of(b, tail, cost, far, wk, -1), tail_of(a, tail, cost, far, wk, b)
+                    x, y, z, w = (qp[a], -1, qn[b], -1) if line in eng else (qp[b], qp[a], qn[a], qn[b])
+                    gap = cost[b] if line in eng else far[b]
+                    hb = max(hb, head[x] + cost[x] if x >= 0 else 0.0)
+                    ha = max(ha, head[y] + cost[y] if y >= 0 else 0.0, hb + gap)
+                    ta = max(ta, tail[z] + cost[a] if z >= 0 else 0.0)
+                    tb = max(tb, tail[w] + cost[b] if w >= 0 else 0.0, ta + gap)
+                    e = max(hb + tb, ha + ta)
+                    s += (e if min(head[a] + tail[a], head[b] + tail[b]) > end - 1e-6 else max(e, end)) / b0
+                rated.append((s + (10.0 if tabu.get((b, a), -1) > step else 0.0), a, b, line))
+            for s, a, b, line in sorted(rated):
+                both = [line] + ([x for x in ops[a]["bank"] if x in ops[b]["bank"]] if line in eng else [])
+                at = [(lines[x].index(a), lines[x].index(b)) for x in both]
+                if any(j != i + 1 for i, j in at):
+                    continue
+                for x, (i, j) in zip(both, at):
+                    lines[x][i], lines[x][j] = b, a
+                if all([link(x) for x in both]) and len(sequence()) == n:
+                    tabu[(a, b)] = step + CFG["tabu"]
+                    break
+                for x, (i, j) in zip(both, at):
+                    lines[x][i], lines[x][j] = a, b
+                    link(x)
+        return best
+
     if not PLAN:
         needs = [o["need"] for o in ops]
         way = [0.0] * n
         for k in range(n - 1, -1, -1):
             way[k] = ops[k]["cost"] + ops[k]["lat"] + wake + max([way[j] for j in users[k]] or [0.0])
-        urge = [-w - o["b"] for w, o in zip(way, ops)]
-        for it in range(CFG["iters"]):
-            got = plan(needs, users, urge, True)
-            if not PLAN or got[0] < PLAN[0][0]:
-                PLAN[:] = [got]
-            back = plan(users, needs, [-(b + o["cost"]) for b, o in zip(got[2], ops)], False)
-            urge = [-(b + o["cost"]) for b, o in zip(back[2], ops)]
+        found = []
+        for lead, CFG["look"] in CFG["starts"]:
+            urge = [-w - o["b"] * lead for w, o in zip(way, ops)]
+            for it in range(CFG["iters"]):
+                got = plan(needs, users, urge, True)
+                found.append((sum(math.log(e) for e in polish(got[1], 1)[3]), got[1]))
+                back = plan(users, needs, [-(b + o["cost"]) for b, o in zip(got[2], ops)], False)
+                urge = [-(b + o["cost"]) for b, o in zip(back[2], ops)]
+        got = polish(min(found)[1], CFG["steps"])
+        PLAN.append((got[3][0], got[1], None, got[2]))
     CFG["ms"], order, _b, more = PLAN[0]
     for o, m in zip(ops, more):
         o["need"].update(m)
@@ -648,11 +824,16 @@ def rank_program(g, core, T, topo):
             p = ops[d]
             if (d, k) in soft or p["sem"] == "none" or (p["q"] == q and q == "t"):
                 continue
-            want[p["sem"]] = max(want.get(p["sem"], 0), p["val"])
+            if p["val"] > want.get(p["sem"], (0, 0))[0]:
+                want[p["sem"]] = (p["val"], d)
         for s in sorted(want):
-            if known[q].get(s, 0) < want[s]:
-                known[q][s] = want[s]
-                eng[q].wait_ge(T.sem[s], want[s])
+            v, d = want[s]
+            if known[q].get(s, 0) < v and not any(ops[e].get("saw", {}).get(s, 0) >= v for s2, (v2, e) in want.items() if s2 != s):
+                eng[q].wait_ge(T.sem[s], v)
+        for s, (v, d) in want.items():
+            for s2, v2 in list(ops[d].get("saw", {}).items()) + [(s, v)]:
+                known[q][s2] = max(known[q].get(s2, 0), v2)
+        o["saw"] = dict(known[q])
         fresh = o["sem"] is None
         for f in o["f"]:
             ins = f()

@@ -1,57 +1,61 @@
-import math
 from concourse.bass import DstId, RemoteDMATransfer
 from concourse.mybir import AluOpType, ActivationFunctionType
 
 OP = AluOpType
 ID = ActivationFunctionType.Identity
 RELU = ActivationFunctionType.Relu
-ABS = ActivationFunctionType.Abs
+SIGN = ActivationFunctionType.Sign
 ROUNDS = 5
 TH = 36.5
 OFF = 2048.0
-NO = -8192.0
 CW = 2048 + 32
 NENG = 16
-TOP = float(2 ** 20)
-CFG = {"gv_a": 0, "gv_b": 0, "gv0": (16, 48), "gv4": (0, 0),
-       "ch_a": 2, "ch_b": 2,
-       "e_dp": "s", "e_wt": "s", "e_p4": "vs", "e_sa": "ss", "e_cf": "ssss", "wmi": 0, "lf": 2.5, "fold": 0, "ciw": 0, "f": 1.1, "ls": 1.7, "e_eq": ["vvvvv"] * 5, "e_th": "v", "e_wc": "v",
-       "cut": {"a0": (64, 48), "b0": (80, 48)},
-       "seq": "",
-       "vf": 0.04, "wake": 0.2, "gam": 1.5, "pe": 0.42,
-       "lr": 5.0, "lx": 4.5, "lc": 2.5, "e2": 0,
-       "b0": 3.0, "bs": -2.0, "bc": -30.0, "look": 0.1, "gain": 0.02, "iters": 3,
-       "starts": [(1, 0.1), (0, 0.1), (0.5, 0.0), (1.5, 0.2), (1, 0.3)], "steps": 400, "tabu": 60,
-       "sets": [(0.92, 1.03, 0.2), (1.27, 1.33, 0.2), (1.1, 0.75, 0.25)]}
-PLAN = []
+M0, M1, M2 = 1.5 * 2 ** 24, 1.5 * 2 ** 23, 1.5 * 2 ** 34
+CFG = {"cut": {"a1": (48, 48, 32), "a0": (48, 48, 32), "b1": (56, 48), "b0": (48, 48, 32)},
+       "cut0": {"a1": (40, 40), "a0": (56, 56)}, "cut4": {"b1": (56, 48), "b0": (64, 64)},
+       "fold": "", "lf": 0.03, "l1": 5.5, "whole": (),
+       "e_dp": "sv", "e_wt": "vs", "e_hd": "vs", "e_hr": "vs", "e_th": "vv", "e_wm": "v" * 8 + "s" * 8,
+       "fill_g": ("cb", "gsb", "half"), "fill_v": ("ca", "hd", "qd_", "gs", "mp", "posw1", "pad", "cw", "cf_", "dlh0", "dlh1"),
+       "chunk": 6, "look": 0.1, "gain": 0.03,
+       "vf": 0.015, "wake": 0.25, "gam": 1.5, "pe": 0.41, "f": 1.05, "ls": 2.1, "lr": 3.0, "lx": 4.8, "lc": 2.6}
+ORDER = {
+    "first": "Gah1.0+ Gah1.1+ Gah0.1+ Gah0.0+ cw0 hd3.1+ hd0.1+ hd6.1+ cw2 WTh1+ cw1 cw3 sgh1+ Dph0+ hr1+ "
+             "rl1 rl0+ qd_4+ qd0+ Gah1.2+ 1ah1.0+ 1ah1.2+ Gah0.2+ 1ah1.1+ Dph1+ 1ah0.1+ Wh1+ 1ah0.2+ 1ah0.0+ hb1+ Tah1+ ow1+ Zh1+ Wh0+ lb1+ hd6.0+ hd0.0+ hd3.0+",
+    "round": "Gbh1.1 Gbh1.0 sgh0 Gah1.0+ Gbh0.2 Gbh0.0 Gbh0.1 Gah1.2+ Gah1.1+ Gah0.0+ SAh1 Gah0.1+ Gah0.2+ hd0.1+ hd6.1+ hd3.1+ SAh0 WTh1+ sgh1+ Dph0+ hr1+ "
+             "R1h1 hb0 Gbh1.2 Tah0 WTh0 Eh1.0 Eh1.1 ow0 1bh1.2 hr0 2bh1.1 Zh0 q21 2bh1.0 lb0 1bh1.0 R1h0 1bh1.1 2bh1.2 ew 1ah1.0+ Eh0.0 Eh0.1 thh1 p4h1 "
+             "1bh0.2 ns1 rp1 lw0 2bh0.0 Xh1 q20 2ah1.0+ 1bh0.1 1bh0.0 bk 2bh0.1 2bh0.2 Sh1 2ah1.2+ 1ah1.2+ 1ah1.1+ thh0 p4h0 2ah1.1+ ns0 rp0 Xh0 "
+             "c0 1ah0.0+ c1 Dph1+ Sh0 c2 Wh1+ 1ah0.1+ c3 1ah0.2+ hb1+ c4 2ah0.1+ Tah1+ 2ah0.0+ c5 2ah0.2+ dlh1+ c6 ow1+ c7 Zh1+ Wh0+ lb1+ dlh0+ hd3.0+ hd6.0+ hd0.0+",
+    "last": "cf3 cf2 Gbh1.0 sgh0 Gbh1.1 Gbh0.0 Gbh0.1 cf0 cf1 SAh1 SAh0 Yh1 Yh0 "
+            "R1h1 Gbh1.2 hb0 WTh0 Tah0 Eh1.0 Eh1.1 ow0 2bh1.0 hr0 Zh0 2bh1.2 q21 lb0 1bh1.2 R1h0 1bh1.1 1bh1.0 2bh1.1 Eh0.0 ew Eh0.1 rp1 p4h1 "
+            "1bh0.0 q20 1bh0.1 Xh1 2bh0.1 2bh0.0 Sh1 thh1 rp0 lw0 p4h0 thh0 ns1 Xh0 c0 dlh1+ c1 Sh0 ns0 c2 dlh0+ c3 c4 c5 c6 c7"}
 
 SCRATCH = {
     "xw": ("sbuf", [128, 4096], "bfloat16"), "cw": ("sbuf", [128, CW], "float32"), "cf": ("sbuf", [128, CW], "float32"),
     "ci": ("sbuf", [128, 2048], "int32"), "ri": ("sbuf", [128, 256], "int32"),
-    "pint": ("sbuf", [128, 4], "int32"), "pf": ("sbuf", [128, 20], "float32"),
-    "cy": ("sbuf", [128, 256], "bfloat16"), "posw": ("sbuf", [128, 384], "bfloat16"),
+    "pint": ("sbuf", [128, 4], "int32"), "pf": ("sbuf", [128, 16], "float32"),
+    "cy": ("sbuf", [128, 256], "bfloat16"), "posw": ("sbuf", [128, 8, 4, 16], "bfloat16"),
     "ca": ("sbuf", [128, 8, 32], "bfloat16"), "cb": ("sbuf", [128, 8, 32], "bfloat16"),
     "gs": ("sbuf", [128, 8, 16], "bfloat16"), "gm": ("sbuf", [128, 8, 16], "bfloat16"),
-    "c15": ("sbuf", [128, 144], "bfloat16"), "pair": ("sbuf", [128, 8, 128], "bfloat16"), "wm": ("sbuf", [128, 16, 128], "bfloat16"), "wn": ("sbuf", [128, 16, 128], "bfloat16"),
-    "wt": ("sbuf", [128, 16], "bfloat16"), "w16": ("sbuf", [128, 6, 16], "float32"), "lohi": ("sbuf", [128, 2, 16], "float32"),
-    "acc": ("sbuf", [128, 4], "float32"), "mp": ("sbuf", [128, 128], "bfloat16"),
-    "qi": ("sbuf", [128, 2, 16], "int32"), "qb": ("sbuf", [128, 4, 32], "float32"), "bk": ("sbuf", [128, 16], "float32"),
-    "hs": ("sbuf", [128, 16], "float32"), "hi": ("sbuf", [128, 2, 16], "int32"), "ow": ("sbuf", [128, 16], "uint16"),
-    "h16": ("sbuf", [128, 16], "float16"), "ew": ("sbuf", [128, 384], "bfloat16"), "lw": ("sbuf", [128, 16], "uint16"),
+    "gsb": ("sbuf", [128, 8, 16], "bfloat16"), "gp": ("sbuf", [128, 8], "bfloat16"),
+    "pair": ("sbuf", [128, 8, 128], "bfloat16"), "wm": ("sbuf", [128, 16, 8, 16], "bfloat16"),
+    "wt": ("sbuf", [128, 16], "bfloat16"), "w16": ("sbuf", [128, 6, 16], "float32"),
+    "acc": ("sbuf", [128, 4], "float32"), "dump": ("sbuf", [128, 16], "float32"),
+    "qd": ("sbuf", [128, 4, 192], "float32"), "hd": ("sbuf", [128, 176], "float32"), "hb": ("sbuf", [128, 176], "float32"),
+    "ow": ("sbuf", [128, 16], "uint16"), "hr": ("sbuf", [128, 8, 16], "float16"),
+    "ew": ("sbuf", [128, 8, 3, 16], "bfloat16"), "lw": ("sbuf", [128, 16], "uint16"),
     "la": ("sbuf", [128, 10, 128], "uint16"), "lb": ("sbuf", [128, 10, 128], "uint16"),
     "rq": ("sbuf", [128, 10, 128], "float16"), "rl": ("sbuf", [128, 10, 8, 16], "float16"),
     "sq": ("sbuf", [128, 10, 144], "bfloat16"), "sl": ("sbuf", [128, 10, 8, 16], "bfloat16"),
-    "gsb": ("sbuf", [128, 8, 16], "bfloat16"), "gp": ("sbuf", [128, 8], "bfloat16"),
-    "ns": ("sbuf", [128, 10, 64], "float16"), "tl": ("sbuf", [128, 10, 64], "float16"), "nl": ("sbuf", [128, 10, 8, 8], "float16"),
-    "nf": ("sbuf", [128, 8, 2048], "bfloat16"),
-    "PE0": ("psum", [128, 512], "float32"), "PE1": ("psum", [128, 512], "float32"),
+    "ns": ("sbuf", [128, 10, 64], "float16"), "nl": ("sbuf", [128, 10, 8, 8], "float16"),
+    "tl": ("sbuf", [128, 10, 64], "float16"), "nf": ("sbuf", [128, 8, 2048], "bfloat16"), "zero": ("sbuf", [128, 64], "bfloat16"),
+    "PE0": ("psum", [128, 8, 64], "float32"), "PE1": ("psum", [128, 8, 4, 16], "float32"),
 }
-for _n in ("ic", "gcl", "pd", "cm", "blk", "mask", "i4", "kc", "t0", "t1", "t2", "t3"):
+for _n in ("ic", "gcl", "pd", "mask", "i4", "kc", "t1", "t2", "t3"):
     SCRATCH[_n] = ("sbuf", [128, 128], "float32")
-for _n in ("ib", "nib", "pk", "nk", "n4", "ism", "nb4", "ib4", "ibk", "one", "half", "g10", "g10k", "s15", "pb"):
+for _n in ("blk", "ib", "nib", "pk", "nk", "n4", "ps", "ib4", "nb4", "ibk", "nbk", "one", "half", "s15", "pb", "gsp", "mp"):
     SCRATCH[_n] = ("sbuf", [128, 128], "bfloat16")
 for _u in "01":
-    for _n in ("WT", "Dn", "p4", "X4"):
+    for _n in ("X", "p4", "sg", "WT"):
         SCRATCH[_n + "h" + _u] = ("sbuf", [128, 128], "bfloat16")
     for _n in ("R1", "S"):
         SCRATCH[_n + "h" + _u] = ("sbuf", [128, 128], "float16")
@@ -64,7 +68,6 @@ for _u in "01":
     SCRATCH["Dph" + _u] = ("sbuf", [128, 256], "bfloat16")
     SCRATCH["Wh" + _u] = ("sbuf", [128, 256], "float32")
     SCRATCH["thh" + _u] = ("sbuf", [128, 64], "bfloat16")
-    SCRATCH["Wch" + _u] = ("sbuf", [128, 10], "bfloat16")
     SCRATCH["Tah" + _u] = ("sbuf", [128, 144], "float16")
     SCRATCH["PA" + _u] = ("psum", [128, 8, 64], "float32")
     SCRATCH["PB" + _u] = ("psum", [128, 8, 64], "float32")
@@ -80,8 +83,7 @@ def rank_program(g, core, T, topo):
         return
     n_ranks = len(T.cores)
     eng = {"v": g.vector, "s": g.scalar, "t": g.tensor, "g": g, "y": g.sync}
-    ops, lastw, readers = [], {}, {}
-    cur, tag, soft = [0.0], {}, set()
+    ops, lastw, readers, tag, now, sent = [], {}, {}, {}, [-1], []
 
     def add(q, fns, reads, writes, cost, sem=None, val=0, lat=0.0, deps=()):
         k = len(ops)
@@ -100,8 +102,14 @@ def rank_program(g, core, T, topo):
             lastw[a] = k
             readers[a] = []
         need.discard(k)
-        ops.append({"q": q, "f": fns, "need": need, "cost": cost, "sem": sem, "val": val, "lat": lat, "b": cur[0], "bank": bank, "st": False, "sp": False,
-                    "fix": 0.0 if q == "t" else CFG["vf"], "ind": any(a in reads for a in ("xw", "ow0", "ow1", "lw0"))})
+        if q in ("v", "s") and writes:
+            nm = writes[0][:2] + str(int(writes[0][2:]) % 2) if writes[0][:2] in ("lb", "q2", "rp", "ns", "nl") else writes[0]
+            if nm in ("cw", "cf"):
+                nm = "c%d" % sum((now[0], "c%d" % j) in tag for j in range(8))
+            tag[(now[0], nm)] = k
+        ind = any(a in reads for a in ("xw", "ow0", "ow1", "lw0"))
+        ops.append({"q": q, "f": fns, "need": need, "cost": cost + (0.05 if ind else 0.0), "sem": sem, "val": val, "lat": lat, "bank": bank,
+                    "st": False, "sp": False, "ind": ind})
         return k
 
     def dur(n, c=1.0):
@@ -129,43 +137,48 @@ def rank_program(g, core, T, topo):
     def cp(out, a, c=1.0, extra=()):
         return add("v", [lambda: g.vector.tensor_copy(out=out[1], in_=a[1])], [a[0]] + list(extra), [out[0]], dur(size(out[1]), c))
 
-    def scan(out, a, b, op0, op1, c=1.0, extra=()):
-        return add("v", [lambda: g.vector.tensor_tensor_scan(out=out[1], data0=a[1], data1=b[1], initial=0.0, op0=op0, op1=op1)],
+    def scan(out, a, b, op0, op1, c=1.0, extra=(), first=0.0):
+        return add("v", [lambda: g.vector.tensor_tensor_scan(out=out[1], data0=a[1], data1=b[1], initial=first, op0=op0, op1=op1)],
                    [a[0], b[0]] + list(extra), [out[0]], dur(size(out[1]), c))
 
     def act(out, a, func, bias=0.0, scale=1.0, c=1.0, extra=(), acc=None):
         kw = {"accum_out": acc[1]} if acc else {}
         return add("s", [lambda: g.scalar.activation(out=out[1], in_=a[1], func=func, bias=bias, scale=scale, **kw)],
-                   [a[0]] + list(extra), [out[0]] + ([acc[0]] if acc else []), dur(size(out[1]), c) + 0.01)
+                   [a[0]] + list(extra), [out[0]] + ([acc[0]] if acc else []), dur(size(out[1]), c) + (0.02 if acc else 0.0))
+
+    def select(key, out, a, pat, op, v, base, step):
+        return add("g", [lambda: g.affine_select(out, a[1], pat, op, v, base, step)], [a[0]], [key], (0.17 + 0.00166 * size(out)) * CFG["f"])
+
+    def iota(name, pat, base):
+        add("g", [lambda: g.iota(T[name][:], pat, base, 0, allow_small_or_imprecise_dtypes=True)], [], [name], (0.13 + size(T[name][:]) * 0.00166) * CFG["f"])
 
     def fill(key, ap, v):
-        return act((key, ap), ("cy0", T.cy[:, 0:size(ap)]), ID, v, 0.0)
+        n = size(ap)
+        if key in CFG["fill_v"]:
+            return add("v", [lambda: g.vector.memset(ap, v)], [], [key], dur(n, 0.5 if key in ("ca", "cb", "mp", "half", "posw1", "pad") else 1.0))
+        if key in CFG["fill_g"]:
+            return select(key, ap, ("cy", T.cy[:, 0:n]), [[0, n]], OP.is_gt, v, 0, 0)
+        return act((key, ap), ("cy", T.cy[:, 0:n]), ID, v, 0.0)
 
-    def lin(e, out, a, add_, mul, extra=()):
+    def lin(e, out, a, mul, add_, extra=()):
         if e == "s":
-            return act(out, a, ID, add_ * mul if mul != 1.0 else add_, mul, extra=extra)
-        return ts(out, a, add_, OP.add, mul, OP.mult, extra=extra)
-
-    def zero(e, out, a):
-        if e == "s":
-            act(out, a, ABS)
-            return act(out, out, RELU, 1.0, -1.0)
-        return ts(out, a, 0.0, OP.is_equal)
+            return act(out, a, ID, add_, mul, extra=extra)
+        return ts(out, a, mul, OP.mult, add_, OP.add, extra=extra)
 
     def mm(items, reads, writes, st=True, sp=True, c=1):
         fns, cost = [], 0.0
+        if not st and not sp and len(items) > CFG["chunk"]:
+            mm(items[CFG["chunk"]:], reads, writes, st, sp, c)
+            items = items[:CFG["chunk"]]
         for n, (o, l, r) in enumerate(items):
             a, b = st and n == 0, sp and n == len(items) - 1
             fns.append(lambda o=o, l=l, r=r, a=a, b=b: g.tensor.matmul(out=o, lhsT=l, rhs=r, start=a, stop=b))
-            cost += max(64, size(r)) * 0.001 * CFG["pe"] * 1.1 * c
+            cost += max(min(64, size(l)), size(r)) * 0.001 * CFG["pe"] * CFG["f"] * c
         if not st and not sp:
             reads, writes = list(reads) + list(writes), []
         k = add("t", fns, reads, writes, cost, lat=0.05)
         ops[k]["st"], ops[k]["sp"] = st, sp
         return k
-
-    def iota(name, pat, base, key=None):
-        add("g", [lambda: g.iota(T[name][:], pat, base, 0, allow_small_or_imprecise_dtypes=True)], [], [key or name], 0.13 + size(T[name][:]) * 0.002)
 
     def B(name, u=None):
         nm = name if u is None else "%sh%d" % (name, u)
@@ -182,26 +195,25 @@ def rank_program(g, core, T, topo):
     def send(src, dst, sem, d=1, extra=()):
         rid, pid, m = route(d)
         sd = add("g", [lambda: g.remote_dma(out_ap=dst[1], in_ap=src[1], remote_sem=T.sem[sem], local_sem=T.sem.sent, pid=pid, routing_id=rid, dma_engine_mask=m)],
-                 [src[0]] + list(extra), [], 0.3, "none", 0, CFG["ls"])
+                 [src[0]] + list(extra), [], CFG["l1"] if sem == "arq1" else 0.3, "none", 0, CFG["ls"], deps=[o for o in sent if sem != "arq1"])
+        if sem == "arq1":
+            sent.append(sd)
         add(None, [], [], [dst[0]], 0.0, sem, NENG, 0.0, deps=[sd])
 
     g.sync.dma_start(T.ri[:], T.r0[:]).then_inc(T.sem.ldr, 16)
     g.scalar.dma_start(T.xw[0:64, :], T.x[0:64, :]).then_inc(T.sem.ldx0, 16)
     g.sync.dma_start(T.xw[64:128, :], T.x[64:128, :]).then_inc(T.sem.ldx1, 16)
+    g.sync.dma_start(T.ci[:], T.c0[:]).then_inc(T.sem.ldc, 16)
     add(None, [], [], ["ri"], 0.0, "ldr", 16, CFG["lr"])
     add(None, [], [], ["xw"], 0.0, "ldx0", 16, CFG["lx"])
     add(None, [], [], ["xw_"], 0.0, "ldx1", 16, CFG["lx"])
-    if CFG["ciw"]:
-        add("y", [lambda: g.sync.dma_start(T.ci[:], T.c0[:])], [], ["ci"], 0.1, "ldc", 16, CFG["lc"], deps=(1, 2))
-    else:
-        g.sync.dma_start(T.ci[:], T.c0[:]).then_inc(T.sem.ldc, 16)
-        add(None, [], [], ["ci"], 0.0, "ldc", 16, CFG["lx"] + CFG["lc"])
+    add(None, [], [], ["ci"], 0.0, "ldc", 16, CFG["lx"] + CFG["lc"])
 
-    add("g", [lambda: g.iota(T.pint[:, 0:1], [[0, 1]], 0, 1)], [], ["pint"], 0.2)
+    add("g", [lambda: g.iota(T.pint[:, 0:1], [[0, 1]], 0, 1)], [], ["pint"], 0.14)
+    iota("cy", [[0, 8], [16, 8], [2, 4]], 2)
     iota("ic", [[0, 8], [1, 16]], 0)
     iota("gcl", [[1, 8], [0, 16]], 0)
-    iota("cy", [[0, 8], [1, 32]], 128, "cy0")
-    iota("cm", [[0, 8], [-4, 8], [-1, 2]], 31)
+    iota("one", [[0, 128]], 1)
     iota("pd", [[1, 8], [1, 16]], 1)
     for u in (0, 1):
         cp(("la%d" % u, T.la[:, u, :]), ("ri", T.ri[:, 128 * u:128 * u + 128]))
@@ -215,20 +227,23 @@ def rank_program(g, core, T, topo):
     ts(("pi2", T.pint[:, 2:3]), ("pint", T.pint[:, 0:1]), 4, OP.arith_shift_right)
     cp(C(0), ("pi1", T.pint[:, 1:2]))
     cp(C(1), ("pi2", T.pint[:, 2:3]))
-    cp(C(2), ("pint", T.pint[:, 0:1]))
-    ts(C(3), C(0), 15.0, OP.is_equal)
-    ts(C(12), C(3), -1.0, OP.mult, 1.0, OP.add)
-    ts(C(13), C(3), 4096.0, OP.mult)
-    ts(C(14), C(13), -OFF, OP.add)
-    ts(C(15), C(14), -1.0, OP.mult)
     ic, gcl = B("ic"), B("gcl")
     ts(B("mask"), ic, col(0), OP.is_equal, extra=["pf0"])
     ts(B("blk"), gcl, col(1), OP.is_equal, extra=["pf1"])
-    tt(B("i4"), B("mask"), B("blk"), OP.mult)
-    for nm, w in (("ib", 1.0), ("nib", -1.0), ("pk", 1024.0), ("nk", -1024.0), ("n4", -988.0), ("ism", 1.0 / 4096), ("nb4", -4096.0), ("ib4", 4096.0)):
+    r15 = ("mask", T.mask[:, 15:16])
+    act(C(2), C(0), ID, 127.0, -8.0)
+    act(C(4), r15, ID, 4096.0, -4096.0)
+    act(C(14), r15, ID, -OFF, 4096.0)
+    act(C(5), r15, ID, -1.0, 1.0 - 2.0 ** -13)
+    act(C(6), C(5), ID, 0.0, 4096.0)
+    act(C(12), C(5), ID, 0.0, OFF)
+    act(C(15), r15, ID, -1.0, -8191.0)
+    select("i4", T.i4[:], B("one"), [[-1, 128]], OP.is_equal, 0.0, 0, 1)
+    for nm, w in (("ib", 1.0), ("nib", -1.0), ("pk", 1024.0), ("nk", -1024.0), ("n4", -988.0), ("ps", 241.0), ("ib4", 4096.0), ("nb4", -4096.0)):
         act(B(nm), B("i4"), ID, 0.0, w)
-    act(B("ibk"), B("i4"), ID, 0.0, col(12), extra=["pf12"])
-    act(B("s15"), B("blk"), ID, 0.0, col(3), extra=["pf3"])
+    act(B("ibk"), B("i4"), ID, 0.0, col(4), extra=["pf4"])
+    act(B("nbk"), B("i4"), ID, 0.0, col(14), extra=["pf14"])
+    act(B("s15"), B("blk"), ID, 0.0, r15[1], extra=["mask"])
     act(B("gs"), B("blk"), ID)
     fill("gs", T.gs[:, :, 8], 0.0)
     act(B("gsb"), B("blk"), ID)
@@ -239,21 +254,16 @@ def rank_program(g, core, T, topo):
     for ap, v in ((T.ca[:], 0.0), (T.ca[:, :, 1:32:4], -2048.0), (T.ca[:, :, 2:32:4], -2048.0), (T.ca[:, :, 0], 1536.0)):
         fill("ca", ap, v)
     for u in (0, 1):
-        ts(B("Ta", u), ("cy0", T.cy[:, 0:144]), 0.0, OP.mult, c=0.5)
-        fill("Wch%d" % u, T["Wch%d" % u][:], 1.0)
-    fill("c15", T.c15[:], 0.0)
-    act(("c15", T.c15[:, 0:128]), B("i4"), ID, 0.0, col(3), extra=["pf3"])
-    ts(C(4), C(2), 8.0, OP.is_equal, -8192.0, OP.mult)
-    ts(C(5), C(2), 9.0, OP.is_equal, -TOP, OP.mult)
-    fill("cm", T.cm[:, 15:128:16], 0.0)
-    ts(B("t0"), B("cm"), 0.5, OP.add, col(4), OP.mult, extra=["pf4"])
-    ts(B("t1"), gcl, col(2), OP.is_equal, col(5), OP.add, extra=["pf2", "pf5"])
-    tt(B("g10"), B("t0"), B("t1"), OP.add)
-    act(B("g10k"), B("g10"), ID)
-    fill("g10k", T.g10k[:, 15:128:16], 0.0)
-    ts(C(6), C(3), -1.0 / 64, OP.mult)
-    act(B("kc"), B("ic"), ID, col(6), 0.0, extra=["pf6"])
-    ts(C(7), C(0), 16.0, OP.add)
+        ts(B("Ta", u), ("cy", T.cy[:, 0:144]), 0.0, OP.mult, c=0.5)
+    fill("hd", T.hd[:], M0)
+    for j, v in ((2, -M0), (4, -31.5 / 4096), (5, M1 / 4096), (8, -1023.5), (9, M2), (10, -M2)):
+        fill("hd", T.hd[:, j:176:11], v)
+    select("gsp", T.gsp[0:32, :], ("one", T.one[0:32, :]), [[1, 8], [0, 16]], OP.is_equal, 0.0, 0, -1)
+    fill("qd_", T.qd[:, 0, 0:176], 1.0)
+    for j, v in ((0, 0.0), (3, -1.0), (5, 1.0 / 64), (7, 4096.0)):
+        fill("qd_", T.qd[:, 0, j:176:11], v)
+    act(B("kc"), B("ic"), ID, r15[1], 0.0, extra=["mask"])
+    act(C(7), C(0), ID, 16.0)
     ts(B("t2"), B("pd"), col(0), OP.is_equal, extra=["pf0"])
     ts(B("t3"), B("pd"), col(7), OP.is_equal, extra=["pf7"])
     tt(B("t2"), B("t2"), B("t3"), OP.add)
@@ -262,70 +272,52 @@ def rank_program(g, core, T, topo):
         ts(("pair%d" % k, T.pair[:, k, :]), B("pb"), T.blk[:, 16 * k:16 * k + 1], OP.mult, c=0.5, extra=["blk"])
     ts(C(8), C(0), col(1), OP.add, 1.0, OP.add, extra=["pf1"])
     ts(C(9), C(8), 16.0, OP.is_ge, -16.0, OP.mult)
-    tt(C(8), C(8), C(9), OP.add)
-    tt(C(9), C(8), C(0), OP.min)
-    tt(C(10), C(8), C(0), OP.max)
+    act(C(10), C(8), ID, col(9), extra=["pf9"])
     r16 = ("ic", T.ic[:, 0:16])
 
     def W(j):
         return ("w16%d" % j, T.w16[:, j, :])
-    fill("w160", T.w16[:, 0, :], 2.0 ** -10)
-    fill("w161", T.w16[:, 1, :], 0.0)
-    fill("w161", T.w16[:, 1, 0:1], 2.0 ** 75)
-    scan(W(2), W(0), W(1), OP.mult, OP.add)
-    ts(W(3), r16, col(9), OP.is_equal, extra=["pf9"])
-    tt(W(3), W(3), W(2), OP.mult)
-    fill("w161", T.w16[:, 1, :], 1.0)
-    scan(W(2), W(1), W(3), OP.mult, OP.max)
-    ts(W(4), r16, col(9), OP.is_gt, 33.0, OP.mult, extra=["pf9"])
-    ts(W(5), r16, col(10), OP.is_le, extra=["pf10"])
-    tt(W(4), W(4), W(5), OP.mult)
-    ts(B("wt"), W(4), -1.0, OP.add, T.w16[:, 2, 15:16], OP.mult, extra=["w162"])
+    ts(W(0), r16, col(0), OP.is_gt, 2.0 ** -10, OP.max, extra=["pf0"])
+    ts(W(1), r16, col(10), OP.is_gt, 2.0 ** -10, OP.max, extra=["pf10"])
+    tt(W(2), W(0), W(1), OP.max)
+    scan(W(3), W(2), ("one", T.one[:, 0:16]), OP.mult, OP.mult, first=2.0 ** 85)
+    tt(W(4), W(0), W(1), OP.not_equal)
+    act(W(5), W(4), ID, -1.0, 33.0)
+    act(B("wt"), W(5), ID, 0.0, T.w16[:, 3, 15:16], extra=["w163"])
     fill("half", T.half[:], 0.5)
+    if CFG["fold"]:
+        iota("zero", [[0, 64]], 0)
     fill("pad", T.sq[:, :, 128:144], 0.5)
-    for ap, v in ((T.cb[:], -512.0), (T.cb[:, :, 1:32:4], 1024.0), (T.cb[:, :, 3:32:4], -1024.0), (T.cb[:, :, 29], 512.0), (T.cb[:, :, 0:31:30], -2048.0)):
+    for ap, v in ((T.cb[:], -157.0), (T.cb[:, :, 1:32:4], 1024.0), (T.cb[:, :, 3:32:4], -1024.0), (T.cb[:, :, 29], 512.0), (T.cb[:, :, 0:31:30], -2048.0)):
         fill("cb", ap, v)
-    fill("mp", T.mp[:], -1.0e9)
-    fill("mp", T.mp[:, 0:128:16], OFF)
-    fill("mp", T.mp[:, 15:128:16], OFF)
-    for u in (0, 1):
-        iota("dlh%d" % u, [[0, 128]], 0)
+    fill("mp", T.mp[:], 1.0e9)
+    fill("mp", T.mp[:, 0:128:16], -0.5)
+    fill("mp", T.mp[:, 15:128:16], -0.5)
     fill("cw", T.cw[:, 2048:CW], 0.0)
     fill("cf_", T.cf[:, 2048:CW], 0.0)
-    act(B("cy"), ("cy0", T.cy[:]), ID, 0.0, 8192.0)
-    lastw["cy0"] = lastw["cy"]
-    ops[lastw["cy"]]["need"].update(readers["cy0"][:-1])
-    iota("one", [[0, 128]], 1)
     for i in range(16):
-        add("g", [lambda i=i: g.affine_select(T.wm[:, i, :], T.one[:], [[-16, 8], [0, 16]], OP.is_equal, 0.0, -i, 1)], ["one"], ["wm%d" % i], 0.41)
-        if CFG["wmi"]:
-            add("g", [lambda i=i: g.affine_select(T.wn[:, i, :], T.nib[:], [[-16, 8], [0, 16]], OP.not_equal, 1.0, -i, 1)], ["nib"], ["wn%d" % i], 0.41)
-            add("g", [lambda i=i: g.affine_select(T.wn[:, i, i:128:16], T.wn[:, i, i:128:16], [[-16, 8]], OP.not_equal, 0.0, -i, 1)], ["wn%d" % i], ["wn%d" % i], 0.2)
-    ts(B("t1"), ic, col(0), OP.is_gt, 16384.0, OP.mult, extra=["pf0"])
-    ts(B("t3"), B("mask"), -4096.0, OP.mult)
-    tt(("posw", T.posw[:, 0:128]), B("t1"), B("t3"), OP.add)
-    act(("posw", T.posw[:, 128:256]), ("posw", T.posw[:, 0:128]), ID)
-    fill("posw", T.posw[:, 256:384], 0.0)
-    ts(C(11), C(0), OFF, OP.add)
-    ts(C(16), C(0), OFF + 16.0, OP.add)
-    cur[0] = CFG["bc"]
+        if CFG["e_wm"][i] == "v":
+            ts(("wm%d" % i, T.wm[:, i, :, :]), B("blk"), T.mask[:, i:i + 1], OP.mult, c=0.5, extra=["mask"])
+        else:
+            act(("wm%d" % i, T.wm[:, i, :, :]), B("blk"), ID, 0.0, T.mask[:, i:i + 1], extra=["mask"])
+    wms = ["wm%d" % i for i in range(16)]
+    for u in (0, 1):
+        fill("dlh%d" % u, T["dlh%d" % u][:], 0.0)
+    ts(B("t1"), ic, col(0), OP.is_lt, extra=["pf0"])
+    tt(("posw0", T.posw[:, :, 0, :]), B("t1"), B("mask"), OP.subtract)
+    act(("posw2", T.posw[:, :, 2, :]), ("posw0", T.posw[:, :, 0, :]), ID)
+    fill("posw1", T.posw[:, :, 1:4:2, :], 1.0)
+    iota("dump", [[0, 8], [16, 2]], 2048)
+    act(B("dump"), B("dump"), ID, col(0), extra=["pf0"])
     for k in range(4):
-        ts(("cw%d" % k, T.cw[:, 512 * k:512 * k + 512]), ("ci", T.ci[:, 512 * k:512 * k + 512]), col(14), OP.add, extra=["pf14"])
+        act(("cw%d" % k, T.cw[:, 512 * k:512 * k + 512]), ("ci", T.ci[:, 512 * k:512 * k + 512]), ID, 0.0, col(5), extra=["pf5"])
     cws = ["cw%d" % k for k in range(4)]
-    cur[0] = 0.0
+    bk = ("bk", T.hd[:, 7:176:11])
 
     def gather(u, st, t, lst):
         G, M, N = (T["%s%sh%d" % (n, st, u)] for n in "GMN")
         win, slot = T.xw[:, 0:4096], 2 * t + u
-        nch, ndve = CFG["ch_" + st], CFG["gv_" + st]
-        if t == 0 and st == "a":
-            ndve = CFG["gv0"][u]
-        if t == ROUNDS - 1 and st == "b":
-            ndve = CFG["gv4"][u]
-        w = (128 - ndve) // nch
-        cut = [w] * (nch - 1) + [128 - ndve - w * (nch - 1)]
-        if 0 < t + (st == "b") < ROUNDS:
-            cut = CFG["cut"].get(st + str(u), cut)
+        cut = CFG["cut0" if t == 0 and st == "a" else "cut4" if t == ROUNDS - 1 and st == "b" else "cut"][st + str(u)]
         parts = [("s", sum(cut[:n]), sum(cut[:n + 1])) for n in range(len(cut))] + ([("v", sum(cut), 128)] if sum(cut) < 128 else [])
         kg, km, kn = [], [], []
         for n, (q, a, b) in enumerate(parts):
@@ -334,37 +326,45 @@ def rank_program(g, core, T, topo):
             o, i = G[:, 16 * a:16 * b], win.indirect(T[lst][:, slot, a:b])
             more = ["xw_", "%s%d" % (lst, slot), "done%s%d.%d" % (st, u, t - 1)]
             if q == "s":
-                tag[(t, st, u, n)] = act((key, o), ("xw", i), ID, c=CFG["gam"], extra=more)
+                act((key, o), ("xw", i), ID, c=CFG["gam"], extra=more)
             else:
                 cp((key, o), ("xw", i), c=CFG["gam"], extra=more)
         for step, D, ks in ((2, N, kn), (1, M, km)):
             if step == 2 and t == 0 and st == "a":
                 continue
-            if step == 2 and st == "b" and t < CFG["fold"]:
+            if step == 2 and st == "b" and t < ROUNDS - 1 and str(u) in CFG["fold"]:
                 rid, pid, m = route(1)
                 sd = []
                 for n, (q, a, b) in enumerate(parts):
                     tr = RemoteDMATransfer(dst_ids=[DstId(rid=rid, pnc=pid)], dma_engine_mask=m, remote_sem=T.sem["arf%d" % slot],
                                            srcs=[G[:, 16 * a:16 * b - 2], G[:, 16 * a + 2:16 * b]], dsts=[T.nf[:, slot, 16 * a:16 * b - 2]], alu_op=3)
-                    sd.append(add("g", [lambda tr=tr: g.remote_dma_fused([tr], local_sem=T.sem["sf%d" % slot])], [kg[n]], [], 0.3, "none", 0, CFG["lf"]))
+                    sd.append(add("g", [lambda tr=tr: g.remote_dma_fused([tr], local_sem=T.sem["sf%d" % slot])], [kg[n]], [], 0.3, "none", 0, CFG["ls"] + (b - a) * CFG["lf"]))
                 add(None, [], [], ["nf%d" % (slot + 2)], 0.0, "arf%d" % slot, NENG * len(sd), 0.0, deps=sd)
                 add(None, [], [], ["doneb%d.%d" % (u, t)], 0.0, "sf%d" % slot, NENG * len(sd), 0.0, deps=sd)
                 continue
-            for n, (q, a, b) in enumerate(parts):
+            whole = step == 2 and st + str(u) in CFG["whole"]
+            for n, (q, a, b) in enumerate([("v", 0, 128)] if whole else parts):
                 key = "%d%sh%d.%d" % (step, st, u, n)
                 ks.append(key)
                 a, b = 16 * a, 16 * b
-                scan((key, D[:, a // step:b // step - 1]), (kg[n], G[:, a:b - step:step]), (kg[n], G[:, a + step:b:step]), OP.max, OP.min, 0.5)
+                scan((key, D[:, a // step:b // step - 1]), (kg[n], G[:, a:b - step:step]), (kg[n], G[:, a + step:b:step]), OP.max, OP.min, 0.5, extra=kg if whole else ())
         return kg, km, kn
+
+    def sums(P, kd, D, step, items, keys, last=False):
+        calls = [(P[:, :, cols], D[:, p:128 * step:step], w) for cols, p, w in items]
+        mm(calls[:-1] if last else calls, keys, [kd], st=False, sp=False)
+        if last:
+            mm(calls[-1:], keys, [kd], st=False)
 
     def first_fail(t, u):
         k = 2 * t + u
+        now[0] = t
         PA, PM, G, M, N = T["PA%d" % u], T["PM%d" % u], T["Gah%d" % u], T["Mah%d" % u], T["Nah%d" % u]
         kd, kr = "PA%d:D" % u, "rl%d" % k
         ky, Y = "PM%d:Y" % u, PM[:, 0:256]
-        mm([(Y, T.ib[:], T.cy[:])] + [(PM[:, j:256:4], T.ib4[:], T.rl[:, k, :, (14 if j else 15)::-2]) for j in range(4)], ["ib", "ib4", "cy", kr], [ky])
+        mm([(Y, T.ib[:], T.cy[:])] + [(PM[:, j:256:4], T.ib[:], T.rl[:, k, :, (14 if j else 15)::-2]) for j in range(4)], ["ib", "cy", kr], [ky])
         kg, km, kn = gather(u, "a", t, "la")
-        mm([(PA[:, :, 0:32], T.ib[:], T.ca[:])], ["ib", "ca"], [kd], sp=False)
+        mm([(PA[:, :, 0:32], T.ib[:], T.ca[:])], ["ib", "ca", "la%d" % k, "sgh%d" % u], [kd], sp=False)
         if t:
             c0, c1 = T.sl[:, k, :, 15::-2], T.sl[:, k, :, 14:0:-2]
             mm([(PA[:, :, 0:32:4], T.nk[:], c0), (PA[:, :, 1:32:4], T.pk[:], c0), (PA[:, :, 2:32:4], T.pk[:], c0), (PA[:, :, 4:32:4], T.pk[:], c1),
@@ -373,32 +373,30 @@ def rank_program(g, core, T, topo):
         for p in range(16):
             z = 4 * (7 - p // 2)
             if p % 2:
-                items.append((PA[:, :, z:z + 4], G[:, p:2048:16], T.gs[:, :, 7:11]))
+                items.append((slice(z, z + 4), p, T.gs[:, :, 7:11]))
             else:
                 n = 5 if p else 3
-                items.append((PA[:, :, z + 1:z + 1 + n], G[:, p:2048:16], T.gs[:, :, 3:3 + n]))
-        mm(items, ["gs"] + kg, [kd], st=False, sp=False)
+                items.append((slice(z + 1, z + 1 + n), p, T.gs[:, :, 3:3 + n]))
+        sums(PA, kd, G, 16, items, kg + ["gs"])
         if t:
-            mm([(PA[:, :, 4 * (7 - i) + 1], N[:, i:1024:8], T.gm[:, :, 0]) for i in range(7)], kn + ["gm"], [kd], st=False, sp=False)
+            sums(PA, kd, N, 8, [(4 * (7 - i) + 1, i, T.gm[:, :, 0]) for i in range(7)], kn + ["gm"])
+            if str(u) in CFG["fold"]:
+                kf, F = "PM%d:F" % u, PM[:, 384:448]
+                mm([(F, T.ib[:], T.zero[:])] + [(PM[:, 384 + i:448:8], T.nf[:, k - 2, 2 * i:2048:16], T.gp[:]) for i in range(7)],
+                   ["ib", "zero", "gp", "nf%d" % k], [kf])
+                tt(("nl%d" % k, T.nl[:, k, :, :]), (kf, F), ("tl%d" % k, T.tl[:, k, :]), OP.is_ge)
+            nl = T.nl[:, k, :, 7::-1]
+            mm([(PA[:, :, j:32:4], w[:], nl) for j, w in enumerate((T.nk, T.pk, T.pk, T.nk))], ["nl%d" % k, "pk", "nk"], [kd], st=False, sp=False)
         items = []
         for p in range(15):
             z = 4 * (7 - p // 2)
-            items.append((PA[:, :, z], M[:, p:2048:16], T.gm[:, :, 0]) if p % 2 else (PA[:, :, z + 2:z + 4], M[:, p:2048:16], T.gm[:, :, 0:2]))
-        mm(items[:8], km + ["gm"], [kd], st=False, sp=False)
-        mm(items[8:], km + ["gm"], [kd], st=False, sp=t == 0)
-        if 0 < t <= CFG["fold"]:
-            kf, F = "PM%d:F" % u, PM[:, 384:448]
-            mm([(F, T.ib[:], T.posw[:, 256:320])] + [(PM[:, 384 + i:448:8], T.nf[:, k - 2, 2 * i:2048:16], T.gp[:]) for i in range(7)],
-               ["ib", "posw", "gp", "nf%d" % k], [kf])
-            tt(("nl%d" % k, T.nl[:, k, :, :]), (kf, F), ("tl%d" % k, T.tl[:, k, :]), OP.is_ge)
-        if t:
-            nl = T.nl[:, k, :, 7::-1]
-            mm([(PA[:, :, j:32:4], w[:], nl) for j, w in enumerate((T.nk, T.pk, T.pk, T.nk))], ["nl%d" % k, "pk", "nk"], [kd], st=False)
-        tag[(t, "D", u, 0)] = lin(CFG["e_dp"], B("Dp", u), (kd, PA[:, :, 0:32]), -TH, float(2 ** 22))
+            items.append((z, p, T.gm[:, :, 0]) if p % 2 else (slice(z + 2, z + 4), p, T.gm[:, :, 0:2]))
+        sums(PA, kd, M, 16, items, km + ["gm"], True)
+        lin(CFG["e_dp"][u], B("Dp", u), (kd, PA[:, :, 0:32]), 256.0, -256.0 * TH)
         lastw["donea%d.%d" % (u, t)] = scan(B("W", u), B("Dp", u), (ky, Y), OP.max, OP.min)
 
     def moved(u, near, rp, out, kout, last):
-        kf, F = "PM%d:F" % u, T["PM%d" % u][:, 384:448]
+        kf, F = "PB%d:F" % u, T["PB%d" % u][:, :, 32:40]
         mm([(F, T.ib4[:], rp[2]), (F, T.nb4[:], rp[3])], [rp[0], "ib4", "nb4"], [kf])
         tt(("dlh%d" % u, T["dlh%d" % u][:, 1:128:2]), (kf, F), near, OP.mult)
         mm([(out, T["dlh%d" % u][:], T.i4[:])], ["dlh%d" % u, "i4"], [kout], sp=False, c=4)
@@ -407,61 +405,52 @@ def rank_program(g, core, T, topo):
     def stage_a(t, u):
         k = 2 * t + u
         PA, PB, PM = T["PA%d" % u], T["PB%d" % u], T["PM%d" % u]
-        Wd, Wc, Ta, WT = T["Wh%d" % u], T["Wch%d" % u], T["Tah%d" % u], T["WTh%d" % u]
-        end = ("Wh%d" % u, Wd[:, 31:256:32])
-        wc = ("Wch%d" % u, Wc[:, 0:8])
-        tag[(t, "C", u, 0)] = lin(CFG["e_wc"], wc, end, 0.0, 1.0)
-        tt(("Tah%d" % u, Ta[:, 15:128:16]), end, wc, OP.subtract)
-        kl, L = "PM%d:L" % u, PM[:, 448:456]
-        mm([(L, Ta[:, 15 - i:143 - i], T.ib[:, i:128:16]) for i in range(16)], ["Tah%d" % u, "ib"], [kl])
+        Ta, sg = T["Tah%d" % u], T["sgh%d" % u]
         d = t % n_ranks
-        c0, c1 = 8 * u, 8 * u + 8
-        hs = ("hs%d" % u, T.hs[:, c0:c1])
-        tt(hs, (kl, L), ("qb%d" % d, T.qb[:, d, c0:c1]), OP.mult)
-        kt, TT_ = "PB%d:T" % u, PB[0:10, :, 48:64]
-        mm([(TT_, Wc[:, 0:10], T.ib[:])], [wc[0], "ib"], [kt])
-        wt = ("WTh%d" % u, WT[0:10, :])
-        tag[(t, "W", u, 0)] = lin(CFG["e_wt"], wt, (kt, TT_), 0.0, 1.0)
-        k1, P1 = "PB%d:U" % u, PB[:, :, 32:48]
-        mm([(P1, T.g10[0:10, :], wt[1])], ["g10", wt[0]], [k1])
+        a, b = 88 * u, 88 * u + 88
+        end = ("Wh%d" % u, T["Wh%d" % u][:, 31:256:32])
+        for j in (0, 3, 6):
+            lin(CFG["e_hd"][u], ("hd%d.%d" % (j, u), T.hd[:, a + j:b:11]), end, 1.0, 0.0, extra=["hd"])
+        scan(("hb%d" % u, T.hb[:, a:b]), ("qd%d" % d, T.qd[:, d, a:b]), ("bk", T.hd[:, a:b]), OP.mult, OP.add, extra=["qd_4"] + ["hd%d.%d" % (j, u) for j in (0, 3, 6)])
+        tt(("Tah%d" % u, Ta[:, 15:128:16]), ("hb%d" % u, T.hb[:, a + 7:b:11]), ("hb%d" % u, T.hb[:, a + 10:b:11]), OP.subtract)
+        kl, L = "PM%d:H" % u, PM[:, 256:320]
+        mm([(L, Ta[:, 15 - i:143 - i], T.wm[:, i, :, 0:8]) for i in range(16)], ["Tah%d" % u] + wms, [kl])
+        ow = ("ow%d" % u, T.ow[:, 8 * u:8 * u + 8])
+        cp(ow, (kl, PM[:, 256:320:8]))
+        lin(CFG["e_hr"][u], ("hr%d" % u, T.hr[:, 4 * u:4 * u + 4, :]), (kl, L), 1.0 / 4096, 0.0)
+        k1, P1 = "PA%d:U" % u, PA[:, :, 48:64]
+        mm([(PA[0:8, :, 48:64], end[1], T.i4[:])], [end[0], "i4"], [k1], c=4)
+        wt = ("WTh%d" % u, T["WTh%d" % u][0:8, :])
+        lin(CFG["e_wt"][u], wt, (k1, PA[0:8, :, 48:64]), 1.0, 0.0)
+        mm([(P1, T.gsp[0:8, :], wt[1])], ["gsp", wt[0]], [k1])
         j = 2 * (t % 2) + u
-        tag[(t, "N", u, 0)] = act(B("Dn", u), (k1, P1), RELU, 0.0, -1.0, acc=("acc%d" % j, T.acc[:, j:j + 1]))
-        kk, K = "PA%d:D" % u, PA[:, :, 32:48]
+        act(B("sg", u), (k1, P1), SIGN, col(2), -1.0, extra=["pf2"], acc=("acc%d" % j, T.acc[:, j:j + 1]))
+        kk, K = "PB%d:K" % u, PB[:, :, 48:64]
         if t:
             moved(u, ("nl%d" % k, T.nl[:, k, :, :]), ("rl%d" % k, T.rl[:, k, :, :], T.rl[:, k, :, 0:16:2], T.rl[:, k, :, 1:16:2]), K, kk, False)
         else:
             mm([(K, T.rl[:, k, :, :], T.ib4[:])], ["ib4", "rl%d" % k], [kk], sp=False)
-        mm([(K, T.g10k[0:10, :], wt[1]), (K, T.ibk[:], T["Dnh%d" % u][:])], ["g10k", wt[0], "ibk", "Dnh%d" % u], [kk], st=False)
-        h0, h1 = ("hi0%d" % u, T.hi[:, 0, c0:c1]), ("hi1%d" % u, T.hi[:, 1, c0:c1])
-        tt(h0, hs, ("bk", T.bk[:, c0:c1]) if t else ("qb0", T.qb[:, 0, 16 + c0:16 + c1]), OP.add)
-        ts(h1, h0, 6, OP.arith_shift_right, 2047, OP.bitwise_and)
-        ow = ("ow%d" % u, T.ow[:, c0:c1])
-        cp(ow, h1)
-        if t:
-            tt(B("Z", u), ("cw", T.cw[:, 0:CW].indirect(ow[1])), B("Dn", u), OP.add, c=CFG["gam"], extra=[ow[0]])
-        else:
-            ts(B("Y", u), ("ci", T.ci[:, 0:2048].indirect(ow[1])), col(14), OP.add, c=CFG["gam"], extra=[ow[0], "pf14"])
-            tt(B("Z", u), B("Y", u), B("Dn", u), OP.add)
-        tt(B("R1", u), B("Z", u), (kk, K), OP.min)
+        mm([(K, T.nbk[:], T.one[:])], ["nbk", "one"], [kk], st=False, sp=False)
+        mm([(K, T.ibk[:], sg[:])], ["ibk", "sgh%d" % u], [kk], st=False)
+        tt(B("Z", u), ("cw", T.cw[:, 0:CW].indirect(ow[1])), B("sg", u), OP.mult, c=CFG["gam"], extra=[ow[0]] + cws)
         lb = ("lb%d" % k, T.lb[:, k, :])
-        ts(lb, B("R1", u), OFF, OP.add, c=0.5)
+        tt(lb, B("Z", u), (kk, K), OP.max)
+        ts(B("R1", u), lb, -OFF, OP.add, 1.0 / 4096, OP.mult, c=0.5)
         if t < ROUNDS - 1:
             send(lb, ("la%d" % (k + 2), T.la[:, k + 2, :]), "arl%d" % k)
         R1, E = T["R1h%d" % u], T["Eh%d" % u]
-        ks, Sc = "PM%d:H" % u, PM[:, 256:384]
-        for b in (0, 1):
-            P, kp = T["PE%d" % (b * CFG["e2"])], "PE%d:E" % (b * CFG["e2"])
+        kh, H = "PM%d:H" % u, PM[:, 256:384]
+        for b, (P, kp) in enumerate(((T.PE0, ["PE0:E"]), (PA, ["PA%d:D" % u, k1]))):
             for j in range(4):
-                mm([(P[:, 128 * j:128 * j + 128], T.pair[:, 4 * b + j, :], R1[:])], ["R1h%d" % u, "pair%d" % (4 * b + j)], [kp])
-            zero(CFG["e_eq"][t][2 * u + b], ("Eh%d.%d" % (u, b), E[:, 512 * b:512 * b + 512]), (kp, P[:, 0:512]))
+                mm([(P[:, 2 * j:2 * j + 2, :], T.pair[:, 4 * b + j, :], R1[:])], ["R1h%d" % u, "pair%d" % (4 * b + j)], kp)
+            ts(("Eh%d.%d" % (u, b), E[:, 512 * b:512 * b + 512]), (kp[0], P[:]), 0.0, OP.is_equal, extra=kp[1:])
         for j in range(8):
-            mm([(PM[:, 256 + 16 * j:272 + 16 * j], E[:, 128 * j:128 * j + 128], T.wt[:])], ["Eh%d.%d" % (u, j // 4), "wt"], [ks])
+            mm([(PM[:, 256 + 16 * j:272 + 16 * j], E[:, 128 * j:128 * j + 128], T.wt[:])], ["Eh%d.%d" % (u, j // 4), "wt"], [kh])
         q2 = ("q2%d" % k, T.sq[:, k, 0:128])
-        ts(q2, (ks, Sc), 0.0, OP.is_le, -0.5, OP.add)
+        ts(q2, (kh, H), 0.0, OP.is_le, -0.5, OP.add)
         if t < ROUNDS - 1:
             send(q2, ("sl%d" % (k + 2), T.sl[:, k + 2, :, :]), "ars%d" % k)
-        kh, H = "PM%d:H" % u, PM[:, 256:384]
-        mm([(H, R1[:], T.ism[:]), (H, T.ib[:], T.half[:]), (H, T.nib[:], q2[1])], ["R1h%d" % u, "ib", "ism", "half", "nib", q2[0]], [kh])
+        mm([(H, R1[:], T.ib[:]), (H, T.ib[:], T.half[:]), (H, T.nib[:], q2[1])], ["R1h%d" % u, "ib", "half", "nib", q2[0]], [kh])
         rp = ("rp%d" % k, T.rq[:, k, :])
         scan(rp, q2, (kh, H), OP.max, OP.min)
         if t < ROUNDS - 1:
@@ -469,84 +458,80 @@ def rank_program(g, core, T, topo):
 
     def stage_b(t, u):
         k = 2 * t + u
-        PA, PB, PM, G, M, N = T["PA%d" % u], T["PB%d" % u], T["PM%d" % u], T["Gbh%d" % u], T["Mbh%d" % u], T["Nbh%d" % u]
+        PB, PM, G, M, N = T["PB%d" % u], T["PM%d" % u], T["Gbh%d" % u], T["Mbh%d" % u], T["Nbh%d" % u]
         kg, km, kn = gather(u, "b", t, "lb")
         kd, kq, kp = "PB%d:D" % u, "q2%d" % k, "rp%d" % k
         c0, c1 = T.sq[:, k, 1:128:2], T.sq[:, k, 2:130:2]
         mm([(PB[:, :, 0:32], T.ib[:], T.cb[:])], ["ib", "cb", "lb%d" % k], [kd], sp=False)
         mm([(PB[:, :, 1:32:4], T.n4[:], c0), (PB[:, :, 3:32:4], T.pk[:], c0), (PB[:, :, 1:32:4], T.n4[:], c1),
-            (PB[:, :, 3:32:4], T.nk[:], c1), (PB[:, :, 0:32:2], T.pk[:], T.sq[:, k, 0:128])], [kq, "pad", "pk", "nk", "n4"], [kd], st=False, sp=False)
+            (PB[:, :, 3:32:4], T.nk[:], c1), (PB[:, :, 0:32:2], T.ps[:], T.sq[:, k, 0:128])], [kq, "pad", "pk", "nk", "n4", "ps"], [kd], st=False, sp=False)
         items = []
         for p in range(15):
             z = 4 * (p // 2)
             if p % 2:
-                items.append((PB[:, :, z + 2:z + 5], G[:, p:2048:16], T.gs[:, :, 3:6]))
+                items.append((slice(z + 2, z + 5), p, T.gs[:, :, 3:6]))
             else:
                 a, b = (4 if p == 0 else 0), (4 if p == 14 else 7)
-                items.append((PB[:, :, z - 3 + a:z - 3 + b], G[:, p:2048:16], T.gsb[:, :, a:b]))
-        mm(items, ["gs", "gsb"] + kg, [kd], st=False, sp=False)
-        if t >= CFG["fold"]:
-            mm([(PB[:, :, 4 * i + 1], N[:, i:1024:8], T.gp[:]) for i in range(7)], kn + ["gp"], [kd], st=False, sp=False)
+                items.append((slice(z - 3 + a, z - 3 + b), p, T.gsb[:, :, a:b]))
+        sums(PB, kd, G, 16, items, kg + ["gs", "gsb"])
+        if kn:
+            sums(PB, kd, N, 8, [(4 * i + 1, i, T.gp[:]) for i in range(7)], kn + ["gp"])
         items = []
         for p in range(14):
             z = 4 * (p // 2)
-            items.append((PB[:, :, z + 4], M[:, p:2048:16], T.gm[:, :, 0]) if p % 2 else (PB[:, :, z + 2:z + 4], M[:, p:2048:16], T.gm[:, :, 0:2]))
-        mm(items[:-1], km + ["gm"], [kd], st=False, sp=False)
-        mm(items[-1:], km + ["gm"], [kd], st=False)
+            items.append((z + 4, p, T.gm[:, :, 0]) if p % 2 else (slice(z + 2, z + 4), p, T.gm[:, :, 0:2]))
+        sums(PB, kd, M, 16, items, km + ["gm"], True)
+        cp(B("p4", u), (kd, PB[:, :, 0:32:2]))
+        scan(B("X", u), B("mp"), B("p4", u), OP.min, OP.max, 0.5)
         ns = ("ns%d" % k, T.ns[:, k, :])
-        if CFG["e_th"] == "s":
-            tag[(t, "T", u, 0)] = act(B("th", u), (kd, PB[:, :, 3:32:4]), RELU, -TH * 8192.0, 8192.0)
+        if CFG["e_th"][u] == "s":
+            act(B("th", u), (kd, PB[:, :, 3:32:4]), RELU, -TH * 8192.0, 8192.0)
         else:
             ts(B("th", u), (kd, PB[:, :, 3:32:4]), TH, OP.is_gt, 4096.0, OP.mult)
-        if t < CFG["fold"]:
-            tt(ns, B("th", u), (kd, PB[:, :, 1:32:4]), OP.subtract, c=1)
+        if not kn:
+            tt(ns, B("th", u), (kd, PB[:, :, 1:32:4]), OP.subtract)
             send(ns, ("tl%d" % (k + 2), T.tl[:, k + 2, :]), "arn%d" % k)
         else:
             tt(ns, (kd, PB[:, :, 1:32:4]), B("th", u), OP.is_ge)
             if t < ROUNDS - 1:
                 send(ns, ("nl%d" % (k + 2), T.nl[:, k + 2, :, :]), "arn%d" % k)
-        cur[0] += CFG["bs"]
-        if CFG["e_p4"][u] == "s":
-            tag[(t, "P", u, 0)] = act(B("p4", u), (kd, PB[:, :, 0:32:2]), RELU, -TH * 8192.0, 8192.0)
-        else:
-            ts(B("p4", u), (kd, PB[:, :, 0:32:2]), TH, OP.is_gt, 4096.0, OP.mult)
-        scan(B("X4", u), B("mp"), B("p4", u), OP.max, OP.subtract, 0.5)
         kh, H = "PM%d:H" % u, PM[:, 256:384]
-        mm([(H, T.ib4[:], T.rq[:, k, :]), (H, T.ib4[:], T.half[:]), (H, T.nib[:], T["X4h%d" % u][:])], [kp, "ib4", "half", "nib", "X4h%d" % u], [kh])
-        scan(B("S", u), B("X4", u), (kh, H), OP.max, OP.min)
+        mm([(H, T.ib[:], T.rq[:, k, :]), (H, T.nib[:], T.half[:])], [kp, "ib", "half", "nib"], [kh], sp=False)
+        mm([(H, T.nib[:], T["Xh%d" % u][:])], ["nib", "Xh%d" % u], [kh], st=False)
+        scan(B("S", u), B("X", u), (kh, H), OP.min, OP.max)
         mm([(H, T["Sh%d" % u][:], T.ib[:])], ["Sh%d" % u, "ib"], [kh])
-        tag[(t, "S", u, 0)] = lin(CFG["e_sa"][u], B("SA", u), (kh, H), OFF if t == ROUNDS - 1 else col(13), 1.0, extra=["pf13"])
-        if t == ROUNDS - 1:
-            cur[0] -= 3.0
-            kk, K = "PA%d:D" % u, PA[:, :, 32:48]
+        if t < ROUNDS - 1:
+            act(B("SA", u), (kh, H), ID, col(12), col(6), extra=["pf6", "pf12"])
+        else:
+            act(B("SA", u), (kh, H), ID, OFF, 4096.0)
+            kk, K = "PB%d:K" % u, PB[:, :, 48:64]
+            now[0] = t + 1
             moved(u, ns, (kp, T.rq[:, k, 0:128], T.rq[:, k, 0:128:2], T.rq[:, k, 1:128:2]), K, kk, True)
+            now[0] = t
             act(B("Y", u), (kk, K), ID, OFF)
-            add("y", [lambda: g.sync.dma_start(T.yr[:, 128 * u:128 * u + 128], T["Yh%d" % u][:])], ["Yh%d" % u], [], 0.1, "sty%d" % u, 16, 2.0)
+            add("y", [lambda: g.sync.dma_start(T.yr[:, 128 * u:128 * u + 128], T["Yh%d" % u][:])], ["Yh%d" % u], [], 0.1, "sty%d" % u, 16, 5.3)
 
     def count(t):
-        P, c = T.PE1[:, 0:1], 2 * (t % 2)
+        P, c = T.PE1[:, 0, 3, 2:3], 2 * (t % 2)
         mm([(P, T.kc[:], T.acc[:, c + u:c + u + 1]) for u in (0, 1)], ["kc", "acc%d" % c, "acc%d" % (c + 1)], ["PE1:E"], c=4)
         d = (t + 1) % n_ranks
-        ts(B("bk"), ("qb%d" % d, T.qb[:, d, 16:32]), P, OP.add, extra=["PE1:E"])
+        ts(bk, ("qd%d" % d, T.qd[:, d, 176:192]), P, OP.add, -0.5, OP.mult, extra=["PE1:E"])
 
-    def winners(t):
+    def winners():
         P, kp = T.PE1, "PE1:E"
-        cp(B("h16"), ("hi10", T.hi[:, 1, :]), extra=["hi11"])
-        mm([(P[:, 0:384], T.ib[:], T.posw[:])] + [(P[:, 128 * u:128 * u + 128], T.s15[:], T["Dnh%d" % u][:]) for u in (0, 1)]
-           + [(P[:, 256 + 16 * m:272 + 16 * m], T.s15[:], T["Dnh%d" % (m // 4)][:, 32 * (m % 4):32 * (m % 4) + 16]) for m in range(8)],
-           ["ib", "posw", "s15", "Dnh0", "Dnh1"], [kp], sp=False)
+        mm([(P[:], T.ib[:], T.posw[:])], ["ib", "posw0", "posw1", "posw2"], [kp], sp=False)
+        for u in (0, 1):
+            mm([(P[:, 4 * u:4 * u + 4, s:4:2, :], T.s15[:], T["sgh%d" % u][:]) for s in (0, 1)], ["s15", "sgh%d" % u], [kp], st=False, sp=False)
+        mm([(P[:, :, s, 8 * r:8 * r + 8], T.nib[:], T.hr[:, :, 8 * min(s, 1):8 * min(s, 1) + 8]) for s in range(3) for r in (0, 1)],
+           ["nib", "hr0", "hr1"], [kp], st=False, sp=False)
         for a in range(0, 16, 4):
-            items = []
-            for i in range(a, a + 4):
-                items += [(P[:, i:256:16], T.wn[:, i, :], T.h16[:])] if CFG["wmi"] else [(P[:, i:256:16], T.nib[:], T.h16[:]), (P[:, i:256:16], T.wm[:, i, :], T.h16[:])]
-                items += [(P[:, 256 + i:384:16], T.nib[:], T.h16[:, 1:16:2]), (P[:, 256 + i:384:16], T.wm[:, i, :], T.h16[:, 0:16:2])]
-            mm(items, ["h16", "nib"] + ["w%s%d" % (c, i) for c in "mn" for i in range(a, a + 4)], [kp], st=False, sp=a == 12)
-        zero(CFG["e_eq"][t][4], B("ew"), (kp, P[:, 0:384]))
-        Q = P[:, 384:400]
-        mm([(Q, T.ib[:], T.h16[:])] + [(Q, T.ib4[:], T.ew[:, i:256:16]) for i in range(16)], ["ib", "h16", "ib4", "ew"], [kp], sp=False)
-        mm([(P[:, 385:400:2], T.ib4[:], T.ew[:, 256 + i:384:16]) for i in range(16)], ["ib4", "ew"], [kp], st=False)
-        ts(("lw0", T.lw[:, 0:16:2]), (kp, P[:, 384:400:2]), col(11), OP.min, extra=["pf11"])
-        ts(("lw1", T.lw[:, 1:16:2]), (kp, P[:, 385:400:2]), col(16), OP.min, extra=["pf16"])
+            mm([(P[:, :, 0:3, i], T.wm[:, i, :, :], T.hr[:, :, 0:12:4]) for i in range(a, a + 4)], ["hr0", "hr1"] + wms, [kp], st=False, sp=a == 12)
+        ts(B("ew"), (kp, P[:, :, 0:3, :]), 0.0, OP.is_equal)
+        Q = P[:, :, 3, 0:2]
+        mm([(Q, T.ib4[:], T.hr[:, :, 0:16:8])], ["hr0", "hr1", "ib4", "ew"], [kp], sp=False)
+        mm([(Q, T.ib4[:], T.ew[:, :, 0:2, i]) for i in range(16)] + [(P[:, :, 3, 1], T.ib4[:], T.ew[:, :, 2, i]) for i in range(15)], ["ib4", "ew"], [kp], st=False, sp=False)
+        mm([(P[:, :, 3, 1], T.ib4[:], T.ew[:, :, 2, 15])], ["ib4", "ew"], [kp], st=False)
+        tt(("lw0", T.lw[:]), (kp, Q), B("dump"), OP.min)
 
     def scatter(t, u):
         win, key = (T.cw, "cw") if t < ROUNDS - 1 else (T.cf, "cf")
@@ -554,263 +539,100 @@ def rank_program(g, core, T, topo):
             j = 8 * u + 2 * c
             o = win[:, 0:CW].indirect(T.lw[:, j:j + 2])
             add("v", [lambda o=o, c=c: g.vector.tensor_copy(out=o, in_=T["SAh%d" % u][:, 32 * c:32 * c + 32])],
-                ["SAh%d" % u, "lw0", "lw1"] + cws + ["cf_", "cf0", "cf1", "cf2", "cf3"], [key], 0.05 + 32 * 3.5 * 0.00083 * 1.1)
+                ["SAh%d" % u, "lw0"] + cws + ["cf_", "cf0", "cf1", "cf2", "cf3"], [key], CFG["vf"] + 32 * 3.5 * 0.00083 * CFG["f"])
 
-    order_u = (1, 0)
-    for u in order_u:
-        cur[0] = CFG["b0"] * u
-        ts(B("R1", u), ("la%d" % u, T.la[:, u, :]), -OFF, OP.add, c=0.5)
+    halves = (1, 0)
+    for u in halves:
+        ts(B("R1", u), ("la%d" % u, T.la[:, u, :]), -OFF, OP.add, 1.0 / 4096, OP.mult, c=0.5)
         H = ("PM%d:H" % u, T["PM%d" % u][:, 256:384])
-        mm([(H[1], T["R1h%d" % u][:], T.ism[:])], ["R1h%d" % u, "ism"], [H[0]])
+        mm([(H[1], T["R1h%d" % u][:], T.ib[:])], ["R1h%d" % u, "ib"], [H[0]])
         cp(("rl%d" % u, T.rl[:, u, :, :]), H)
         first_fail(0, u)
-    cur[0] = 0.0
-    for u in (0, 1):
-        mm([(T.PE0[:, 8 * u:8 * u + 8], T.c15[:, 15 - i:143 - i], T["R1h%d" % u][:, i:128:16]) for i in range(16)], ["c15", "R1h%d" % u], ["PE0:E"])
-    ts(("qi0", T.qi[:, 0, :]), ("PE0:E", T.PE0[:, 0:16]), OFF + 64.0, OP.add)
-    ts(("qi1", T.qi[:, 1, :]), ("qi0", T.qi[:, 0, :]), 63, OP.bitwise_and)
-    cp(("qb0", T.qb[:, 0, 0:16]), ("qi0", T.qi[:, 0, :]))
-    ts(("qb0", T.qb[:, 0, 16:32]), ("qi1", T.qi[:, 1, :]), 2048.0, OP.mult)
+    dst = ("rl0", T.rl[:, 0:2, :, 15])
+    ts(("qd_4", T.qd[:, 0, 4:176:11]), dst, 4096.0, OP.mult, OFF, OP.add, extra=["rl1", "qd_"])
+    ts(("qd0", T.qd[:, 0, 176:192]), dst, -262144.0, OP.mult, -2 * (65536.0 + 1024.0 - M1), OP.add, extra=["rl1"])
+    ts(bk, dst, 131072.0, OP.mult, 65536.0 - M1, OP.add, extra=["rl1", "hd"])
     for d in range(1, n_ranks):
-        send(("qb0", T.qb[:, 0, :]), ("qb%d" % d, T.qb[:, d, :]), "arq%d" % d, d)
+        send(("qd0", T.qd[:, 0, :]), ("qd%d" % d, T.qd[:, d, :]), "arq%d" % d, d, ["qd_4"])
     for t in range(ROUNDS):
         if t == ROUNDS - 1:
-            cur[0] = CFG["bc"]
             for k in range(4):
-                lin(CFG["e_cf"][k], ("cf%d" % k, T.cf[:, 512 * k:512 * k + 512]), ("cw", T.cw[:, 512 * k:512 * k + 512]), col(15), 1.0, extra=["pf15"])
-        for u in order_u:
-            cur[0] = CFG["b0"] * u
+                act(("cf%d" % k, T.cf[:, 512 * k:512 * k + 512]), ("cw", T.cw[:, 512 * k:512 * k + 512]), ID, 0.0, col(15), extra=["pf15"])
+        for u in halves:
             stage_a(t, u)
-        cur[0] = CFG["bs"]
-        winners(t)
+        winners()
         if t < ROUNDS - 1:
             count(t)
-        for u in order_u:
-            cur[0] = CFG["b0"] * u
+        for u in halves:
             stage_b(t, u)
-        cur[0] = CFG["bs"]
-        for u in order_u:
+        for u in halves:
             scatter(t, u)
         if t < ROUNDS - 1:
-            for u in order_u:
-                cur[0] = CFG["b0"] * u
+            for u in halves:
                 first_fail(t + 1, u)
     add("s", [lambda: g.scalar.dma_start(T.yc[0:64, :], T.cf[0:64, 0:2048])], ["cf"], [], 0.1, "stc0", 16, 5.0)
     add("y", [lambda: g.sync.dma_start(T.yc[64:128, :], T.cf[64:128, 0:2048])], ["cf"], [], 0.1, "stc1", 16, 5.0)
 
-    seq = []
-    for t in range(ROUNDS):
-        for w in CFG["seq"].split():
-            k = tag.get((t + (w[0] in "aDCWN") - (w[-1] == "-"), w[0], int(w[1]), int(w[2]) if w[0] in "ab" else 0))
-            if k is not None and ops[k]["q"] == "s" and (t < ROUNDS - 1 or w[-1] == "-") and (t or w[-1] != "-"):
-                seq.append(k)
-    for a, b in zip(seq, seq[1:]):
-        if a not in ops[b]["need"]:
-            ops[b]["need"].add(a)
-            soft.update([(a, b), (b, a)])
-    n = len(ops)
+    n, wake = len(ops), CFG["wake"]
+    pre = [[(d, 0 if ops[d]["q"] == o["q"] == "t" else 1 if o["q"] is None else 2) for d in sorted(o["need"])] for o in ops]
+    lines = {"v": [], "s": []}
+    for t in range(-1, ROUNDS):
+        for w in ORDER["first" if t < 0 else "round" if t < ROUNDS - 1 else "last"].split():
+            k = tag[(t + (w[-1] == "+"), w.rstrip("+"))]
+            lines[ops[k]["q"]].append(k)
+    for line in lines.values():
+        for a, b in zip(line, line[1:]):
+            if a not in ops[b]["need"]:
+                pre[b].append((a, 0))
     users = [[] for _ in range(n)]
-    for k, o in enumerate(ops):
-        for d in o["need"]:
-            users[d].append(k)
-    wake = CFG["wake"]
-
-    def plan(before, after, urge, fwd):
-        left = [len(b) for b in before]
-        at, begin, more = [0.0] * n, [0.0] * n, [()] * n
-        free = {q: 0.0 for q in ("v", "s", "t", "g", "y", None)}
-        pool = [k for k in range(n) if left[k] == 0]
-        order, opened, banks = [], set(), {}
-        first, last = ("st", "sp") if fwd else ("sp", "st")
-        while pool:
-            cand = []
-            for k in pool:
-                o = ops[k]
-                st = max(free[o["q"]], at[k]) if o["q"] else at[k]
-                if o["bank"]:
-                    if o[first] and o["bank"][0] in opened:
-                        continue
-                    for a in o["bank"]:
-                        for qq, (j, tj) in banks.get(a, {}).items():
-                            if qq != o["q"]:
-                                st = max(st, tj + wake)
-                cand.append((st, k))
-            st0, k0 = min(cand)
-            q0, c0 = ops[k0]["q"], ops[k0]["cost"]
-            best, bst = k0, st0
-            for st, k in sorted(cand, key=lambda e: urge[e[1]]):
-                if ops[k]["q"] == q0 and st <= st0 + CFG["look"] * c0 + 1e-9 + CFG["gain"] * (urge[k0] - urge[k]) * (st < st0 + c0):
-                    best, bst = k, st
-                    break
-            pool.remove(best)
-            o = ops[best]
-            begin[best] = bst
-            if o["q"]:
-                free[o["q"]] = bst + o["cost"]
-            done = bst + o["cost"] + o["lat"]
+    for k in range(n):
+        for d, how in pre[k]:
+            users[d].append((k, how))
+    left = [len(e) for e in users]
+    todo, way = [k for k in range(n) if not left[k]], [0.0] * n
+    for k in todo:
+        c, lat = ops[k]["cost"], ops[k]["lat"]
+        way[k] = max([way[j] + (c, c + lat, c + lat + wake)[how] for j, how in users[k]] or [c + lat])
+        for d, how in pre[k]:
+            left[d] -= 1
+            if not left[d]:
+                todo.append(d)
+    left, at, free = [len(e) for e in pre], [0.0] * n, {}
+    pool, order, opened, banks = [k for k in range(n) if not left[k]], [], set(), {}
+    while pool:
+        cand = []
+        for k in pool:
+            o = ops[k]
+            st = max(at[k], free.get(o["q"], 0.0))
+            if o["st"] and o["bank"][0] in opened:
+                continue
             for a in o["bank"]:
-                use = banks.setdefault(a, {})
-                more[best] += tuple(j for qq, (j, tj) in use.items() if qq != o["q"])
-                use[o["q"]] = (best, done)
-                if o[first] and not o[last]:
-                    opened.add(a)
-                if o[last]:
-                    opened.discard(a)
-            order.append(best)
-            for j in after[best]:
-                if ops[j]["q"] == o["q"] == "t" or (best, j) in soft:
-                    lag = -o["lat"]
-                else:
-                    lag = wake if fwd else wake - o["lat"] + ops[j]["lat"]
-                at[j] = max(at[j], done + lag)
-                left[j] -= 1
-                if left[j] == 0:
-                    pool.append(j)
-        return max(begin[k] + ops[k]["cost"] + (ops[k]["lat"] if fwd else 0.0) for k in range(n)), order, begin, more
-
-    def polish(order, steps):
-        sets = []
-        for f, gam, wk in CFG["sets"]:
-            cost = [o["cost"] if o["q"] not in ("v", "s", "t") else (o["cost"] - o["fix"]) * f * (gam if o["ind"] else 1.0) + o["fix"] for o in ops]
-            sets.append((cost, [c + o["lat"] + wk for c, o in zip(cost, ops)], wk))
-        qs = [o["q"] for o in ops]
-        pre = [[(d, qs[d] == qs[k] == "t", qs[k] is None) for d in ops[k]["need"]] for k in range(n)]
-        lines = {}
-        for k in order:
-            for a in ([qs[k]] if qs[k] else []) + ops[k]["bank"]:
-                lines.setdefault(a, []).append(k)
-        qp, qn, bp, bn = [-1] * n, [-1] * n, [{} for _ in range(n)], [{} for _ in range(n)]
-
-        def link(a):
-            line = lines[a]
-            if a in eng:
-                for x, y in zip([-1] + line, line + [-1]):
-                    if x >= 0:
-                        qn[x] = y
-                    if y >= 0:
-                        qp[y] = x
-                return True
-            seen, on = {}, False
-            for k in line:
-                if ops[k]["st"] and on:
-                    return False
-                on = (on or ops[k]["st"]) and not ops[k]["sp"]
-                bn[k][a] = []
-            for k in line:
-                bp[k][a] = [j for qq, j in seen.items() if qq != qs[k]]
-                for j in bp[k][a]:
-                    bn[j][a].append(k)
-                seen[qs[k]] = k
-            return True
-        for a in lines:
-            link(a)
-
-        def sequence():
-            left = [len(pre[k]) + (qp[k] >= 0) + sum(len(v) for v in bp[k].values()) for k in range(n)]
-            out = [k for k in range(n) if not left[k]]
-            for k in out:
-                for j in users[k] + ([qn[k]] if qn[k] >= 0 else []) + [x for v in bn[k].values() for x in v]:
-                    left[j] -= 1
-                    if not left[j]:
-                        out.append(j)
-            return out
-
-        def head_of(k, head, cost, far, wk, skip):
-            h = 0.0
-            for d, same, none in pre[k]:
-                h = max(h, head[d] + (cost[d] if same else far[d] - wk if none else far[d]))
-            for v in bp[k].values():
-                for d in v:
-                    if d != skip:
-                        h = max(h, head[d] + far[d])
-            return h
-
-        def tail_of(k, tail, cost, far, wk, skip):
-            h = far[k] - wk
-            for j in users[k]:
-                h = max(h, tail[j] + (cost[k] if qs[j] == qs[k] == "t" else far[k] - wk if qs[j] is None else far[k]))
-            for v in bn[k].values():
-                for j in v:
-                    if j != skip:
-                        h = max(h, tail[j] + far[k])
-            return h
-        best, tabu = None, {}
-        for step in range(steps):
-            tp = sequence()
-            got = []
-            for cost, far, wk in sets:
-                head, tail = [0.0] * n, [0.0] * n
-                for k in tp:
-                    h = head_of(k, head, cost, far, wk, -1)
-                    head[k] = max(h, head[qp[k]] + cost[qp[k]]) if qp[k] >= 0 else h
-                for k in reversed(tp):
-                    h = tail_of(k, tail, cost, far, wk, -1)
-                    tail[k] = max(h, tail[qn[k]] + cost[k]) if qn[k] >= 0 else h
-                got.append((head, tail, max(tail)))
-            if not step:
-                base = [e[2] for e in got]
-            score = sum(e[2] / b for e, b in zip(got, base))
-            if best is None or score < best[0] - 1e-9:
-                best = (score, tp, [[j for v in bp[k].values() for j in v] for k in range(n)], [e[2] for e in got])
-            moves = set()
-            for (cost, far, wk), (head, tail, end) in zip(sets, got):
-                for b in range(n):
-                    if head[b] + tail[b] > end - 1e-6:
-                        a = qp[b]
-                        if a >= 0 and abs(head[a] + cost[a] - head[b]) < 1e-6 and a not in ops[b]["need"]:
-                            moves.add((a, b, qs[a]))
-                        for bank, v in bp[b].items():
-                            for a in v:
-                                if abs(head[a] + far[a] - head[b]) < 1e-6 and a not in ops[b]["need"]:
-                                    moves.add((a, b, bank))
-            rated = []
-            for a, b, line in moves:
-                s = 0.0
-                for (cost, far, wk), (head, tail, end), b0 in zip(sets, got, base):
-                    hb, ha = head_of(b, head, cost, far, wk, a), head_of(a, head, cost, far, wk, -1)
-                    tb, ta = tail_of(b, tail, cost, far, wk, -1), tail_of(a, tail, cost, far, wk, b)
-                    x, y, z, w = (qp[a], -1, qn[b], -1) if line in eng else (qp[b], qp[a], qn[a], qn[b])
-                    gap = cost[b] if line in eng else far[b]
-                    hb = max(hb, head[x] + cost[x] if x >= 0 else 0.0)
-                    ha = max(ha, head[y] + cost[y] if y >= 0 else 0.0, hb + gap)
-                    ta = max(ta, tail[z] + cost[a] if z >= 0 else 0.0)
-                    tb = max(tb, tail[w] + cost[b] if w >= 0 else 0.0, ta + gap)
-                    e = max(hb + tb, ha + ta)
-                    s += (e if min(head[a] + tail[a], head[b] + tail[b]) > end - 1e-6 else max(e, end)) / b0
-                rated.append((s + (10.0 if tabu.get((b, a), -1) > step else 0.0), a, b, line))
-            for s, a, b, line in sorted(rated):
-                both = [line] + ([x for x in ops[a]["bank"] if x in ops[b]["bank"]] if line in eng else [])
-                at = [(lines[x].index(a), lines[x].index(b)) for x in both]
-                if any(j != i + 1 for i, j in at):
-                    continue
-                for x, (i, j) in zip(both, at):
-                    lines[x][i], lines[x][j] = b, a
-                if all([link(x) for x in both]) and len(sequence()) == n:
-                    tabu[(a, b)] = step + CFG["tabu"]
-                    break
-                for x, (i, j) in zip(both, at):
-                    lines[x][i], lines[x][j] = a, b
-                    link(x)
-        return best
-
-    if not PLAN:
-        needs = [o["need"] for o in ops]
-        way = [0.0] * n
-        for k in range(n - 1, -1, -1):
-            way[k] = ops[k]["cost"] + ops[k]["lat"] + wake + max([way[j] for j in users[k]] or [0.0])
-        found = []
-        for lead, CFG["look"] in CFG["starts"]:
-            urge = [-w - o["b"] * lead for w, o in zip(way, ops)]
-            for it in range(CFG["iters"]):
-                got = plan(needs, users, urge, True)
-                found.append((sum(math.log(e) for e in polish(got[1], 1)[3]), got[1]))
-                back = plan(users, needs, [-(b + o["cost"]) for b, o in zip(got[2], ops)], False)
-                urge = [-(b + o["cost"]) for b, o in zip(back[2], ops)]
-        got = polish(min(found)[1], CFG["steps"])
-        PLAN.append((got[3][0], got[1], None, got[2]))
-    CFG["ms"], order, _b, more = PLAN[0]
-    for o, m in zip(ops, more):
-        o["need"].update(m)
+                st = max([st] + [tj for qq, (j, tj) in banks.get(a, {}).items() if qq != o["q"]])
+            cand.append((st, k))
+        st0, k0 = min(cand)
+        best, bst, c0 = k0, st0, ops[k0]["cost"]
+        for st, k in cand:
+            if ops[k]["q"] == ops[k0]["q"] and way[k] > way[best] and st <= st0 + CFG["look"] * c0 + 1e-9 + CFG["gain"] * (way[k] - way[k0]) * (st < st0 + c0):
+                best, bst = k, st
+        pool.remove(best)
+        o = ops[best]
+        ends = (bst + o["cost"], bst + o["cost"] + o["lat"], bst + o["cost"] + o["lat"] + wake)
+        if o["q"]:
+            free[o["q"]] = ends[0]
+        for a in o["bank"]:
+            use = banks.setdefault(a, {})
+            o["need"].update(j for qq, (j, tj) in use.items() if qq != o["q"])
+            use[o["q"]] = (best, ends[2])
+            if o["st"] and not o["sp"]:
+                opened.add(a)
+            if o["sp"]:
+                opened.discard(a)
+        order.append(best)
+        for j, how in users[best]:
+            at[j] = max(at[j], ends[how])
+            left[j] -= 1
+            if not left[j]:
+                pool.append(j)
 
     total = {"qv": 0, "qs": 0, "qt": 0, "qg": 0}
     known = {q: {} for q in eng}
@@ -822,7 +644,7 @@ def rank_program(g, core, T, topo):
         want = {}
         for d in o["need"]:
             p = ops[d]
-            if (d, k) in soft or p["sem"] == "none" or (p["q"] == q and q == "t"):
+            if p["sem"] == "none" or (p["q"] == q and q == "t"):
                 continue
             if p["val"] > want.get(p["sem"], (0, 0))[0]:
                 want[p["sem"]] = (p["val"], d)

from concourse.bass import DstId, RemoteDMATransfer
from concourse.mybir import AluOpType, ActivationFunctionType

OP = AluOpType
ID = ActivationFunctionType.Identity
RELU = ActivationFunctionType.Relu
SIGN = ActivationFunctionType.Sign
ROUNDS = 5
TH = 36.5
OFF = 2048.0
CW = 2048 + 32
NENG = 16
M0, M1, M2 = 1.5 * 2 ** 24, 1.5 * 2 ** 23, 1.5 * 2 ** 34
CFG = {"cut": {"a1": (48, 48, 32), "a0": (48, 48, 32), "b1": (56, 48), "b0": (48, 48, 32)},
       "cut0": {"a1": (40, 40), "a0": (56, 56)}, "cut4": {"b1": (56, 48), "b0": (64, 64)},
       "fold": "", "lf": 0.03, "l1": 5.5, "whole": (),
       "e_dp": "sv", "e_wt": "vs", "e_hd": "vs", "e_hr": "vs", "e_th": "vv", "e_wm": "v" * 8 + "s" * 8,
       "fill_g": ("cb", "gsb", "half"), "fill_v": ("ca", "hd", "qd_", "gs", "mp", "posw1", "pad", "cw", "cf_", "dlh0", "dlh1"),
       "chunk": 6, "look": 0.1, "gain": 0.03,
       "vf": 0.015, "wake": 0.25, "gam": 1.5, "pe": 0.41, "f": 1.05, "ls": 2.1, "lr": 3.0, "lx": 4.8, "lc": 2.6}
ORDER = {
    "first": "Gah1.0+ Gah1.1+ Gah0.1+ Gah0.0+ cw0 hd3.1+ hd0.1+ hd6.1+ cw2 WTh1+ cw1 cw3 sgh1+ Dph0+ hr1+ "
             "rl1 rl0+ qd_4+ qd0+ Gah1.2+ 1ah1.0+ 1ah1.2+ Gah0.2+ 1ah1.1+ Dph1+ 1ah0.1+ Wh1+ 1ah0.2+ 1ah0.0+ hb1+ Tah1+ ow1+ Zh1+ Wh0+ lb1+ hd6.0+ hd0.0+ hd3.0+",
    "round": "Gbh1.1 Gbh1.0 sgh0 Gah1.0+ Gbh0.2 Gbh0.0 Gbh0.1 Gah1.2+ Gah1.1+ Gah0.0+ SAh1 Gah0.1+ Gah0.2+ hd0.1+ hd6.1+ hd3.1+ SAh0 WTh1+ sgh1+ Dph0+ hr1+ "
             "R1h1 hb0 Gbh1.2 Tah0 WTh0 Eh1.0 Eh1.1 ow0 1bh1.2 hr0 2bh1.1 Zh0 q21 2bh1.0 lb0 1bh1.0 R1h0 1bh1.1 2bh1.2 ew 1ah1.0+ Eh0.0 Eh0.1 thh1 p4h1 "
             "1bh0.2 ns1 rp1 lw0 2bh0.0 Xh1 q20 2ah1.0+ 1bh0.1 1bh0.0 bk 2bh0.1 2bh0.2 Sh1 2ah1.2+ 1ah1.2+ 1ah1.1+ thh0 p4h0 2ah1.1+ ns0 rp0 Xh0 "
             "c0 1ah0.0+ c1 Dph1+ Sh0 c2 Wh1+ 1ah0.1+ c3 1ah0.2+ hb1+ c4 2ah0.1+ Tah1+ 2ah0.0+ c5 2ah0.2+ dlh1+ c6 ow1+ c7 Zh1+ Wh0+ lb1+ dlh0+ hd3.0+ hd6.0+ hd0.0+",
    "last": "cf3 cf2 Gbh1.0 sgh0 Gbh1.1 Gbh0.0 Gbh0.1 cf0 cf1 SAh1 SAh0 Yh1 Yh0 "
            "R1h1 Gbh1.2 hb0 WTh0 Tah0 Eh1.0 Eh1.1 ow0 2bh1.0 hr0 Zh0 2bh1.2 q21 lb0 1bh1.2 R1h0 1bh1.1 1bh1.0 2bh1.1 Eh0.0 ew Eh0.1 rp1 p4h1 "
            "1bh0.0 q20 1bh0.1 Xh1 2bh0.1 2bh0.0 Sh1 thh1 rp0 lw0 p4h0 thh0 ns1 Xh0 c0 dlh1+ c1 Sh0 ns0 c2 dlh0+ c3 c4 c5 c6 c7"}

SCRATCH = {
    "xw": ("sbuf", [128, 4096], "bfloat16"), "cw": ("sbuf", [128, CW], "float32"), "cf": ("sbuf", [128, CW], "float32"),
    "ci": ("sbuf", [128, 2048], "int32"), "ri": ("sbuf", [128, 256], "int32"),
    "pint": ("sbuf", [128, 4], "int32"), "pf": ("sbuf", [128, 16], "float32"),
    "cy": ("sbuf", [128, 256], "bfloat16"), "posw": ("sbuf", [128, 8, 4, 16], "bfloat16"),
    "ca": ("sbuf", [128, 8, 32], "bfloat16"), "cb": ("sbuf", [128, 8, 32], "bfloat16"),
    "gs": ("sbuf", [128, 8, 16], "bfloat16"), "gm": ("sbuf", [128, 8, 16], "bfloat16"),
    "gsb": ("sbuf", [128, 8, 16], "bfloat16"), "gp": ("sbuf", [128, 8], "bfloat16"),
    "pair": ("sbuf", [128, 8, 128], "bfloat16"), "wm": ("sbuf", [128, 16, 8, 16], "bfloat16"),
    "wt": ("sbuf", [128, 16], "bfloat16"), "w16": ("sbuf", [128, 6, 16], "float32"),
    "acc": ("sbuf", [128, 4], "float32"), "dump": ("sbuf", [128, 16], "float32"),
    "qd": ("sbuf", [128, 4, 192], "float32"), "hd": ("sbuf", [128, 176], "float32"), "hb": ("sbuf", [128, 176], "float32"),
    "ow": ("sbuf", [128, 16], "uint16"), "hr": ("sbuf", [128, 8, 16], "float16"),
    "ew": ("sbuf", [128, 8, 3, 16], "bfloat16"), "lw": ("sbuf", [128, 16], "uint16"),
    "la": ("sbuf", [128, 10, 128], "uint16"), "lb": ("sbuf", [128, 10, 128], "uint16"),
    "rq": ("sbuf", [128, 10, 128], "float16"), "rl": ("sbuf", [128, 10, 8, 16], "float16"),
    "sq": ("sbuf", [128, 10, 144], "bfloat16"), "sl": ("sbuf", [128, 10, 8, 16], "bfloat16"),
    "ns": ("sbuf", [128, 10, 64], "float16"), "nl": ("sbuf", [128, 10, 8, 8], "float16"),
    "tl": ("sbuf", [128, 10, 64], "float16"), "nf": ("sbuf", [128, 8, 2048], "bfloat16"), "zero": ("sbuf", [128, 64], "bfloat16"),
    "PE0": ("psum", [128, 8, 64], "float32"), "PE1": ("psum", [128, 8, 4, 16], "float32"),
}
for _n in ("ic", "gcl", "pd", "mask", "i4", "kc", "t1", "t2", "t3"):
    SCRATCH[_n] = ("sbuf", [128, 128], "float32")
for _n in ("blk", "ib", "nib", "pk", "nk", "n4", "ps", "ib4", "nb4", "ibk", "nbk", "one", "half", "s15", "pb", "gsp", "mp"):
    SCRATCH[_n] = ("sbuf", [128, 128], "bfloat16")
for _u in "01":
    for _n in ("X", "p4", "sg", "WT"):
        SCRATCH[_n + "h" + _u] = ("sbuf", [128, 128], "bfloat16")
    for _n in ("R1", "S"):
        SCRATCH[_n + "h" + _u] = ("sbuf", [128, 128], "float16")
    for _n in ("SA", "Z", "dl", "Y"):
        SCRATCH[_n + "h" + _u] = ("sbuf", [128, 128], "float32")
    for _n in ("Ga", "Gb", "Ma", "Mb"):
        SCRATCH[_n + "h" + _u] = ("sbuf", [128, 2048], "bfloat16")
    for _n in ("Na", "Nb", "E"):
        SCRATCH[_n + "h" + _u] = ("sbuf", [128, 1024], "bfloat16")
    SCRATCH["Dph" + _u] = ("sbuf", [128, 256], "bfloat16")
    SCRATCH["Wh" + _u] = ("sbuf", [128, 256], "float32")
    SCRATCH["thh" + _u] = ("sbuf", [128, 64], "bfloat16")
    SCRATCH["Tah" + _u] = ("sbuf", [128, 144], "float16")
    SCRATCH["PA" + _u] = ("psum", [128, 8, 64], "float32")
    SCRATCH["PB" + _u] = ("psum", [128, 8, 64], "float32")
    SCRATCH["PM" + _u] = ("psum", [128, 512], "float32")

DMAS = ["ldr", "ldx0", "ldx1", "ldc", "sty0", "sty1", "stc0", "stc1"]
SEMAPHORES = ["qv", "qs", "qt", "qg", "sent"] + ["arq%d" % d for d in (1, 2, 3)] + ["%s%d" % (c, k) for c in ("arl", "arr", "arn", "ars", "arf", "sf") for k in range(8)] + DMAS


def rank_program(g, core, T, topo):
    rank = T.rank_of(core)
    if rank is None:
        return
    n_ranks = len(T.cores)
    eng = {"v": g.vector, "s": g.scalar, "t": g.tensor, "g": g, "y": g.sync}
    ops, lastw, readers, tag, now, sent = [], {}, {}, {}, [-1], []

    def add(q, fns, reads, writes, cost, sem=None, val=0, lat=0.0, deps=()):
        k = len(ops)
        need = set(deps)
        for a in reads:
            if a in lastw:
                need.add(lastw[a])
        for a in writes:
            if a in lastw:
                need.add(lastw[a])
            need.update(readers.get(a, ()))
        bank = sorted(set(a.split(":")[0] for a in list(reads) + list(writes) if a[0] == "P"))
        for a in reads:
            readers.setdefault(a, []).append(k)
        for a in writes:
            lastw[a] = k
            readers[a] = []
        need.discard(k)
        if q in ("v", "s") and writes:
            nm = writes[0][:2] + str(int(writes[0][2:]) % 2) if writes[0][:2] in ("lb", "q2", "rp", "ns", "nl") else writes[0]
            if nm in ("cw", "cf"):
                nm = "c%d" % sum((now[0], "c%d" % j) in tag for j in range(8))
            tag[(now[0], nm)] = k
        ind = any(a in reads for a in ("xw", "ow0", "ow1", "lw0"))
        ops.append({"q": q, "f": fns, "need": need, "cost": cost + (0.05 if ind else 0.0), "sem": sem, "val": val, "lat": lat, "bank": bank,
                    "st": False, "sp": False, "ind": ind})
        return k

    def dur(n, c=1.0):
        return CFG["vf"] + max(64.0, n * c) * 0.00083 * CFG["f"]

    def size(ap):
        r = 1
        for s in ap.shape[1:]:
            r *= s
        return r

    def tt(out, a, b, op, c=None, extra=()):
        ps = a[0][0] == "P" or b[0][0] == "P"
        n = size(out[1])
        return add("v", [lambda: g.vector.tensor_tensor(out=out[1], in0=a[1], in1=b[1], op=op)], [a[0], b[0]] + list(extra), [out[0]], dur(n, c or (1 if ps else 2)))

    def ts(out, a, s1, op0, s2=None, op1=None, c=1.0, extra=()):
        n = size(out[1])
        if op1 is None:
            f = lambda: g.vector.tensor_scalar(out=out[1], in0=a[1], scalar1=s1, scalar2=None, op0=op0)
        else:
            f = lambda: g.vector.tensor_scalar(out=out[1], in0=a[1], scalar1=s1, scalar2=s2, op0=op0, op1=op1)
        return add("v", [f], [a[0]] + list(extra), [out[0]], dur(n, c))

    def cp(out, a, c=1.0, extra=()):
        return add("v", [lambda: g.vector.tensor_copy(out=out[1], in_=a[1])], [a[0]] + list(extra), [out[0]], dur(size(out[1]), c))

    def scan(out, a, b, op0, op1, c=1.0, extra=(), first=0.0):
        return add("v", [lambda: g.vector.tensor_tensor_scan(out=out[1], data0=a[1], data1=b[1], initial=first, op0=op0, op1=op1)],
                   [a[0], b[0]] + list(extra), [out[0]], dur(size(out[1]), c))

    def act(out, a, func, bias=0.0, scale=1.0, c=1.0, extra=(), acc=None):
        kw = {"accum_out": acc[1]} if acc else {}
        return add("s", [lambda: g.scalar.activation(out=out[1], in_=a[1], func=func, bias=bias, scale=scale, **kw)],
                   [a[0]] + list(extra), [out[0]] + ([acc[0]] if acc else []), dur(size(out[1]), c) + (0.02 if acc else 0.0))

    def select(key, out, a, pat, op, v, base, step):
        return add("g", [lambda: g.affine_select(out, a[1], pat, op, v, base, step)], [a[0]], [key], (0.17 + 0.00166 * size(out)) * CFG["f"])

    def iota(name, pat, base):
        add("g", [lambda: g.iota(T[name][:], pat, base, 0, allow_small_or_imprecise_dtypes=True)], [], [name], (0.13 + size(T[name][:]) * 0.00166) * CFG["f"])

    def fill(key, ap, v):
        n = size(ap)
        if key in CFG["fill_v"]:
            return add("v", [lambda: g.vector.memset(ap, v)], [], [key], dur(n, 0.5 if key in ("ca", "cb", "mp", "half", "posw1", "pad") else 1.0))
        if key in CFG["fill_g"]:
            return select(key, ap, ("cy", T.cy[:, 0:n]), [[0, n]], OP.is_gt, v, 0, 0)
        return act((key, ap), ("cy", T.cy[:, 0:n]), ID, v, 0.0)

    def lin(e, out, a, mul, add_, extra=()):
        if e == "s":
            return act(out, a, ID, add_, mul, extra=extra)
        return ts(out, a, mul, OP.mult, add_, OP.add, extra=extra)

    def mm(items, reads, writes, st=True, sp=True, c=1):
        fns, cost = [], 0.0
        if not st and not sp and len(items) > CFG["chunk"]:
            mm(items[CFG["chunk"]:], reads, writes, st, sp, c)
            items = items[:CFG["chunk"]]
        for n, (o, l, r) in enumerate(items):
            a, b = st and n == 0, sp and n == len(items) - 1
            fns.append(lambda o=o, l=l, r=r, a=a, b=b: g.tensor.matmul(out=o, lhsT=l, rhs=r, start=a, stop=b))
            cost += max(min(64, size(l)), size(r)) * 0.001 * CFG["pe"] * CFG["f"] * c
        if not st and not sp:
            reads, writes = list(reads) + list(writes), []
        k = add("t", fns, reads, writes, cost, lat=0.05)
        ops[k]["st"], ops[k]["sp"] = st, sp
        return k

    def B(name, u=None):
        nm = name if u is None else "%sh%d" % (name, u)
        return (nm, T[nm][:])

    def route(d):
        to = T.cores[(rank + d) % n_ranks]
        rid, pid, _s = topo.addr(to)
        m = 0
        for e in topo.engines(core, to)[:NENG]:
            m |= 1 << e
        return rid, pid, m

    def send(src, dst, sem, d=1, extra=()):
        rid, pid, m = route(d)
        sd = add("g", [lambda: g.remote_dma(out_ap=dst[1], in_ap=src[1], remote_sem=T.sem[sem], local_sem=T.sem.sent, pid=pid, routing_id=rid, dma_engine_mask=m)],
                 [src[0]] + list(extra), [], CFG["l1"] if sem == "arq1" else 0.3, "none", 0, CFG["ls"], deps=[o for o in sent if sem != "arq1"])
        if sem == "arq1":
            sent.append(sd)
        add(None, [], [], [dst[0]], 0.0, sem, NENG, 0.0, deps=[sd])

    g.sync.dma_start(T.ri[:], T.r0[:]).then_inc(T.sem.ldr, 16)
    g.scalar.dma_start(T.xw[0:64, :], T.x[0:64, :]).then_inc(T.sem.ldx0, 16)
    g.sync.dma_start(T.xw[64:128, :], T.x[64:128, :]).then_inc(T.sem.ldx1, 16)
    g.sync.dma_start(T.ci[:], T.c0[:]).then_inc(T.sem.ldc, 16)
    add(None, [], [], ["ri"], 0.0, "ldr", 16, CFG["lr"])
    add(None, [], [], ["xw"], 0.0, "ldx0", 16, CFG["lx"])
    add(None, [], [], ["xw_"], 0.0, "ldx1", 16, CFG["lx"])
    add(None, [], [], ["ci"], 0.0, "ldc", 16, CFG["lx"] + CFG["lc"])

    add("g", [lambda: g.iota(T.pint[:, 0:1], [[0, 1]], 0, 1)], [], ["pint"], 0.14)
    iota("cy", [[0, 8], [16, 8], [2, 4]], 2)
    iota("ic", [[0, 8], [1, 16]], 0)
    iota("gcl", [[1, 8], [0, 16]], 0)
    iota("one", [[0, 128]], 1)
    iota("pd", [[1, 8], [1, 16]], 1)
    for u in (0, 1):
        cp(("la%d" % u, T.la[:, u, :]), ("ri", T.ri[:, 128 * u:128 * u + 128]))

    def col(j):
        return T.pf[:, j:j + 1]

    def C(j):
        return ("pf%d" % j, col(j))
    ts(("pi1", T.pint[:, 1:2]), ("pint", T.pint[:, 0:1]), 15, OP.bitwise_and)
    ts(("pi2", T.pint[:, 2:3]), ("pint", T.pint[:, 0:1]), 4, OP.arith_shift_right)
    cp(C(0), ("pi1", T.pint[:, 1:2]))
    cp(C(1), ("pi2", T.pint[:, 2:3]))
    ic, gcl = B("ic"), B("gcl")
    ts(B("mask"), ic, col(0), OP.is_equal, extra=["pf0"])
    ts(B("blk"), gcl, col(1), OP.is_equal, extra=["pf1"])
    r15 = ("mask", T.mask[:, 15:16])
    act(C(2), C(0), ID, 127.0, -8.0)
    act(C(4), r15, ID, 4096.0, -4096.0)
    act(C(14), r15, ID, -OFF, 4096.0)
    act(C(5), r15, ID, -1.0, 1.0 - 2.0 ** -13)
    act(C(6), C(5), ID, 0.0, 4096.0)
    act(C(12), C(5), ID, 0.0, OFF)
    act(C(15), r15, ID, -1.0, -8191.0)
    select("i4", T.i4[:], B("one"), [[-1, 128]], OP.is_equal, 0.0, 0, 1)
    for nm, w in (("ib", 1.0), ("nib", -1.0), ("pk", 1024.0), ("nk", -1024.0), ("n4", -988.0), ("ps", 241.0), ("ib4", 4096.0), ("nb4", -4096.0)):
        act(B(nm), B("i4"), ID, 0.0, w)
    act(B("ibk"), B("i4"), ID, 0.0, col(4), extra=["pf4"])
    act(B("nbk"), B("i4"), ID, 0.0, col(14), extra=["pf14"])
    act(B("s15"), B("blk"), ID, 0.0, r15[1], extra=["mask"])
    act(B("gs"), B("blk"), ID)
    fill("gs", T.gs[:, :, 8], 0.0)
    act(B("gsb"), B("blk"), ID)
    fill("gsb", T.gsb[:, :, 1:3], 0.0)
    act(("gsb", T.gsb[:, :, 0:5:4]), ("gs", T.gs[:, :, 0:2]), ID, 0.0, -1.0)
    act(B("gp"), ("blk", T.blk[:, 0:128:16]), ID, 0.0, 2.0)
    act(B("gm"), B("blk"), ID, 0.0, -2.0)
    for ap, v in ((T.ca[:], 0.0), (T.ca[:, :, 1:32:4], -2048.0), (T.ca[:, :, 2:32:4], -2048.0), (T.ca[:, :, 0], 1536.0)):
        fill("ca", ap, v)
    for u in (0, 1):
        ts(B("Ta", u), ("cy", T.cy[:, 0:144]), 0.0, OP.mult, c=0.5)
    fill("hd", T.hd[:], M0)
    for j, v in ((2, -M0), (4, -31.5 / 4096), (5, M1 / 4096), (8, -1023.5), (9, M2), (10, -M2)):
        fill("hd", T.hd[:, j:176:11], v)
    select("gsp", T.gsp[0:32, :], ("one", T.one[0:32, :]), [[1, 8], [0, 16]], OP.is_equal, 0.0, 0, -1)
    fill("qd_", T.qd[:, 0, 0:176], 1.0)
    for j, v in ((0, 0.0), (3, -1.0), (5, 1.0 / 64), (7, 4096.0)):
        fill("qd_", T.qd[:, 0, j:176:11], v)
    act(B("kc"), B("ic"), ID, r15[1], 0.0, extra=["mask"])
    act(C(7), C(0), ID, 16.0)
    ts(B("t2"), B("pd"), col(0), OP.is_equal, extra=["pf0"])
    ts(B("t3"), B("pd"), col(7), OP.is_equal, extra=["pf7"])
    tt(B("t2"), B("t2"), B("t3"), OP.add)
    tt(B("pb"), B("mask"), B("t2"), OP.subtract)
    for k in range(8):
        ts(("pair%d" % k, T.pair[:, k, :]), B("pb"), T.blk[:, 16 * k:16 * k + 1], OP.mult, c=0.5, extra=["blk"])
    ts(C(8), C(0), col(1), OP.add, 1.0, OP.add, extra=["pf1"])
    ts(C(9), C(8), 16.0, OP.is_ge, -16.0, OP.mult)
    act(C(10), C(8), ID, col(9), extra=["pf9"])
    r16 = ("ic", T.ic[:, 0:16])

    def W(j):
        return ("w16%d" % j, T.w16[:, j, :])
    ts(W(0), r16, col(0), OP.is_gt, 2.0 ** -10, OP.max, extra=["pf0"])
    ts(W(1), r16, col(10), OP.is_gt, 2.0 ** -10, OP.max, extra=["pf10"])
    tt(W(2), W(0), W(1), OP.max)
    scan(W(3), W(2), ("one", T.one[:, 0:16]), OP.mult, OP.mult, first=2.0 ** 85)
    tt(W(4), W(0), W(1), OP.not_equal)
    act(W(5), W(4), ID, -1.0, 33.0)
    act(B("wt"), W(5), ID, 0.0, T.w16[:, 3, 15:16], extra=["w163"])
    fill("half", T.half[:], 0.5)
    if CFG["fold"]:
        iota("zero", [[0, 64]], 0)
    fill("pad", T.sq[:, :, 128:144], 0.5)
    for ap, v in ((T.cb[:], -157.0), (T.cb[:, :, 1:32:4], 1024.0), (T.cb[:, :, 3:32:4], -1024.0), (T.cb[:, :, 29], 512.0), (T.cb[:, :, 0:31:30], -2048.0)):
        fill("cb", ap, v)
    fill("mp", T.mp[:], 1.0e9)
    fill("mp", T.mp[:, 0:128:16], -0.5)
    fill("mp", T.mp[:, 15:128:16], -0.5)
    fill("cw", T.cw[:, 2048:CW], 0.0)
    fill("cf_", T.cf[:, 2048:CW], 0.0)
    for i in range(16):
        if CFG["e_wm"][i] == "v":
            ts(("wm%d" % i, T.wm[:, i, :, :]), B("blk"), T.mask[:, i:i + 1], OP.mult, c=0.5, extra=["mask"])
        else:
            act(("wm%d" % i, T.wm[:, i, :, :]), B("blk"), ID, 0.0, T.mask[:, i:i + 1], extra=["mask"])
    wms = ["wm%d" % i for i in range(16)]
    for u in (0, 1):
        fill("dlh%d" % u, T["dlh%d" % u][:], 0.0)
    ts(B("t1"), ic, col(0), OP.is_lt, extra=["pf0"])
    tt(("posw0", T.posw[:, :, 0, :]), B("t1"), B("mask"), OP.subtract)
    act(("posw2", T.posw[:, :, 2, :]), ("posw0", T.posw[:, :, 0, :]), ID)
    fill("posw1", T.posw[:, :, 1:4:2, :], 1.0)
    iota("dump", [[0, 8], [16, 2]], 2048)
    act(B("dump"), B("dump"), ID, col(0), extra=["pf0"])
    for k in range(4):
        act(("cw%d" % k, T.cw[:, 512 * k:512 * k + 512]), ("ci", T.ci[:, 512 * k:512 * k + 512]), ID, 0.0, col(5), extra=["pf5"])
    cws = ["cw%d" % k for k in range(4)]
    bk = ("bk", T.hd[:, 7:176:11])

    def gather(u, st, t, lst):
        G, M, N = (T["%s%sh%d" % (n, st, u)] for n in "GMN")
        win, slot = T.xw[:, 0:4096], 2 * t + u
        cut = CFG["cut0" if t == 0 and st == "a" else "cut4" if t == ROUNDS - 1 and st == "b" else "cut"][st + str(u)]
        parts = [("s", sum(cut[:n]), sum(cut[:n + 1])) for n in range(len(cut))] + ([("v", sum(cut), 128)] if sum(cut) < 128 else [])
        kg, km, kn = [], [], []
        for n, (q, a, b) in enumerate(parts):
            key = "G%sh%d.%d" % (st, u, n)
            kg.append(key)
            o, i = G[:, 16 * a:16 * b], win.indirect(T[lst][:, slot, a:b])
            more = ["xw_", "%s%d" % (lst, slot), "done%s%d.%d" % (st, u, t - 1)]
            if q == "s":
                act((key, o), ("xw", i), ID, c=CFG["gam"], extra=more)
            else:
                cp((key, o), ("xw", i), c=CFG["gam"], extra=more)
        for step, D, ks in ((2, N, kn), (1, M, km)):
            if step == 2 and t == 0 and st == "a":
                continue
            if step == 2 and st == "b" and t < ROUNDS - 1 and str(u) in CFG["fold"]:
                rid, pid, m = route(1)
                sd = []
                for n, (q, a, b) in enumerate(parts):
                    tr = RemoteDMATransfer(dst_ids=[DstId(rid=rid, pnc=pid)], dma_engine_mask=m, remote_sem=T.sem["arf%d" % slot],
                                           srcs=[G[:, 16 * a:16 * b - 2], G[:, 16 * a + 2:16 * b]], dsts=[T.nf[:, slot, 16 * a:16 * b - 2]], alu_op=3)
                    sd.append(add("g", [lambda tr=tr: g.remote_dma_fused([tr], local_sem=T.sem["sf%d" % slot])], [kg[n]], [], 0.3, "none", 0, CFG["ls"] + (b - a) * CFG["lf"]))
                add(None, [], [], ["nf%d" % (slot + 2)], 0.0, "arf%d" % slot, NENG * len(sd), 0.0, deps=sd)
                add(None, [], [], ["doneb%d.%d" % (u, t)], 0.0, "sf%d" % slot, NENG * len(sd), 0.0, deps=sd)
                continue
            whole = step == 2 and st + str(u) in CFG["whole"]
            for n, (q, a, b) in enumerate([("v", 0, 128)] if whole else parts):
                key = "%d%sh%d.%d" % (step, st, u, n)
                ks.append(key)
                a, b = 16 * a, 16 * b
                scan((key, D[:, a // step:b // step - 1]), (kg[n], G[:, a:b - step:step]), (kg[n], G[:, a + step:b:step]), OP.max, OP.min, 0.5, extra=kg if whole else ())
        return kg, km, kn

    def sums(P, kd, D, step, items, keys, last=False):
        calls = [(P[:, :, cols], D[:, p:128 * step:step], w) for cols, p, w in items]
        mm(calls[:-1] if last else calls, keys, [kd], st=False, sp=False)
        if last:
            mm(calls[-1:], keys, [kd], st=False)

    def first_fail(t, u):
        k = 2 * t + u
        now[0] = t
        PA, PM, G, M, N = T["PA%d" % u], T["PM%d" % u], T["Gah%d" % u], T["Mah%d" % u], T["Nah%d" % u]
        kd, kr = "PA%d:D" % u, "rl%d" % k
        ky, Y = "PM%d:Y" % u, PM[:, 0:256]
        mm([(Y, T.ib[:], T.cy[:])] + [(PM[:, j:256:4], T.ib[:], T.rl[:, k, :, (14 if j else 15)::-2]) for j in range(4)], ["ib", "cy", kr], [ky])
        kg, km, kn = gather(u, "a", t, "la")
        mm([(PA[:, :, 0:32], T.ib[:], T.ca[:])], ["ib", "ca", "la%d" % k, "sgh%d" % u], [kd], sp=False)
        if t:
            c0, c1 = T.sl[:, k, :, 15::-2], T.sl[:, k, :, 14:0:-2]
            mm([(PA[:, :, 0:32:4], T.nk[:], c0), (PA[:, :, 1:32:4], T.pk[:], c0), (PA[:, :, 2:32:4], T.pk[:], c0), (PA[:, :, 4:32:4], T.pk[:], c1),
                (PA[:, :, 5:32:4], T.pk[:], c1), (PA[:, :, 6:32:4], T.nk[:], c1)], ["sl%d" % k, "pk", "nk"], [kd], st=False, sp=False)
        items = []
        for p in range(16):
            z = 4 * (7 - p // 2)
            if p % 2:
                items.append((slice(z, z + 4), p, T.gs[:, :, 7:11]))
            else:
                n = 5 if p else 3
                items.append((slice(z + 1, z + 1 + n), p, T.gs[:, :, 3:3 + n]))
        sums(PA, kd, G, 16, items, kg + ["gs"])
        if t:
            sums(PA, kd, N, 8, [(4 * (7 - i) + 1, i, T.gm[:, :, 0]) for i in range(7)], kn + ["gm"])
            if str(u) in CFG["fold"]:
                kf, F = "PM%d:F" % u, PM[:, 384:448]
                mm([(F, T.ib[:], T.zero[:])] + [(PM[:, 384 + i:448:8], T.nf[:, k - 2, 2 * i:2048:16], T.gp[:]) for i in range(7)],
                   ["ib", "zero", "gp", "nf%d" % k], [kf])
                tt(("nl%d" % k, T.nl[:, k, :, :]), (kf, F), ("tl%d" % k, T.tl[:, k, :]), OP.is_ge)
            nl = T.nl[:, k, :, 7::-1]
            mm([(PA[:, :, j:32:4], w[:], nl) for j, w in enumerate((T.nk, T.pk, T.pk, T.nk))], ["nl%d" % k, "pk", "nk"], [kd], st=False, sp=False)
        items = []
        for p in range(15):
            z = 4 * (7 - p // 2)
            items.append((z, p, T.gm[:, :, 0]) if p % 2 else (slice(z + 2, z + 4), p, T.gm[:, :, 0:2]))
        sums(PA, kd, M, 16, items, km + ["gm"], True)
        lin(CFG["e_dp"][u], B("Dp", u), (kd, PA[:, :, 0:32]), 256.0, -256.0 * TH)
        lastw["donea%d.%d" % (u, t)] = scan(B("W", u), B("Dp", u), (ky, Y), OP.max, OP.min)

    def moved(u, near, rp, out, kout, last):
        kf, F = "PB%d:F" % u, T["PB%d" % u][:, :, 32:40]
        mm([(F, T.ib4[:], rp[2]), (F, T.nb4[:], rp[3])], [rp[0], "ib4", "nb4"], [kf])
        tt(("dlh%d" % u, T["dlh%d" % u][:, 1:128:2]), (kf, F), near, OP.mult)
        mm([(out, T["dlh%d" % u][:], T.i4[:])], ["dlh%d" % u, "i4"], [kout], sp=False, c=4)
        mm([(out, rp[1], T.ib4[:])], ["ib4", rp[0]], [kout], st=False, sp=last)

    def stage_a(t, u):
        k = 2 * t + u
        PA, PB, PM = T["PA%d" % u], T["PB%d" % u], T["PM%d" % u]
        Ta, sg = T["Tah%d" % u], T["sgh%d" % u]
        d = t % n_ranks
        a, b = 88 * u, 88 * u + 88
        end = ("Wh%d" % u, T["Wh%d" % u][:, 31:256:32])
        for j in (0, 3, 6):
            lin(CFG["e_hd"][u], ("hd%d.%d" % (j, u), T.hd[:, a + j:b:11]), end, 1.0, 0.0, extra=["hd"])
        scan(("hb%d" % u, T.hb[:, a:b]), ("qd%d" % d, T.qd[:, d, a:b]), ("bk", T.hd[:, a:b]), OP.mult, OP.add, extra=["qd_4"] + ["hd%d.%d" % (j, u) for j in (0, 3, 6)])
        tt(("Tah%d" % u, Ta[:, 15:128:16]), ("hb%d" % u, T.hb[:, a + 7:b:11]), ("hb%d" % u, T.hb[:, a + 10:b:11]), OP.subtract)
        kl, L = "PM%d:H" % u, PM[:, 256:320]
        mm([(L, Ta[:, 15 - i:143 - i], T.wm[:, i, :, 0:8]) for i in range(16)], ["Tah%d" % u] + wms, [kl])
        ow = ("ow%d" % u, T.ow[:, 8 * u:8 * u + 8])
        cp(ow, (kl, PM[:, 256:320:8]))
        lin(CFG["e_hr"][u], ("hr%d" % u, T.hr[:, 4 * u:4 * u + 4, :]), (kl, L), 1.0 / 4096, 0.0)
        k1, P1 = "PA%d:U" % u, PA[:, :, 48:64]
        mm([(PA[0:8, :, 48:64], end[1], T.i4[:])], [end[0], "i4"], [k1], c=4)
        wt = ("WTh%d" % u, T["WTh%d" % u][0:8, :])
        lin(CFG["e_wt"][u], wt, (k1, PA[0:8, :, 48:64]), 1.0, 0.0)
        mm([(P1, T.gsp[0:8, :], wt[1])], ["gsp", wt[0]], [k1])
        j = 2 * (t % 2) + u
        act(B("sg", u), (k1, P1), SIGN, col(2), -1.0, extra=["pf2"], acc=("acc%d" % j, T.acc[:, j:j + 1]))
        kk, K = "PB%d:K" % u, PB[:, :, 48:64]
        if t:
            moved(u, ("nl%d" % k, T.nl[:, k, :, :]), ("rl%d" % k, T.rl[:, k, :, :], T.rl[:, k, :, 0:16:2], T.rl[:, k, :, 1:16:2]), K, kk, False)
        else:
            mm([(K, T.rl[:, k, :, :], T.ib4[:])], ["ib4", "rl%d" % k], [kk], sp=False)
        mm([(K, T.nbk[:], T.one[:])], ["nbk", "one"], [kk], st=False, sp=False)
        mm([(K, T.ibk[:], sg[:])], ["ibk", "sgh%d" % u], [kk], st=False)
        tt(B("Z", u), ("cw", T.cw[:, 0:CW].indirect(ow[1])), B("sg", u), OP.mult, c=CFG["gam"], extra=[ow[0]] + cws)
        lb = ("lb%d" % k, T.lb[:, k, :])
        tt(lb, B("Z", u), (kk, K), OP.max)
        ts(B("R1", u), lb, -OFF, OP.add, 1.0 / 4096, OP.mult, c=0.5)
        if t < ROUNDS - 1:
            send(lb, ("la%d" % (k + 2), T.la[:, k + 2, :]), "arl%d" % k)
        R1, E = T["R1h%d" % u], T["Eh%d" % u]
        kh, H = "PM%d:H" % u, PM[:, 256:384]
        for b, (P, kp) in enumerate(((T.PE0, ["PE0:E"]), (PA, ["PA%d:D" % u, k1]))):
            for j in range(4):
                mm([(P[:, 2 * j:2 * j + 2, :], T.pair[:, 4 * b + j, :], R1[:])], ["R1h%d" % u, "pair%d" % (4 * b + j)], kp)
            ts(("Eh%d.%d" % (u, b), E[:, 512 * b:512 * b + 512]), (kp[0], P[:]), 0.0, OP.is_equal, extra=kp[1:])
        for j in range(8):
            mm([(PM[:, 256 + 16 * j:272 + 16 * j], E[:, 128 * j:128 * j + 128], T.wt[:])], ["Eh%d.%d" % (u, j // 4), "wt"], [kh])
        q2 = ("q2%d" % k, T.sq[:, k, 0:128])
        ts(q2, (kh, H), 0.0, OP.is_le, -0.5, OP.add)
        if t < ROUNDS - 1:
            send(q2, ("sl%d" % (k + 2), T.sl[:, k + 2, :, :]), "ars%d" % k)
        mm([(H, R1[:], T.ib[:]), (H, T.ib[:], T.half[:]), (H, T.nib[:], q2[1])], ["R1h%d" % u, "ib", "half", "nib", q2[0]], [kh])
        rp = ("rp%d" % k, T.rq[:, k, :])
        scan(rp, q2, (kh, H), OP.max, OP.min)
        if t < ROUNDS - 1:
            send(rp, ("rl%d" % (k + 2), T.rl[:, k + 2, :, :]), "arr%d" % k)

    def stage_b(t, u):
        k = 2 * t + u
        PB, PM, G, M, N = T["PB%d" % u], T["PM%d" % u], T["Gbh%d" % u], T["Mbh%d" % u], T["Nbh%d" % u]
        kg, km, kn = gather(u, "b", t, "lb")
        kd, kq, kp = "PB%d:D" % u, "q2%d" % k, "rp%d" % k
        c0, c1 = T.sq[:, k, 1:128:2], T.sq[:, k, 2:130:2]
        mm([(PB[:, :, 0:32], T.ib[:], T.cb[:])], ["ib", "cb", "lb%d" % k], [kd], sp=False)
        mm([(PB[:, :, 1:32:4], T.n4[:], c0), (PB[:, :, 3:32:4], T.pk[:], c0), (PB[:, :, 1:32:4], T.n4[:], c1),
            (PB[:, :, 3:32:4], T.nk[:], c1), (PB[:, :, 0:32:2], T.ps[:], T.sq[:, k, 0:128])], [kq, "pad", "pk", "nk", "n4", "ps"], [kd], st=False, sp=False)
        items = []
        for p in range(15):
            z = 4 * (p // 2)
            if p % 2:
                items.append((slice(z + 2, z + 5), p, T.gs[:, :, 3:6]))
            else:
                a, b = (4 if p == 0 else 0), (4 if p == 14 else 7)
                items.append((slice(z - 3 + a, z - 3 + b), p, T.gsb[:, :, a:b]))
        sums(PB, kd, G, 16, items, kg + ["gs", "gsb"])
        if kn:
            sums(PB, kd, N, 8, [(4 * i + 1, i, T.gp[:]) for i in range(7)], kn + ["gp"])
        items = []
        for p in range(14):
            z = 4 * (p // 2)
            items.append((z + 4, p, T.gm[:, :, 0]) if p % 2 else (slice(z + 2, z + 4), p, T.gm[:, :, 0:2]))
        sums(PB, kd, M, 16, items, km + ["gm"], True)
        cp(B("p4", u), (kd, PB[:, :, 0:32:2]))
        scan(B("X", u), B("mp"), B("p4", u), OP.min, OP.max, 0.5)
        ns = ("ns%d" % k, T.ns[:, k, :])
        if CFG["e_th"][u] == "s":
            act(B("th", u), (kd, PB[:, :, 3:32:4]), RELU, -TH * 8192.0, 8192.0)
        else:
            ts(B("th", u), (kd, PB[:, :, 3:32:4]), TH, OP.is_gt, 4096.0, OP.mult)
        if not kn:
            tt(ns, B("th", u), (kd, PB[:, :, 1:32:4]), OP.subtract)
            send(ns, ("tl%d" % (k + 2), T.tl[:, k + 2, :]), "arn%d" % k)
        else:
            tt(ns, (kd, PB[:, :, 1:32:4]), B("th", u), OP.is_ge)
            if t < ROUNDS - 1:
                send(ns, ("nl%d" % (k + 2), T.nl[:, k + 2, :, :]), "arn%d" % k)
        kh, H = "PM%d:H" % u, PM[:, 256:384]
        mm([(H, T.ib[:], T.rq[:, k, :]), (H, T.nib[:], T.half[:])], [kp, "ib", "half", "nib"], [kh], sp=False)
        mm([(H, T.nib[:], T["Xh%d" % u][:])], ["nib", "Xh%d" % u], [kh], st=False)
        scan(B("S", u), B("X", u), (kh, H), OP.min, OP.max)
        mm([(H, T["Sh%d" % u][:], T.ib[:])], ["Sh%d" % u, "ib"], [kh])
        if t < ROUNDS - 1:
            act(B("SA", u), (kh, H), ID, col(12), col(6), extra=["pf6", "pf12"])
        else:
            act(B("SA", u), (kh, H), ID, OFF, 4096.0)
            kk, K = "PB%d:K" % u, PB[:, :, 48:64]
            now[0] = t + 1
            moved(u, ns, (kp, T.rq[:, k, 0:128], T.rq[:, k, 0:128:2], T.rq[:, k, 1:128:2]), K, kk, True)
            now[0] = t
            act(B("Y", u), (kk, K), ID, OFF)
            add("y", [lambda: g.sync.dma_start(T.yr[:, 128 * u:128 * u + 128], T["Yh%d" % u][:])], ["Yh%d" % u], [], 0.1, "sty%d" % u, 16, 5.3)

    def count(t):
        P, c = T.PE1[:, 0, 3, 2:3], 2 * (t % 2)
        mm([(P, T.kc[:], T.acc[:, c + u:c + u + 1]) for u in (0, 1)], ["kc", "acc%d" % c, "acc%d" % (c + 1)], ["PE1:E"], c=4)
        d = (t + 1) % n_ranks
        ts(bk, ("qd%d" % d, T.qd[:, d, 176:192]), P, OP.add, -0.5, OP.mult, extra=["PE1:E"])

    def winners():
        P, kp = T.PE1, "PE1:E"
        mm([(P[:], T.ib[:], T.posw[:])], ["ib", "posw0", "posw1", "posw2"], [kp], sp=False)
        for u in (0, 1):
            mm([(P[:, 4 * u:4 * u + 4, s:4:2, :], T.s15[:], T["sgh%d" % u][:]) for s in (0, 1)], ["s15", "sgh%d" % u], [kp], st=False, sp=False)
        mm([(P[:, :, s, 8 * r:8 * r + 8], T.nib[:], T.hr[:, :, 8 * min(s, 1):8 * min(s, 1) + 8]) for s in range(3) for r in (0, 1)],
           ["nib", "hr0", "hr1"], [kp], st=False, sp=False)
        for a in range(0, 16, 4):
            mm([(P[:, :, 0:3, i], T.wm[:, i, :, :], T.hr[:, :, 0:12:4]) for i in range(a, a + 4)], ["hr0", "hr1"] + wms, [kp], st=False, sp=a == 12)
        ts(B("ew"), (kp, P[:, :, 0:3, :]), 0.0, OP.is_equal)
        Q = P[:, :, 3, 0:2]
        mm([(Q, T.ib4[:], T.hr[:, :, 0:16:8])], ["hr0", "hr1", "ib4", "ew"], [kp], sp=False)
        mm([(Q, T.ib4[:], T.ew[:, :, 0:2, i]) for i in range(16)] + [(P[:, :, 3, 1], T.ib4[:], T.ew[:, :, 2, i]) for i in range(15)], ["ib4", "ew"], [kp], st=False, sp=False)
        mm([(P[:, :, 3, 1], T.ib4[:], T.ew[:, :, 2, 15])], ["ib4", "ew"], [kp], st=False)
        tt(("lw0", T.lw[:]), (kp, Q), B("dump"), OP.min)

    def scatter(t, u):
        win, key = (T.cw, "cw") if t < ROUNDS - 1 else (T.cf, "cf")
        for c in range(3, -1, -1):
            j = 8 * u + 2 * c
            o = win[:, 0:CW].indirect(T.lw[:, j:j + 2])
            add("v", [lambda o=o, c=c: g.vector.tensor_copy(out=o, in_=T["SAh%d" % u][:, 32 * c:32 * c + 32])],
                ["SAh%d" % u, "lw0"] + cws + ["cf_", "cf0", "cf1", "cf2", "cf3"], [key], CFG["vf"] + 32 * 3.5 * 0.00083 * CFG["f"])

    halves = (1, 0)
    for u in halves:
        ts(B("R1", u), ("la%d" % u, T.la[:, u, :]), -OFF, OP.add, 1.0 / 4096, OP.mult, c=0.5)
        H = ("PM%d:H" % u, T["PM%d" % u][:, 256:384])
        mm([(H[1], T["R1h%d" % u][:], T.ib[:])], ["R1h%d" % u, "ib"], [H[0]])
        cp(("rl%d" % u, T.rl[:, u, :, :]), H)
        first_fail(0, u)
    dst = ("rl0", T.rl[:, 0:2, :, 15])
    ts(("qd_4", T.qd[:, 0, 4:176:11]), dst, 4096.0, OP.mult, OFF, OP.add, extra=["rl1", "qd_"])
    ts(("qd0", T.qd[:, 0, 176:192]), dst, -262144.0, OP.mult, -2 * (65536.0 + 1024.0 - M1), OP.add, extra=["rl1"])
    ts(bk, dst, 131072.0, OP.mult, 65536.0 - M1, OP.add, extra=["rl1", "hd"])
    for d in range(1, n_ranks):
        send(("qd0", T.qd[:, 0, :]), ("qd%d" % d, T.qd[:, d, :]), "arq%d" % d, d, ["qd_4"])
    for t in range(ROUNDS):
        if t == ROUNDS - 1:
            for k in range(4):
                act(("cf%d" % k, T.cf[:, 512 * k:512 * k + 512]), ("cw", T.cw[:, 512 * k:512 * k + 512]), ID, 0.0, col(15), extra=["pf15"])
        for u in halves:
            stage_a(t, u)
        winners()
        if t < ROUNDS - 1:
            count(t)
        for u in halves:
            stage_b(t, u)
        for u in halves:
            scatter(t, u)
        if t < ROUNDS - 1:
            for u in halves:
                first_fail(t + 1, u)
    add("s", [lambda: g.scalar.dma_start(T.yc[0:64, :], T.cf[0:64, 0:2048])], ["cf"], [], 0.1, "stc0", 16, 5.0)
    add("y", [lambda: g.sync.dma_start(T.yc[64:128, :], T.cf[64:128, 0:2048])], ["cf"], [], 0.1, "stc1", 16, 5.0)

    n, wake = len(ops), CFG["wake"]
    pre = [[(d, 0 if ops[d]["q"] == o["q"] == "t" else 1 if o["q"] is None else 2) for d in sorted(o["need"])] for o in ops]
    lines = {"v": [], "s": []}
    for t in range(-1, ROUNDS):
        for w in ORDER["first" if t < 0 else "round" if t < ROUNDS - 1 else "last"].split():
            k = tag[(t + (w[-1] == "+"), w.rstrip("+"))]
            lines[ops[k]["q"]].append(k)
    for line in lines.values():
        for a, b in zip(line, line[1:]):
            if a not in ops[b]["need"]:
                pre[b].append((a, 0))
    users = [[] for _ in range(n)]
    for k in range(n):
        for d, how in pre[k]:
            users[d].append((k, how))
    left = [len(e) for e in users]
    todo, way = [k for k in range(n) if not left[k]], [0.0] * n
    for k in todo:
        c, lat = ops[k]["cost"], ops[k]["lat"]
        way[k] = max([way[j] + (c, c + lat, c + lat + wake)[how] for j, how in users[k]] or [c + lat])
        for d, how in pre[k]:
            left[d] -= 1
            if not left[d]:
                todo.append(d)
    left, at, free = [len(e) for e in pre], [0.0] * n, {}
    pool, order, opened, banks = [k for k in range(n) if not left[k]], [], set(), {}
    while pool:
        cand = []
        for k in pool:
            o = ops[k]
            st = max(at[k], free.get(o["q"], 0.0))
            if o["st"] and o["bank"][0] in opened:
                continue
            for a in o["bank"]:
                st = max([st] + [tj for qq, (j, tj) in banks.get(a, {}).items() if qq != o["q"]])
            cand.append((st, k))
        st0, k0 = min(cand)
        best, bst, c0 = k0, st0, ops[k0]["cost"]
        for st, k in cand:
            if ops[k]["q"] == ops[k0]["q"] and way[k] > way[best] and st <= st0 + CFG["look"] * c0 + 1e-9 + CFG["gain"] * (way[k] - way[k0]) * (st < st0 + c0):
                best, bst = k, st
        pool.remove(best)
        o = ops[best]
        ends = (bst + o["cost"], bst + o["cost"] + o["lat"], bst + o["cost"] + o["lat"] + wake)
        if o["q"]:
            free[o["q"]] = ends[0]
        for a in o["bank"]:
            use = banks.setdefault(a, {})
            o["need"].update(j for qq, (j, tj) in use.items() if qq != o["q"])
            use[o["q"]] = (best, ends[2])
            if o["st"] and not o["sp"]:
                opened.add(a)
            if o["sp"]:
                opened.discard(a)
        order.append(best)
        for j, how in users[best]:
            at[j] = max(at[j], ends[how])
            left[j] -= 1
            if not left[j]:
                pool.append(j)

    total = {"qv": 0, "qs": 0, "qt": 0, "qg": 0}
    known = {q: {} for q in eng}
    for k in order:
        o = ops[k]
        q = o["q"]
        if q is None:
            continue
        want = {}
        for d in o["need"]:
            p = ops[d]
            if p["sem"] == "none" or (p["q"] == q and q == "t"):
                continue
            if p["val"] > want.get(p["sem"], (0, 0))[0]:
                want[p["sem"]] = (p["val"], d)
        for s in sorted(want):
            v, d = want[s]
            if known[q].get(s, 0) < v and not any(ops[e].get("saw", {}).get(s, 0) >= v for s2, (v2, e) in want.items() if s2 != s):
                eng[q].wait_ge(T.sem[s], v)
        for s, (v, d) in want.items():
            for s2, v2 in list(ops[d].get("saw", {}).items()) + [(s, v)]:
                known[q][s2] = max(known[q].get(s2, 0), v2)
        o["saw"] = dict(known[q])
        fresh = o["sem"] is None
        for f in o["f"]:
            ins = f()
            if fresh:
                o["sem"] = "q" + q
                total["q" + q] += 1
                o["val"] = total["q" + q]
                ins.then_inc(T.sem["q" + q], 1)
            elif o["sem"] != "none":
                ins.then_inc(T.sem[o["sem"]], 16)
    for s in sorted(total):
        g.wait_ge(T.sem[s], total[s])
    for s in DMAS:
        g.wait_ge(T.sem[s], 16)
    g.wait_ge(T.sem.sent, (8 * (ROUNDS - 1) + n_ranks - 1) * NENG)
